import numpy as np
import ml_dtypes


def mxq(x, axis, fmt="e4m3"):
    dtype, down = {"e4m3": (ml_dtypes.float8_e4m3fn, 7), "e5m2": (ml_dtypes.float8_e5m2, 14)}[fmt]
    v = np.moveaxis(np.asarray(x, np.float32).astype(ml_dtypes.bfloat16).astype(np.float64), axis, -1)
    blocks = v.reshape(v.shape[:-1] + (-1, 32))
    amax = np.abs(blocks).max(-1, keepdims=True)
    byte = np.maximum(np.where(amax > 0, np.frexp(amax)[1] - 1 + 127, 0) - down, 1)
    scale = np.exp2(byte - 127.0)
    codes = (blocks / scale).astype(np.float32).astype(dtype).astype(np.float64)
    return np.moveaxis((codes * scale).reshape(v.shape), -1, axis)


WIDE = False


def mx_kscale(k):
    if not WIDE:
        return np.ones(k)
    levels = np.array([10, -10, 5, -5, 0])
    if k % 512:
        return np.exp2(np.random.permutation(np.resize(levels, k // 32))).repeat(32)
    a = np.empty((k // 512, 16))
    for p in range(k // 512):
        a[p, :8] = np.random.permutation(np.resize(levels, 8))
        for g in range(8):
            far = levels[np.abs(levels - a[p, g]) >= 10]
            a[p, g + 8] = far[np.random.randint(len(far))]
    return np.exp2(a.ravel()).repeat(32)


def f64(x):
    return np.asarray(x).astype(np.float64)


def striped(idx):
    return np.tile(idx.reshape(-1, 16).T, (8, 1)).astype(np.uint16)


def unstriped(offs):
    return offs[:16].T.reshape(-1).astype(np.int64)


E2M1 = np.array([0.0, 0.5, 1.0, 1.5, 2.0, 3.0, 4.0, 6.0, -0.0, -0.5, -1.0, -1.5, -2.0, -3.0, -4.0, -6.0])


def pack_weight(w, fmt):
    k, n = w.shape
    w = f64(np.asarray(w, np.float32).astype(ml_dtypes.bfloat16)).reshape(k // 32, 32, n)
    amax = np.abs(w).max(1)
    if fmt == "e4m3":
        byte = np.frexp(amax)[1] - 1 + 127 - 7
    else:
        mant, ex = np.frexp(amax / 6.0)
        byte = np.where(mant > 0.5, ex, ex - 1) + 127
    byte = np.clip(np.where(amax > 0, byte, 1), 1, 254)
    scaled = (w * np.exp2(127.0 - byte)[:, None, :]).reshape(k, n).astype(np.float32)
    by_word = np.ascontiguousarray(scaled.reshape(k // 512, 128, 4, n).transpose(0, 1, 3, 2))
    if fmt == "e4m3":
        words = by_word.astype(ml_dtypes.float8_e4m3fn).view(np.uint8)
    else:
        c = by_word.astype(ml_dtypes.float4_e2m1fn).view(np.uint8) & 0xF
        words = (c[..., 0::2] | (c[..., 1::2] << 4)).reshape(k // 512, 128, 2 * n)
    return np.ascontiguousarray(words), np.ascontiguousarray(byte.astype(np.uint8).reshape(k // 512, 16, n))


def unpack_weight(words, scales, fmt):
    g, _, n = scales.shape
    words = np.ascontiguousarray(words).reshape(g, 128, n, -1)
    if fmt == "e4m3":
        vals = words.view(ml_dtypes.float8_e4m3fn).astype(np.float64)
    else:
        nib = np.empty((g, 128, n, 4), np.uint8)
        nib[..., 0::2] = words & 0xF
        nib[..., 1::2] = words >> 4
        vals = E2M1[nib]
    vals = vals * np.repeat(np.exp2(scales.astype(np.float64) - 127.0), 8, axis=1)[..., None]
    return vals.transpose(0, 1, 3, 2).reshape(g * 512, n)


def d_relu(v):
    return (v > 0).astype(np.float64)


K, T, G, C1, E, C2, H = 256, 1024, 2, 512, 4, 256, 512
N = 512


def by_expert(wq, xq, E, C):
    return np.concatenate([wq[e].T @ xq[:, e * C:(e + 1) * C] for e in range(E)], axis=1)


def setup_inputs():
    n = np.random.standard_normal
    v = mx_kscale(N)
    u = mx_kscale(H)
    slots1 = np.random.permutation(T)
    slots2 = np.concatenate([q * C1 + np.random.permutation(C1) for q in range(G)])
    dy = pack_weight(n((N, T)) * v[:, None], "e4m3")
    wet = [pack_weight(m, "e2m1") for m in n((E, N, H)) / np.sqrt(N) / v[None, :, None] * u]
    wgt = [pack_weight(m, "e4m3") for m in n((G, H, K)) / np.sqrt(H) / u[None, :, None]]
    return {
        "dy_words": dy[0],
        "dy_scales": dy[1],
        "wet_words": np.stack([m[0] for m in wet]),
        "wet_scales": np.stack([m[1] for m in wet]),
        "wgt_words": np.stack([m[0] for m in wgt]),
        "wgt_scales": np.stack([m[1] for m in wgt]),
        "a": (n((H, T))).astype(np.float32),
        "gate": (np.tile(np.random.uniform(0.2, 1.0, T), (128, 1))).astype(np.float32),
        "offs": striped(slots1),
        "offs2": striped(slots2),
        "dst": striped(slots1[slots2]),
    }


def reference(dy_words, dy_scales, wet_words, wet_scales, wgt_words, wgt_scales, a, gate, offs, offs2, dst):
    wet = np.stack([unpack_weight(wet_words[e], wet_scales[e], "e2m1") for e in range(E)])
    wgt = np.stack([unpack_weight(wgt_words[e], wgt_scales[e], "e4m3") for e in range(G)])
    gq = unpack_weight(dy_words, dy_scales, "e4m3")[:, unstriped(dst)]
    z = f64(gate[:1]) * by_expert(wet, gq, E, C2)
    da = np.zeros((H, T))
    da[:, unstriped(offs2)] = z
    dx = by_expert(wgt, mxq(da * d_relu(f64(a)), 0, "e4m3"), G, C1)
    out = np.zeros((K, T))
    out[:, unstriped(offs)] = dx
    return out

@@ -1,0 +1,177 @@
+from contextlib import ExitStack
+
+import concourse.mybir as mybir
+from concourse.masks import make_identity
+
+K, T, G, C1, E, C2, H, N = 256, 1024, 2, 512, 4, 256, 512, 512
+FLOPS = 2 * T * N * H + 2 * T * H * K
+
+F32 = mybir.dt.float32
+BF16 = mybir.dt.bfloat16
+I32 = mybir.dt.int32
+U32 = mybir.dt.uint32
+U16 = mybir.dt.uint16
+U8 = mybir.dt.uint8
+FP8X4 = mybir.dt.float8_e4m3fn_x4
+FP4X4 = mybir.dt.float4_e2m1fn_x4
+ACT = mybir.ActivationFunctionType
+MULT = mybir.AluOpType.mult
+
+P = 128
+PACK = 4
+PER_COL = 16
+BLOCKS = T // P
+HALF = C1 // 2
+
+
+def entries(list_tile, first, count):
+    return list_tile[:, first // PER_COL : (first + count) // PER_COL]
+
+
+def tile_moe_hib_relu_kernel(
+    tc, dy_words, dy_scales, wet_words, wet_scales, wgt_words, wgt_scales, a, gate, offs, offs2, dst, out
+):
+    nc = tc.nc
+    with ExitStack() as ctx:
+        keep = ctx.enter_context(tc.tile_pool(name="keep", bufs=1))
+        reuse = ctx.enter_context(tc.tile_pool(name="reuse", bufs=1))
+        ring = ctx.enter_context(tc.tile_pool(name="ring", bufs=3))
+        psum_z = ctx.enter_context(tc.psum_pool(name="psum_z", bufs=3))
+        psum_t = ctx.enter_context(tc.psum_pool(name="psum_t", bufs=3))
+        psum_x = ctx.enter_context(tc.psum_pool(name="psum_x", bufs=2))
+
+        dst_sb = keep.tile([P, T // PER_COL], U16, name="dst_sb")
+        offs2_sb = keep.tile([P, T // PER_COL], U16, name="offs2_sb")
+        offs_sb = keep.tile([P, T // PER_COL], U16, name="offs_sb")
+        dy_w = keep.tile([P, T], I32, name="dy_w", align_bytes=64)
+        dy_s = keep.tile([P, T], U8, name="dy_s", align_bytes=64)
+        g_w = keep.tile([P, T], U32, name="g_w", align_bytes=64)
+        g_s = keep.tile([P, T], U8, name="g_s", align_bytes=64)
+        wet_w = keep.tile([P, E, 2 * H], U8, name="wet_w", align_bytes=64)
+        wet_s = keep.tile([P, E, H], U8, name="wet_s", align_bytes=64)
+        wgt_w = keep.tile([P, G, K], I32, name="wgt_w", align_bytes=64)
+        wgt_s = keep.tile([P, G, K], U8, name="wgt_s", align_bytes=64)
+        gate_rows = keep.tile([P, P], F32, name="gate_rows")
+        gate_cols = keep.tile([P, BLOCKS], F32, name="gate_cols")
+        ident = keep.tile([P, P], F32, name="ident")
+        z_slots = keep.tile([P, PACK, T], F32, name="z_slots")
+        a_sb = [keep.tile([P, PACK, C1], F32, name="a_sb%d" % f) for f in range(G)]
+
+        nc.gpsimd.memset(dy_s[:].bitcast(I32), 0)
+        nc.gpsimd.dma_start(gate_rows[:], gate.rearrange("r (b c) -> (r b) c", c=P)[0:P, :])
+        nc.vector.memset(wet_s[:].rearrange("p e h -> p (e h)").bitcast(I32), 0)
+        nc.vector.memset(wgt_s[:].rearrange("p f k -> p (f k)").bitcast(I32), 0)
+        make_identity(nc, ident[:])
+
+        nc.sync.dma_start(dst_sb[:], dst)
+        for q in range(4):
+            nc.sync.dma_start(dy_s[32 * q : 32 * q + 4, :].bitcast(I32), dy_scales[0, 4 * q : 4 * q + 4, :].bitcast(I32))
+        nc.sync.dma_start(dy_w[:], dy_words[0].rearrange("p n d -> p (n d)").bitcast(I32))
+        wet_src = wet_words.rearrange("e s p c -> p (e s) c").bitcast(I32)
+        nc.sync.dma_start(wet_w[:, 0:2, :].bitcast(I32), wet_src[:, 0:2, :])
+        wet_s_src = wet_scales.rearrange("e s r h -> r (e s) h").bitcast(I32)
+        for q in range(4):
+            nc.sync.dma_start(wet_s[32 * q : 32 * q + 4, :, :].bitcast(I32), wet_s_src[4 * q : 4 * q + 4, :, :])
+        nc.sync.dma_start(offs2_sb[:], offs2)
+        nc.sync.dma_start(wet_w[:, 2:4, :].bitcast(I32), wet_src[:, 2:4, :])
+        a_src = a.rearrange("(p t) j -> p t j", t=PACK)
+        for f in range(G):
+            nc.sync.dma_start(a_sb[f][:], a_src[:, :, f * C1 : (f + 1) * C1])
+        nc.sync.dma_start(wgt_w[:], wgt_words.rearrange("f s p k d -> p (f s) (k d)").bitcast(I32))
+        wgt_s_src = wgt_scales.rearrange("f s r k -> r (f s) k").bitcast(I32)
+        for q in range(4):
+            nc.sync.dma_start(wgt_s[32 * q : 32 * q + 4, :, :].bitcast(I32), wgt_s_src[4 * q : 4 * q + 4, :, :])
+        nc.sync.dma_start(offs_sb[:], offs)
+
+        gate_t = psum_t.tile([P, PACK, P], F32, name="turned")
+        nc.tensor.transpose(gate_t[:, 0, :], gate_rows[:], ident[:])
+        nc.scalar.copy(gate_cols[:], gate_t[:, 0, 0:BLOCKS])
+
+        def gather_scales(first, count):
+            nc.vector.tensor_copy(g_s[:, first : first + count], dy_s[:].indirect(entries(dst_sb, first, count)))
+
+        def gather_words(first, count):
+            nc.vector.tensor_copy(
+                g_w[:, first : first + count], dy_w[:].bitcast(U32).indirect(entries(dst_sb, first, count))
+            )
+
+        gather_scales(0, 512)
+        gather_words(0, 128)
+        gather_words(128, 128)
+        gather_words(256, 256)
+        gather_scales(512, 512)
+        gather_words(512, 512)
+
+        for b in range(BLOCKS):
+            e = b * P // C2
+            cols = slice(b * P, (b + 1) * P)
+            sums = psum_z.tile([P, H], F32, name="sums")
+            nc.tensor.matmul_mx(
+                out=sums[:],
+                lhsT=g_w[:, cols].bitcast(FP8X4),
+                lhsT_scale=g_s[:, cols],
+                rhs=wet_w[:, e, :].bitcast(FP4X4),
+                rhs_scale=wet_s[:, e, :],
+                start=True,
+                stop=True,
+            )
+            z_t = ring.tile([P, PACK, P], F32, name="z_t")
+            nc.scalar.activation(
+                z_t[:], sums[:].rearrange("m (p t) -> m t p", t=PACK), ACT.Copy, scale=gate_cols[:, b : b + 1]
+            )
+            turned = psum_t.tile([P, PACK, P], F32, name="turned")
+            for t in range(PACK):
+                nc.tensor.transpose(turned[:, t, :], z_t[:, t, :], ident[:])
+            nc.scalar.copy(z_slots[:, :, cols], turned[:])
+
+        dx = {}
+        for f in range(G):
+            mask = keep.tile([P, PACK, C1], BF16, name="mask%d" % f)
+            sign = keep.tile([P, PACK, C1], BF16, name="sign%d" % f)
+            for t in range(PACK):
+                nc.scalar.activation(sign[:, t, :], a_sb[f][:, t, :], ACT.Sign)
+                nc.scalar.activation(mask[:, t, :], sign[:, t, :], ACT.Relu)
+            z_win = []
+            for t in range(PACK):
+                if (f, t) == (1, 2):
+                    z_win.append(reuse.tile([P, T], F32, name="z_win1_2", tag="da0", align_bytes=64))
+                else:
+                    z_win.append(keep.tile([P, T], F32, name="z_win%d_%d" % (f, t)))
+            cuts = [(0, 128), (128, 128), (256, 256)] if f == 0 else [(512, 512)]
+            for first, count in cuts:
+                for t in range(PACK):
+                    nc.vector.tensor_copy(
+                        z_win[t][:].indirect(entries(offs2_sb, first, count)), z_slots[:, t, first : first + count]
+                    )
+            da = reuse.tile([P, C1, PACK], BF16, name="da%d" % f, tag="da%d" % f, align_bytes=64)
+            da_w = keep.tile([P, C1], U32, name="da_w%d" % f, align_bytes=64)
+            da_s = keep.tile([P, C1], U8, name="da_s%d" % f, align_bytes=64)
+            for t in range(PACK):
+                nc.gpsimd.tensor_tensor(da[:, :, t], z_win[t][:, f * C1 : (f + 1) * C1], mask[:, t, :], MULT)
+            nc.vector.quantize_mx(
+                out=da_w[:].bitcast(FP8X4), scales=da_s[:], in_=da[:].rearrange("p j t -> p (j t)")
+            )
+            for kb in range(K // P):
+                k_cols = slice(kb * P, (kb + 1) * P)
+                acc = psum_x.tile([P, C1], F32, name="acc")
+                nc.tensor.matmul_mx(
+                    out=acc[:],
+                    lhsT=wgt_w[:, f, k_cols].bitcast(FP8X4),
+                    lhsT_scale=wgt_s[:, f, k_cols],
+                    rhs=da_w[:].bitcast(FP8X4),
+                    rhs_scale=da_s[:],
+                    start=True,
+                    stop=True,
+                )
+                dx[f, kb] = keep.tile([P, C1], F32, name="dx%d_%d" % (f, kb))
+                nc.scalar.copy(dx[f, kb][:], acc[:])
+
+        out_sb = [
+            keep.tile([P, T], F32, name="out_sb0"),
+            reuse.tile([P, T], F32, name="out_sb1", tag="da1", align_bytes=64),
+        ]
+        for f in range(G):
+            for kb in range(K // P):
+                nc.vector.tensor_copy(out_sb[kb][:].indirect(entries(offs_sb, f * C1, C1)), dx[f, kb][:])
+        for kb in range(K // P):
+            nc.sync.dma_start(out[kb * P : (kb + 1) * P, :], out_sb[kb][:])

@@ -36,7 +36,7 @@ def tile_moe_hib_relu_kernel(
         keep = ctx.enter_context(tc.tile_pool(name="keep", bufs=1))
         reuse = ctx.enter_context(tc.tile_pool(name="reuse", bufs=1))
         ring = ctx.enter_context(tc.tile_pool(name="ring", bufs=3))
-        psum_z = ctx.enter_context(tc.psum_pool(name="psum_z", bufs=3))
+        psum_z = ctx.enter_context(tc.psum_pool(name="psum_z", bufs=1))
         psum_t = ctx.enter_context(tc.psum_pool(name="psum_t", bufs=3))
         psum_x = ctx.enter_context(tc.psum_pool(name="psum_x", bufs=2))
 
@@ -54,14 +54,27 @@ def tile_moe_hib_relu_kernel(
         gate_rows = keep.tile([P, P], F32, name="gate_rows")
         gate_cols = keep.tile([P, BLOCKS], F32, name="gate_cols")
         ident = keep.tile([P, P], F32, name="ident")
-        z_slots = keep.tile([P, PACK, T], F32, name="z_slots")
+        z_first = keep.tile([P, PACK, C1], F32, name="z_first")
+        z_second = [
+            reuse.tile([P, 1, C1], F32, name="z_second0", tag="codes0", align_bytes=64),
+            reuse.tile([P, 2, C1], F32, name="z_second12", tag="out0"),
+            keep.tile([P, 1, C1], F32, name="z_second3"),
+        ]
+        spans = [(0, 1), (1, 3), (3, 4)]
+
+        def z_slots(t, first, count):
+            if first < C1:
+                return z_first[:, t, first : first + count]
+            for tile, (lo, hi) in zip(z_second, spans):
+                if lo <= t < hi:
+                    return tile[:, t - lo, first - C1 : first - C1 + count]
+
         a_sb = [keep.tile([P, PACK, C1], F32, name="a_sb%d" % f) for f in range(G)]
 
         nc.gpsimd.memset(dy_s[:].bitcast(I32), 0)
-        nc.gpsimd.dma_start(gate_rows[:], gate.rearrange("r (b c) -> (r b) c", c=P)[0:P, :])
-        nc.vector.memset(wet_s[:].rearrange("p e h -> p (e h)").bitcast(I32), 0)
-        nc.vector.memset(wgt_s[:].rearrange("p f k -> p (f k)").bitcast(I32), 0)
+        nc.gpsimd.memset(wet_s[:].rearrange("p e h -> p (e h)").bitcast(I32), 0)
         make_identity(nc, ident[:])
+        nc.gpsimd.memset(wgt_s[:].rearrange("p f k -> p (f k)").bitcast(I32), 0)
 
         nc.sync.dma_start(dst_sb[:], dst)
         for q in range(4):
@@ -69,6 +82,7 @@ def tile_moe_hib_relu_kernel(
         nc.sync.dma_start(dy_w[:], dy_words[0].rearrange("p n d -> p (n d)").bitcast(I32))
         wet_src = wet_words.rearrange("e s p c -> p (e s) c").bitcast(I32)
         nc.sync.dma_start(wet_w[:, 0:2, :].bitcast(I32), wet_src[:, 0:2, :])
+        nc.sync.dma_start(gate_rows[:], gate.rearrange("r (b c) -> (r b) c", c=P)[0:P, :])
         wet_s_src = wet_scales.rearrange("e s r h -> r (e s) h").bitcast(I32)
         for q in range(4):
             nc.sync.dma_start(wet_s[32 * q : 32 * q + 4, :, :].bitcast(I32), wet_s_src[4 * q : 4 * q + 4, :, :])
@@ -105,7 +119,7 @@ def tile_moe_hib_relu_kernel(
         for b in range(BLOCKS):
             e = b * P // C2
             cols = slice(b * P, (b + 1) * P)
-            sums = psum_z.tile([P, H], F32, name="sums")
+            sums = psum_z.tile([P, H], F32, name="sums", tag="even" if b > 0 and b % 2 == 0 else "odd")
             nc.tensor.matmul_mx(
                 out=sums[:],
                 lhsT=g_w[:, cols].bitcast(FP8X4),
@@ -115,42 +129,51 @@ def tile_moe_hib_relu_kernel(
                 start=True,
                 stop=True,
             )
-            z_t = ring.tile([P, PACK, P], F32, name="z_t")
-            nc.scalar.activation(
-                z_t[:], sums[:].rearrange("m (p t) -> m t p", t=PACK), ACT.Copy, scale=gate_cols[:, b : b + 1]
-            )
-            turned = psum_t.tile([P, PACK, P], F32, name="turned")
-            for t in range(PACK):
-                nc.tensor.transpose(turned[:, t, :], z_t[:, t, :], ident[:])
-            nc.scalar.copy(z_slots[:, :, cols], turned[:])
+            if b == 1:
+                z_t = reuse.tile([P, PACK, P], F32, name="z_t1", tag="sign")
+            else:
+                z_t = ring.tile([P, PACK, P], F32, name="z_t")
+            by_plane = sums[:].rearrange("m (p t) -> m t p", t=PACK)
+            parts = [(0, 1), (1, PACK)] if b == 0 else [(0, PACK)]
+            for lo, hi in parts:
+                nc.scalar.activation(z_t[:, lo:hi, :], by_plane[:, lo:hi, :], ACT.Copy, scale=gate_cols[:, b : b + 1])
+            for lo, hi in parts:
+                if lo == 1:
+                    turned = psum_z.tile([P, PACK, P], F32, name="turned_rest", tag="even")
+                else:
+                    turned = psum_t.tile([P, PACK, P], F32, name="turned")
+                for t in range(lo, hi):
+                    nc.tensor.transpose(turned[:, t, :], z_t[:, t, :], ident[:])
+                if b * P < C1:
+                    nc.scalar.copy(z_first[:, lo:hi, cols], turned[:, lo:hi, :])
+                else:
+                    for tile, (lo2, hi2) in zip(z_second, spans):
+                        nc.scalar.copy(tile[:, :, b * P - C1 : (b + 1) * P - C1], turned[:, lo2:hi2, :])
 
-        dx = {}
+        relu_on = []
         for f in range(G):
             mask = keep.tile([P, PACK, C1], BF16, name="mask%d" % f)
-            sign = keep.tile([P, PACK, C1], BF16, name="sign%d" % f)
+            relu_on.append(mask)
+            sign = reuse.tile([P, PACK, C1], BF16, name="sign%d" % f, tag="sign")
             for t in range(PACK):
                 nc.scalar.activation(sign[:, t, :], a_sb[f][:, t, :], ACT.Sign)
                 nc.scalar.activation(mask[:, t, :], sign[:, t, :], ACT.Relu)
-            z_win = []
-            for t in range(PACK):
-                if (f, t) == (1, 2):
-                    z_win.append(reuse.tile([P, T], F32, name="z_win1_2", tag="da0", align_bytes=64))
-                else:
-                    z_win.append(keep.tile([P, T], F32, name="z_win%d_%d" % (f, t)))
-            cuts = [(0, 128), (128, 128), (256, 256)] if f == 0 else [(512, 512)]
-            for first, count in cuts:
-                for t in range(PACK):
-                    nc.vector.tensor_copy(
-                        z_win[t][:].indirect(entries(offs2_sb, first, count)), z_slots[:, t, first : first + count]
-                    )
-            da = reuse.tile([P, C1, PACK], BF16, name="da%d" % f, tag="da%d" % f, align_bytes=64)
-            da_w = keep.tile([P, C1], U32, name="da_w%d" % f, align_bytes=64)
+
+        def window(f, t):
+            tag = "last_plane" if t == PACK - 1 else "z_win%d_%d" % (f, t)
+            return reuse.tile([P, T], F32, name="z_win%d_%d" % (f, t), tag=tag)
+
+        def scatter_z(win, t, first, count):
+            nc.vector.tensor_copy(win[:].indirect(entries(offs2_sb, first, count)), z_slots(t, first, count))
+
+        def mask_plane(da, f, t, win):
+            nc.gpsimd.tensor_tensor(da[:, :, t], win[:, f * C1 : (f + 1) * C1], relu_on[f][:, t, :], MULT)
+
+        def second_product(f, da):
+            da_w = reuse.tile([P, C1], U32, name="da_w%d" % f, tag="codes%d" % f, align_bytes=64)
             da_s = keep.tile([P, C1], U8, name="da_s%d" % f, align_bytes=64)
-            for t in range(PACK):
-                nc.gpsimd.tensor_tensor(da[:, :, t], z_win[t][:, f * C1 : (f + 1) * C1], mask[:, t, :], MULT)
-            nc.vector.quantize_mx(
-                out=da_w[:].bitcast(FP8X4), scales=da_s[:], in_=da[:].rearrange("p j t -> p (j t)")
-            )
+            nc.vector.quantize_mx(out=da_w[:].bitcast(FP8X4), scales=da_s[:], in_=da[:].rearrange("p j t -> p (j t)"))
+            dx = []
             for kb in range(K // P):
                 k_cols = slice(kb * P, (kb + 1) * P)
                 acc = psum_x.tile([P, C1], F32, name="acc")
@@ -163,15 +186,35 @@ def tile_moe_hib_relu_kernel(
                     start=True,
                     stop=True,
                 )
-                dx[f, kb] = keep.tile([P, C1], F32, name="dx%d_%d" % (f, kb))
-                nc.scalar.copy(dx[f, kb][:], acc[:])
+                dx_sb = keep.tile([P, C1], F32, name="dx%d_%d" % (f, kb))
+                nc.scalar.copy(dx_sb[:], acc[:])
+                dx.append(dx_sb)
+            return dx
 
-        out_sb = [
-            keep.tile([P, T], F32, name="out_sb0"),
-            reuse.tile([P, T], F32, name="out_sb1", tag="da1", align_bytes=64),
-        ]
-        for f in range(G):
-            for kb in range(K // P):
-                nc.vector.tensor_copy(out_sb[kb][:].indirect(entries(offs_sb, f * C1, C1)), dx[f, kb][:])
-        for kb in range(K // P):
-            nc.sync.dma_start(out[kb * P : (kb + 1) * P, :], out_sb[kb][:])
+        def scatter_dx(out_tile, f, dx_sb):
+            nc.vector.tensor_copy(out_tile[:].indirect(entries(offs_sb, f * C1, C1)), dx_sb[:])
+
+        da = [keep.tile([P, C1, PACK], BF16, name="da%d" % f, align_bytes=64) for f in range(G)]
+        wins = [window(0, t) for t in range(PACK)]
+        for first, count in [(0, 128), (128, 128), (256, 256)]:
+            for t in range(PACK):
+                scatter_z(wins[t], t, first, count)
+        for t in range(PACK):
+            mask_plane(da[0], 0, t, wins[t])
+
+        for t in range(PACK):
+            win = window(1, t)
+            scatter_z(win, t, C1, C1)
+            mask_plane(da[1], 1, t, win)
+            if t == 1:
+                dx_first = second_product(0, da[0])
+
+        out_low = reuse.tile([P, T], F32, name="out_low", tag="out0")
+        scatter_dx(out_low, 0, dx_first[0])
+        dx_second = second_product(1, da[1])
+        out_high = reuse.tile([P, T], F32, name="out_high", tag="last_plane")
+        scatter_dx(out_high, 0, dx_first[1])
+        scatter_dx(out_low, 1, dx_second[0])
+        nc.sync.dma_start(out[0:P, :], out_low[:])
+        scatter_dx(out_high, 1, dx_second[1])
+        nc.sync.dma_start(out[P : 2 * P, :], out_high[:])

@@ -81,13 +81,13 @@ def tile_moe_hib_relu_kernel(
             nc.sync.dma_start(dy_s[32 * q : 32 * q + 4, :].bitcast(I32), dy_scales[0, 4 * q : 4 * q + 4, :].bitcast(I32))
         nc.sync.dma_start(dy_w[:], dy_words[0].rearrange("p n d -> p (n d)").bitcast(I32))
         wet_src = wet_words.rearrange("e s p c -> p (e s) c").bitcast(I32)
-        nc.sync.dma_start(wet_w[:, 0:2, :].bitcast(I32), wet_src[:, 0:2, :])
+        nc.sync.dma_start(wet_w[:, 0:1, :].bitcast(I32), wet_src[:, 0:1, :])
         nc.sync.dma_start(gate_rows[:], gate.rearrange("r (b c) -> (r b) c", c=P)[0:P, :])
         wet_s_src = wet_scales.rearrange("e s r h -> r (e s) h").bitcast(I32)
         for q in range(4):
             nc.sync.dma_start(wet_s[32 * q : 32 * q + 4, :, :].bitcast(I32), wet_s_src[4 * q : 4 * q + 4, :, :])
         nc.sync.dma_start(offs2_sb[:], offs2)
-        nc.sync.dma_start(wet_w[:, 2:4, :].bitcast(I32), wet_src[:, 2:4, :])
+        nc.sync.dma_start(wet_w[:, 1:4, :].bitcast(I32), wet_src[:, 1:4, :])
         a_src = a.rearrange("(p t) j -> p t j", t=PACK)
         for f in range(G):
             nc.sync.dma_start(a_sb[f][:], a_src[:, :, f * C1 : (f + 1) * C1])
@@ -134,11 +134,11 @@ def tile_moe_hib_relu_kernel(
             else:
                 z_t = ring.tile([P, PACK, P], F32, name="z_t")
             by_plane = sums[:].rearrange("m (p t) -> m t p", t=PACK)
-            parts = [(0, 1), (1, PACK)] if b == 0 else [(0, PACK)]
+            parts = [(0, 1), (1, 2), (2, PACK)] if b == 0 else [(0, PACK)]
             for lo, hi in parts:
                 nc.scalar.activation(z_t[:, lo:hi, :], by_plane[:, lo:hi, :], ACT.Copy, scale=gate_cols[:, b : b + 1])
             for lo, hi in parts:
-                if lo == 1:
+                if lo == 2:
                     turned = psum_z.tile([P, PACK, P], F32, name="turned_rest", tag="even")
                 else:
                     turned = psum_t.tile([P, PACK, P], F32, name="turned")
@@ -217,4 +217,5 @@ def tile_moe_hib_relu_kernel(
         scatter_dx(out_low, 1, dx_second[0])
         nc.sync.dma_start(out[0:P, :], out_low[:])
         scatter_dx(out_high, 1, dx_second[1])
-        nc.sync.dma_start(out[P : 2 * P, :], out_high[:])
+        nc.sync.dma_start(out[P : 2 * P, 0 : T // 2], out_high[:, 0 : T // 2])
+        nc.scalar.dma_start(out[P : 2 * P, T // 2 : T], out_high[:, T // 2 : T])

@@ -15,7 +15,7 @@ U8 = mybir.dt.uint8
 FP8X4 = mybir.dt.float8_e4m3fn_x4
 FP4X4 = mybir.dt.float4_e2m1fn_x4
 ACT = mybir.ActivationFunctionType
-MULT = mybir.AluOpType.mult
+ALU = mybir.AluOpType
 
 P = 128
 PACK = 4
@@ -56,11 +56,11 @@ def tile_moe_hib_relu_kernel(
         ident = keep.tile([P, P], F32, name="ident")
         z_first = keep.tile([P, PACK, C1], F32, name="z_first")
         z_second = [
-            reuse.tile([P, 1, C1], F32, name="z_second0", tag="codes0", align_bytes=64),
-            reuse.tile([P, 2, C1], F32, name="z_second12", tag="out0"),
+            reuse.tile([P, 2, C1], F32, name="z_second01", tag="codes0", align_bytes=64),
+            reuse.tile([P, 1, C1], F32, name="z_second2", tag="last_plane"),
             keep.tile([P, 1, C1], F32, name="z_second3"),
         ]
-        spans = [(0, 1), (1, 3), (3, 4)]
+        spans = [(0, 2), (2, 3), (3, 4)]
 
         def z_slots(t, first, count):
             if first < C1:
@@ -72,6 +72,7 @@ def tile_moe_hib_relu_kernel(
         a_sb = [keep.tile([P, PACK, C1], F32, name="a_sb%d" % f) for f in range(G)]
 
         nc.gpsimd.memset(dy_s[:].bitcast(I32), 0)
+        nc.gpsimd.memset(gate_rows[:], 0.0)
         nc.gpsimd.memset(wet_s[:].rearrange("p e h -> p (e h)").bitcast(I32), 0)
         make_identity(nc, ident[:])
         nc.gpsimd.memset(wgt_s[:].rearrange("p f k -> p (f k)").bitcast(I32), 0)
@@ -82,7 +83,7 @@ def tile_moe_hib_relu_kernel(
         nc.sync.dma_start(dy_w[:], dy_words[0].rearrange("p n d -> p (n d)").bitcast(I32))
         wet_src = wet_words.rearrange("e s p c -> p (e s) c").bitcast(I32)
         nc.sync.dma_start(wet_w[:, 0:1, :].bitcast(I32), wet_src[:, 0:1, :])
-        nc.sync.dma_start(gate_rows[:], gate.rearrange("r (b c) -> (r b) c", c=P)[0:P, :])
+        nc.sync.dma_start(gate_rows[0:BLOCKS, :], gate[0].rearrange("(b c) -> b c", c=P))
         wet_s_src = wet_scales.rearrange("e s r h -> r (e s) h").bitcast(I32)
         for q in range(4):
             nc.sync.dma_start(wet_s[32 * q : 32 * q + 4, :, :].bitcast(I32), wet_s_src[4 * q : 4 * q + 4, :, :])
@@ -116,7 +117,7 @@ def tile_moe_hib_relu_kernel(
         gather_scales(512, 512)
         gather_words(512, 512)
 
-        for b in range(BLOCKS):
+        def first_product(b):
             e = b * P // C2
             cols = slice(b * P, (b + 1) * P)
             sums = psum_z.tile([P, H], F32, name="sums", tag="even" if b > 0 and b % 2 == 0 else "odd")
@@ -129,8 +130,8 @@ def tile_moe_hib_relu_kernel(
                 start=True,
                 stop=True,
             )
-            if b == 1:
-                z_t = reuse.tile([P, PACK, P], F32, name="z_t1", tag="sign")
+            if (b + 1) * P % C1 == 0:
+                z_t = reuse.tile([P, PACK, P], F32, name="z_t_last", tag="sign")
             else:
                 z_t = ring.tile([P, PACK, P], F32, name="z_t")
             by_plane = sums[:].rearrange("m (p t) -> m t p", t=PACK)
@@ -150,24 +151,32 @@ def tile_moe_hib_relu_kernel(
                     for tile, (lo2, hi2) in zip(z_second, spans):
                         nc.scalar.copy(tile[:, :, b * P - C1 : (b + 1) * P - C1], turned[:, lo2:hi2, :])
 
-        relu_on = []
-        for f in range(G):
-            mask = keep.tile([P, PACK, C1], BF16, name="mask%d" % f)
-            relu_on.append(mask)
+        def relu_slope(f):
+            slope = keep.tile([P, PACK, C1], BF16, name="slope%d" % f)
             sign = reuse.tile([P, PACK, C1], BF16, name="sign%d" % f, tag="sign")
             for t in range(PACK):
                 nc.scalar.activation(sign[:, t, :], a_sb[f][:, t, :], ACT.Sign)
-                nc.scalar.activation(mask[:, t, :], sign[:, t, :], ACT.Relu)
+                if f == 0:
+                    nc.gpsimd.tensor_scalar(slope[:, t, :], sign[:, t, :], 1.0, 0.0, ALU.min, ALU.max)
+                else:
+                    nc.scalar.activation(slope[:, t, :], sign[:, t, :], ACT.Relu)
+            return slope
+
+        slopes = []
+        for f in range(G):
+            for b in range(f * C1 // P, (f + 1) * C1 // P):
+                first_product(b)
+            slopes.append(relu_slope(f))
 
         def window(f, t):
-            tag = "last_plane" if t == PACK - 1 else "z_win%d_%d" % (f, t)
+            tag = "last_plane" if (f, t) == (1, PACK - 1) else "z_win%d_%d" % (f, t)
             return reuse.tile([P, T], F32, name="z_win%d_%d" % (f, t), tag=tag)
 
         def scatter_z(win, t, first, count):
             nc.vector.tensor_copy(win[:].indirect(entries(offs2_sb, first, count)), z_slots(t, first, count))
 
         def mask_plane(da, f, t, win):
-            nc.gpsimd.tensor_tensor(da[:, :, t], win[:, f * C1 : (f + 1) * C1], relu_on[f][:, t, :], MULT)
+            nc.gpsimd.tensor_tensor(da[:, :, t], win[:, f * C1 : (f + 1) * C1], slopes[f][:, t, :], ALU.mult)
 
         def second_product(f, da):
             da_w = reuse.tile([P, C1], U32, name="da_w%d" % f, tag="codes%d" % f, align_bytes=64)
@@ -196,20 +205,27 @@ def tile_moe_hib_relu_kernel(
 
         da = [keep.tile([P, C1, PACK], BF16, name="da%d" % f, align_bytes=64) for f in range(G)]
         wins = [window(0, t) for t in range(PACK)]
-        for first, count in [(0, 128), (128, 128), (256, 256)]:
-            for t in range(PACK):
-                scatter_z(wins[t], t, first, count)
         for t in range(PACK):
-            mask_plane(da[0], 0, t, wins[t])
+            scatter_z(wins[t], t, 0, P)
+        for t, first, last in [(0, 1, 2), (1, 1, 3), (0, 2, 4), (1, 3, 4), (2, 1, 4), (3, 1, 4)]:
+            scatter_z(wins[t], t, first * P, (last - first) * P)
+            if last == 4:
+                mask_plane(da[0], 0, t, wins[t])
 
-        for t in range(PACK):
-            win = window(1, t)
-            scatter_z(win, t, C1, C1)
-            mask_plane(da[1], 1, t, win)
-            if t == 1:
-                dx_first = second_product(0, da[0])
+        wins = [window(1, t) for t in range(PACK - 1)]
+        for first in (C1, C1 + HALF):
+            for t in range(2):
+                scatter_z(wins[t], t, first, HALF)
+        for t in range(2):
+            mask_plane(da[1], 1, t, wins[t])
+        scatter_z(wins[2], 2, C1, C1)
+        mask_plane(da[1], 1, 2, wins[2])
+        dx_first = second_product(0, da[0])
+        last_win = window(1, PACK - 1)
+        scatter_z(last_win, PACK - 1, C1, C1)
+        mask_plane(da[1], 1, PACK - 1, last_win)
 
-        out_low = reuse.tile([P, T], F32, name="out_low", tag="out0")
+        out_low = keep.tile([P, T], F32, name="out_low")
         scatter_dx(out_low, 0, dx_first[0])
         dx_second = second_product(1, da[1])
         out_high = reuse.tile([P, T], F32, name="out_high", tag="last_plane")

@@ -46,12 +46,12 @@ def tile_moe_hib_relu_kernel(
         dy_w = keep.tile([P, T], I32, name="dy_w", align_bytes=64)
         dy_s = keep.tile([P, T], U8, name="dy_s", align_bytes=64)
         g_w = keep.tile([P, T], U32, name="g_w", align_bytes=64)
-        g_s = keep.tile([P, T], U8, name="g_s", align_bytes=64)
+        g_s = [keep.tile([P, C1], U8, name="g_s0", align_bytes=64)]
         wet_w = keep.tile([P, E, 2 * H], U8, name="wet_w", align_bytes=64)
         wet_s = keep.tile([P, E, H], U8, name="wet_s", align_bytes=64)
         wgt_w = keep.tile([P, G, K], I32, name="wgt_w", align_bytes=64)
         wgt_s = keep.tile([P, G, K], U8, name="wgt_s", align_bytes=64)
-        gate_rows = keep.tile([P, P], F32, name="gate_rows")
+        gate_rows = reuse.tile([P, P], F32, name="gate_rows", tag="gate", align_bytes=64)
         gate_cols = keep.tile([P, BLOCKS], F32, name="gate_cols")
         ident = keep.tile([P, P], F32, name="ident")
         z_first = keep.tile([P, PACK, C1], F32, name="z_first")
@@ -81,9 +81,9 @@ def tile_moe_hib_relu_kernel(
         for q in range(4):
             nc.sync.dma_start(dy_s[32 * q : 32 * q + 4, :].bitcast(I32), dy_scales[0, 4 * q : 4 * q + 4, :].bitcast(I32))
         nc.sync.dma_start(dy_w[:], dy_words[0].rearrange("p n d -> p (n d)").bitcast(I32))
+        nc.sync.dma_start(gate_rows[0:BLOCKS, :], gate[0].rearrange("(b c) -> b c", c=P))
         wet_src = wet_words.rearrange("e s p c -> p (e s) c").bitcast(I32)
         nc.sync.dma_start(wet_w[:, 0:1, :].bitcast(I32), wet_src[:, 0:1, :])
-        nc.sync.dma_start(gate_rows[0:BLOCKS, :], gate[0].rearrange("(b c) -> b c", c=P))
         wet_s_src = wet_scales.rearrange("e s r h -> r (e s) h").bitcast(I32)
         for q in range(4):
             nc.sync.dma_start(wet_s[32 * q : 32 * q + 4, :, :].bitcast(I32), wet_s_src[4 * q : 4 * q + 4, :, :])
@@ -103,7 +103,8 @@ def tile_moe_hib_relu_kernel(
         nc.scalar.copy(gate_cols[:], gate_t[:, 0, 0:BLOCKS])
 
         def gather_scales(first, count):
-            nc.vector.tensor_copy(g_s[:, first : first + count], dy_s[:].indirect(entries(dst_sb, first, count)))
+            at = first % C1
+            nc.vector.tensor_copy(g_s[first // C1][:, at : at + count], dy_s[:].indirect(entries(dst_sb, first, count)))
 
         def gather_words(first, count):
             nc.vector.tensor_copy(
@@ -114,6 +115,7 @@ def tile_moe_hib_relu_kernel(
         gather_words(0, 128)
         gather_words(128, 128)
         gather_words(256, 256)
+        g_s.append(reuse.tile([P, C1], U8, name="g_s1", tag="gate", align_bytes=64))
         gather_scales(512, 512)
         gather_words(512, 512)
 
@@ -124,7 +126,7 @@ def tile_moe_hib_relu_kernel(
             nc.tensor.matmul_mx(
                 out=sums[:],
                 lhsT=g_w[:, cols].bitcast(FP8X4),
-                lhsT_scale=g_s[:, cols],
+                lhsT_scale=g_s[b * P // C1][:, b * P % C1 : b * P % C1 + P],
                 rhs=wet_w[:, e, :].bitcast(FP4X4),
                 rhs_scale=wet_s[:, e, :],
                 start=True,

@@ -22,6 +22,7 @@ PACK = 4
 PER_COL = 16
 BLOCKS = T // P
 HALF = C1 // 2
+EARLY = T // 2
 
 
 def entries(list_tile, first, count):
@@ -37,8 +38,7 @@ def tile_moe_hib_relu_kernel(
         reuse = ctx.enter_context(tc.tile_pool(name="reuse", bufs=1))
         ring = ctx.enter_context(tc.tile_pool(name="ring", bufs=3))
         psum_z = ctx.enter_context(tc.psum_pool(name="psum_z", bufs=1))
-        psum_t = ctx.enter_context(tc.psum_pool(name="psum_t", bufs=3))
-        psum_x = ctx.enter_context(tc.psum_pool(name="psum_x", bufs=2))
+        psum_t = ctx.enter_context(tc.psum_pool(name="psum_t", bufs=4))
 
         dst_sb = keep.tile([P, T // PER_COL], U16, name="dst_sb")
         offs2_sb = keep.tile([P, T // PER_COL], U16, name="offs2_sb")
@@ -46,7 +46,7 @@ def tile_moe_hib_relu_kernel(
         dy_w = keep.tile([P, T], I32, name="dy_w", align_bytes=64)
         dy_s = keep.tile([P, T], U8, name="dy_s", align_bytes=64)
         g_w = keep.tile([P, T], U32, name="g_w", align_bytes=64)
-        g_s = [keep.tile([P, C1], U8, name="g_s0", align_bytes=64)]
+        g_s = [keep.tile([P, EARLY], U8, name="g_s0", align_bytes=64)]
         wet_w = keep.tile([P, E, 2 * H], U8, name="wet_w", align_bytes=64)
         wet_s = keep.tile([P, E, H], U8, name="wet_s", align_bytes=64)
         wgt_w = keep.tile([P, G, K], I32, name="wgt_w", align_bytes=64)
@@ -54,21 +54,7 @@ def tile_moe_hib_relu_kernel(
         gate_rows = reuse.tile([P, P], F32, name="gate_rows", tag="gate", align_bytes=64)
         gate_cols = keep.tile([P, BLOCKS], F32, name="gate_cols")
         ident = keep.tile([P, P], F32, name="ident")
-        z_first = keep.tile([P, PACK, C1], F32, name="z_first")
-        z_second = [
-            reuse.tile([P, 2, C1], F32, name="z_second01", tag="codes0", align_bytes=64),
-            reuse.tile([P, 1, C1], F32, name="z_second2", tag="last_plane"),
-            keep.tile([P, 1, C1], F32, name="z_second3"),
-        ]
-        spans = [(0, 2), (2, 3), (3, 4)]
-
-        def z_slots(t, first, count):
-            if first < C1:
-                return z_first[:, t, first : first + count]
-            for tile, (lo, hi) in zip(z_second, spans):
-                if lo <= t < hi:
-                    return tile[:, t - lo, first - C1 : first - C1 + count]
-
+        z = keep.tile([P, PACK, T], F32, name="z")
         a_sb = [keep.tile([P, PACK, C1], F32, name="a_sb%d" % f) for f in range(G)]
 
         nc.gpsimd.memset(dy_s[:].bitcast(I32), 0)
@@ -102,94 +88,101 @@ def tile_moe_hib_relu_kernel(
         nc.tensor.transpose(gate_t[:, 0, :], gate_rows[:], ident[:])
         nc.scalar.copy(gate_cols[:], gate_t[:, 0, 0:BLOCKS])
 
-        def gather_scales(first, count):
-            at = first % C1
-            nc.vector.tensor_copy(g_s[first // C1][:, at : at + count], dy_s[:].indirect(entries(dst_sb, first, count)))
+        def gather_scales(tile, first, count):
+            nc.vector.tensor_copy(tile[:], dy_s[:].indirect(entries(dst_sb, first, count)))
 
         def gather_words(first, count):
             nc.vector.tensor_copy(
                 g_w[:, first : first + count], dy_w[:].bitcast(U32).indirect(entries(dst_sb, first, count))
             )
 
-        gather_scales(0, 512)
-        gather_words(0, 128)
-        gather_words(128, 128)
-        gather_words(256, 256)
-        g_s.append(reuse.tile([P, C1], U8, name="g_s1", tag="gate", align_bytes=64))
-        gather_scales(512, 512)
-        gather_words(512, 512)
+        gather_scales(g_s[0], 0, EARLY)
+        gather_words(0, 2 * P)
+        g_s.append(reuse.tile([P, T - EARLY], U8, name="g_s1", tag="gate", align_bytes=64))
+        gather_scales(g_s[1], EARLY, T - EARLY)
+        gather_words(2 * P, T - 2 * P)
+
+        def bank(b, name):
+            return psum_z.tile([P, PACK, P], F32, name=name, tag="bank%d" % (b % PACK))
 
         def first_product(b):
             e = b * P // C2
-            cols = slice(b * P, (b + 1) * P)
-            sums = psum_z.tile([P, H], F32, name="sums", tag="even" if b > 0 and b % 2 == 0 else "odd")
+            at = b * P % EARLY
+            sums = bank(b, "sums")[:].rearrange("m a c -> m (a c)")
             nc.tensor.matmul_mx(
-                out=sums[:],
-                lhsT=g_w[:, cols].bitcast(FP8X4),
-                lhsT_scale=g_s[b * P // C1][:, b * P % C1 : b * P % C1 + P],
+                out=sums,
+                lhsT=g_w[:, b * P : (b + 1) * P].bitcast(FP8X4),
+                lhsT_scale=g_s[b * P // EARLY][:, at : at + P],
                 rhs=wet_w[:, e, :].bitcast(FP4X4),
                 rhs_scale=wet_s[:, e, :],
                 start=True,
                 stop=True,
             )
-            if (b + 1) * P % C1 == 0:
-                z_t = reuse.tile([P, PACK, P], F32, name="z_t_last", tag="sign")
-            else:
-                z_t = ring.tile([P, PACK, P], F32, name="z_t")
-            by_plane = sums[:].rearrange("m (p t) -> m t p", t=PACK)
-            parts = [(0, 1), (1, 2), (2, PACK)] if b == 0 else [(0, PACK)]
-            for lo, hi in parts:
-                nc.scalar.activation(z_t[:, lo:hi, :], by_plane[:, lo:hi, :], ACT.Copy, scale=gate_cols[:, b : b + 1])
-            for lo, hi in parts:
-                if lo == 2:
-                    turned = psum_z.tile([P, PACK, P], F32, name="turned_rest", tag="even")
-                else:
-                    turned = psum_t.tile([P, PACK, P], F32, name="turned")
-                for t in range(lo, hi):
-                    nc.tensor.transpose(turned[:, t, :], z_t[:, t, :], ident[:])
-                if b * P < C1:
-                    nc.scalar.copy(z_first[:, lo:hi, cols], turned[:, lo:hi, :])
-                else:
-                    for tile, (lo2, hi2) in zip(z_second, spans):
-                        nc.scalar.copy(tile[:, :, b * P - C1 : (b + 1) * P - C1], turned[:, lo2:hi2, :])
+            return sums.rearrange("m (p t) -> m t p", t=PACK)
+
+        def turn_plane(t, first, last, turned, staged):
+            count = last - first
+            for n in range(count):
+                b = first + n
+                nc.scalar.activation(staged[:, n, :], by_plane[b][:, t, :], ACT.Copy, scale=gate_cols[:, b : b + 1])
+            for n in range(count):
+                nc.tensor.transpose(turned[:, n, :], staged[:, n, :], ident[:])
+            nc.scalar.copy(z[:, t, first * P : last * P], turned[:, 0:count, :].rearrange("p b m -> p (b m)"))
 
         def relu_slope(f):
-            slope = keep.tile([P, PACK, C1], BF16, name="slope%d" % f)
+            slope = [
+                reuse.tile([P, C1], BF16, name="slope", tag="slope%d_%d" % (f, t), align_bytes=64) for t in range(PACK)
+            ]
             sign = reuse.tile([P, PACK, C1], BF16, name="sign%d" % f, tag="sign")
             for t in range(PACK):
                 nc.scalar.activation(sign[:, t, :], a_sb[f][:, t, :], ACT.Sign)
                 if f == 0:
-                    nc.gpsimd.tensor_scalar(slope[:, t, :], sign[:, t, :], 1.0, 0.0, ALU.min, ALU.max)
+                    nc.gpsimd.tensor_scalar(slope[t][:], sign[:, t, :], 1.0, 0.0, ALU.min, ALU.max)
                 else:
-                    nc.scalar.activation(slope[:, t, :], sign[:, t, :], ACT.Relu)
+                    nc.scalar.activation(slope[t][:], sign[:, t, :], ACT.Relu)
             return slope
 
-        slopes = []
-        for f in range(G):
-            for b in range(f * C1 // P, (f + 1) * C1 // P):
-                first_product(b)
-            slopes.append(relu_slope(f))
+        def staging(last_of_group):
+            if last_of_group:
+                return reuse.tile([P, PACK, P], F32, name="staged_last", tag="sign")
+            return ring.tile([P, PACK, P], F32, name="staged")
+
+        def turning():
+            return psum_t.tile([P, PACK, P], F32, name="turned")
+
+        lead = [1, 1, 2, 2]
+        by_plane = [first_product(b) for b in range(2)]
+        for t in range(PACK):
+            turn_plane(t, 0, lead[t], bank(2 + t, "turned_lead") if t < 2 else turning(), staging(False))
+        by_plane.extend(first_product(b) for b in range(2, 4))
+        for t in range(PACK):
+            turn_plane(t, lead[t], 4, turning(), staging(t == PACK - 1))
+        slopes = [relu_slope(0)]
+        by_plane.extend(first_product(b) for b in range(4, 8))
+        for t in range(PACK):
+            turn_plane(t, 4, 8, turning(), staging(t == PACK - 1))
+        slopes.append(relu_slope(1))
 
         def window(f, t):
-            tag = "last_plane" if (f, t) == (1, PACK - 1) else "z_win%d_%d" % (f, t)
+            tag = "z_win%d" % t if f == 0 else "late%d" % (t % 2)
             return reuse.tile([P, T], F32, name="z_win%d_%d" % (f, t), tag=tag)
 
         def scatter_z(win, t, first, count):
-            nc.vector.tensor_copy(win[:].indirect(entries(offs2_sb, first, count)), z_slots(t, first, count))
+            nc.vector.tensor_copy(win[:].indirect(entries(offs2_sb, first, count)), z[:, t, first : first + count])
 
         def mask_plane(da, f, t, win):
-            nc.gpsimd.tensor_tensor(da[:, :, t], win[:, f * C1 : (f + 1) * C1], slopes[f][:, t, :], ALU.mult)
+            nc.gpsimd.tensor_tensor(da[:, :, t], win[:, f * C1 : (f + 1) * C1], slopes[f][t][:], ALU.mult)
 
         def second_product(f, da):
-            da_w = reuse.tile([P, C1], U32, name="da_w%d" % f, tag="codes%d" % f, align_bytes=64)
+            da_w = reuse.tile([P, C1], U32, name="da_w%d" % f, tag="slope1_0" if f == 0 else "codes1", align_bytes=64)
             da_s = keep.tile([P, C1], U8, name="da_s%d" % f, align_bytes=64)
             nc.vector.quantize_mx(out=da_w[:].bitcast(FP8X4), scales=da_s[:], in_=da[:].rearrange("p j t -> p (j t)"))
             dx = []
             for kb in range(K // P):
                 k_cols = slice(kb * P, (kb + 1) * P)
-                acc = psum_x.tile([P, C1], F32, name="acc")
+                acc = bank(G * f + kb, "acc")[:].rearrange("k a c -> k (a c)")
                 nc.tensor.matmul_mx(
-                    out=acc[:],
+                    out=acc,
                     lhsT=wgt_w[:, f, k_cols].bitcast(FP8X4),
                     lhsT_scale=wgt_s[:, f, k_cols],
                     rhs=da_w[:].bitcast(FP8X4),
@@ -198,7 +191,7 @@ def tile_moe_hib_relu_kernel(
                     stop=True,
                 )
                 dx_sb = keep.tile([P, C1], F32, name="dx%d_%d" % (f, kb))
-                nc.scalar.copy(dx_sb[:], acc[:])
+                nc.scalar.copy(dx_sb[:], acc)
                 dx.append(dx_sb)
             return dx
 
@@ -208,29 +201,22 @@ def tile_moe_hib_relu_kernel(
         da = [keep.tile([P, C1, PACK], BF16, name="da%d" % f, align_bytes=64) for f in range(G)]
         wins = [window(0, t) for t in range(PACK)]
         for t in range(PACK):
-            scatter_z(wins[t], t, 0, P)
-        for t, first, last in [(0, 1, 2), (1, 1, 3), (0, 2, 4), (1, 3, 4), (2, 1, 4), (3, 1, 4)]:
-            scatter_z(wins[t], t, first * P, (last - first) * P)
-            if last == 4:
-                mask_plane(da[0], 0, t, wins[t])
+            scatter_z(wins[t], t, 0, lead[t] * P)
+        for t in range(PACK):
+            scatter_z(wins[t], t, lead[t] * P, C1 - lead[t] * P)
+            mask_plane(da[0], 0, t, wins[t])
 
-        wins = [window(1, t) for t in range(PACK - 1)]
-        for first in (C1, C1 + HALF):
-            for t in range(2):
-                scatter_z(wins[t], t, first, HALF)
-        for t in range(2):
-            mask_plane(da[1], 1, t, wins[t])
-        scatter_z(wins[2], 2, C1, C1)
-        mask_plane(da[1], 1, 2, wins[2])
-        dx_first = second_product(0, da[0])
-        last_win = window(1, PACK - 1)
-        scatter_z(last_win, PACK - 1, C1, C1)
-        mask_plane(da[1], 1, PACK - 1, last_win)
+        for t in range(PACK):
+            if t == 2:
+                dx_first = second_product(0, da[0])
+            win = window(1, t)
+            scatter_z(win, t, C1, C1)
+            mask_plane(da[1], 1, t, win)
 
-        out_low = keep.tile([P, T], F32, name="out_low")
+        out_low = reuse.tile([P, T], F32, name="out_low", tag="late0")
         scatter_dx(out_low, 0, dx_first[0])
         dx_second = second_product(1, da[1])
-        out_high = reuse.tile([P, T], F32, name="out_high", tag="last_plane")
+        out_high = reuse.tile([P, T], F32, name="out_high", tag="late1")
         scatter_dx(out_high, 0, dx_first[1])
         scatter_dx(out_low, 1, dx_second[0])
         nc.sync.dma_start(out[0:P, :], out_low[:])

@@ -22,7 +22,7 @@ PACK = 4
 PER_COL = 16
 BLOCKS = T // P
 HALF = C1 // 2
-EARLY = T // 2
+EARLY = 4 * P
 
 
 def entries(list_tile, first, count):
@@ -107,12 +107,13 @@ def tile_moe_hib_relu_kernel(
 
         def first_product(b):
             e = b * P // C2
-            at = b * P % EARLY
+            late = b * P >= EARLY
+            at = b * P - EARLY if late else b * P
             sums = bank(b, "sums")[:].rearrange("m a c -> m (a c)")
             nc.tensor.matmul_mx(
                 out=sums,
                 lhsT=g_w[:, b * P : (b + 1) * P].bitcast(FP8X4),
-                lhsT_scale=g_s[b * P // EARLY][:, at : at + P],
+                lhsT_scale=g_s[1 if late else 0][:, at : at + P],
                 rhs=wet_w[:, e, :].bitcast(FP4X4),
                 rhs_scale=wet_s[:, e, :],
                 start=True,
@@ -134,7 +135,7 @@ def tile_moe_hib_relu_kernel(
                 reuse.tile([P, C1], BF16, name="slope", tag="slope%d_%d" % (f, t), align_bytes=64) for t in range(PACK)
             ]
             sign = reuse.tile([P, PACK, C1], BF16, name="sign%d" % f, tag="sign")
-            for t in range(PACK):
+            for t in (3, 0, 1, 2) if f == 0 else (2, 0, 1, 3):
                 nc.scalar.activation(sign[:, t, :], a_sb[f][:, t, :], ACT.Sign)
                 if f == 0:
                     nc.gpsimd.tensor_scalar(slope[t][:], sign[:, t, :], 1.0, 0.0, ALU.min, ALU.max)
@@ -150,22 +151,23 @@ def tile_moe_hib_relu_kernel(
         def turning():
             return psum_t.tile([P, PACK, P], F32, name="turned")
 
-        lead = [1, 1, 2, 2]
         by_plane = [first_product(b) for b in range(2)]
-        for t in range(PACK):
-            turn_plane(t, 0, lead[t], bank(2 + t, "turned_lead") if t < 2 else turning(), staging(False))
+        lead = [1, 2, 2, 4]
+        for t in range(2):
+            turn_plane(t, 0, lead[t], bank(2 + t, "turned_lead"), staging(False))
+        turn_plane(2, 0, lead[2], turning(), staging(False))
         by_plane.extend(first_product(b) for b in range(2, 4))
-        for t in range(PACK):
-            turn_plane(t, lead[t], 4, turning(), staging(t == PACK - 1))
+        turn_plane(3, 0, lead[3], turning(), staging(False))
+        for t in range(PACK - 1):
+            turn_plane(t, lead[t], 4, turning(), staging(t == PACK - 2))
         slopes = [relu_slope(0)]
         by_plane.extend(first_product(b) for b in range(4, 8))
-        for t in range(PACK):
+        for t in (2, 0, 1, 3):
             turn_plane(t, 4, 8, turning(), staging(t == PACK - 1))
         slopes.append(relu_slope(1))
 
-        def window(f, t):
-            tag = "z_win%d" % t if f == 0 else "late%d" % (t % 2)
-            return reuse.tile([P, T], F32, name="z_win%d_%d" % (f, t), tag=tag)
+        def window(tag):
+            return reuse.tile([P, T], F32, name="window", tag=tag)
 
         def scatter_z(win, t, first, count):
             nc.vector.tensor_copy(win[:].indirect(entries(offs2_sb, first, count)), z[:, t, first : first + count])
@@ -174,7 +176,7 @@ def tile_moe_hib_relu_kernel(
             nc.gpsimd.tensor_tensor(da[:, :, t], win[:, f * C1 : (f + 1) * C1], slopes[f][t][:], ALU.mult)
 
         def second_product(f, da):
-            da_w = reuse.tile([P, C1], U32, name="da_w%d" % f, tag="slope1_0" if f == 0 else "codes1", align_bytes=64)
+            da_w = reuse.tile([P, C1], U32, name="da_w%d" % f, tag="slope1_2" if f == 0 else "codes1", align_bytes=64)
             da_s = keep.tile([P, C1], U8, name="da_s%d" % f, align_bytes=64)
             nc.vector.quantize_mx(out=da_w[:].bitcast(FP8X4), scales=da_s[:], in_=da[:].rearrange("p j t -> p (j t)"))
             dx = []
@@ -199,24 +201,30 @@ def tile_moe_hib_relu_kernel(
             nc.vector.tensor_copy(out_tile[:].indirect(entries(offs_sb, f * C1, C1)), dx_sb[:])
 
         da = [keep.tile([P, C1, PACK], BF16, name="da%d" % f, align_bytes=64) for f in range(G)]
-        wins = [window(0, t) for t in range(PACK)]
+        wins = [window("plane%d" % t) for t in range(PACK)]
         for t in range(PACK):
             scatter_z(wins[t], t, 0, lead[t] * P)
-        for t in range(PACK):
+        mask_plane(da[0], 0, 3, wins[3])
+        for t in range(2):
             scatter_z(wins[t], t, lead[t] * P, C1 - lead[t] * P)
             mask_plane(da[0], 0, t, wins[t])
+        scatter_z(wins[2], 2, lead[2] * P, T - lead[2] * P)
+        for f in range(G):
+            mask_plane(da[f], f, 2, wins[2])
 
-        for t in range(PACK):
-            if t == 2:
-                dx_first = second_product(0, da[0])
-            win = window(1, t)
-            scatter_z(win, t, C1, C1)
-            mask_plane(da[1], 1, t, win)
+        late = [window("late%d" % t) for t in range(2)]
+        for t in range(2):
+            scatter_z(late[t], t, C1, C1)
+            mask_plane(da[1], 1, t, late[t])
+        dx_first = second_product(0, da[0])
+        last = window("plane2")
+        scatter_z(last, 3, C1, C1)
+        mask_plane(da[1], 1, 3, last)
 
-        out_low = reuse.tile([P, T], F32, name="out_low", tag="late0")
+        out_low = window("late1")
         scatter_dx(out_low, 0, dx_first[0])
         dx_second = second_product(1, da[1])
-        out_high = reuse.tile([P, T], F32, name="out_high", tag="late1")
+        out_high = window("plane2")
         scatter_dx(out_high, 0, dx_first[1])
         scatter_dx(out_low, 1, dx_second[0])
         nc.sync.dma_start(out[0:P, :], out_low[:])

@@ -23,6 +23,7 @@ PER_COL = 16
 BLOCKS = T // P
 HALF = C1 // 2
 EARLY = 4 * P
+FIRST = 2 * P
 
 
 def entries(list_tile, first, count):
@@ -45,7 +46,10 @@ def tile_moe_hib_relu_kernel(
         offs_sb = keep.tile([P, T // PER_COL], U16, name="offs_sb")
         dy_w = keep.tile([P, T], I32, name="dy_w", align_bytes=64)
         dy_s = keep.tile([P, T], U8, name="dy_s", align_bytes=64)
-        g_w = keep.tile([P, T], U32, name="g_w", align_bytes=64)
+        g_w = [
+            reuse.tile([P, FIRST], U32, name="g_w0", tag="first_words", align_bytes=64),
+            keep.tile([P, T - FIRST], U32, name="g_w1", align_bytes=64),
+        ]
         g_s = [keep.tile([P, EARLY], U8, name="g_s0", align_bytes=64)]
         wet_w = keep.tile([P, E, 2 * H], U8, name="wet_w", align_bytes=64)
         wet_s = keep.tile([P, E, H], U8, name="wet_s", align_bytes=64)
@@ -91,16 +95,12 @@ def tile_moe_hib_relu_kernel(
         def gather_scales(tile, first, count):
             nc.vector.tensor_copy(tile[:], dy_s[:].indirect(entries(dst_sb, first, count)))
 
-        def gather_words(first, count):
-            nc.vector.tensor_copy(
-                g_w[:, first : first + count], dy_w[:].bitcast(U32).indirect(entries(dst_sb, first, count))
-            )
+        def gather_words(tile, first, count):
+            nc.vector.tensor_copy(tile[:], dy_w[:].bitcast(U32).indirect(entries(dst_sb, first, count)))
 
         gather_scales(g_s[0], 0, EARLY)
-        gather_words(0, 2 * P)
-        g_s.append(reuse.tile([P, T - EARLY], U8, name="g_s1", tag="gate", align_bytes=64))
-        gather_scales(g_s[1], EARLY, T - EARLY)
-        gather_words(2 * P, T - 2 * P)
+        gather_words(g_w[0], 0, FIRST)
+        gather_words(g_w[1], FIRST, T - FIRST)
 
         def bank(b, name):
             return psum_z.tile([P, PACK, P], F32, name=name, tag="bank%d" % (b % PACK))
@@ -109,10 +109,11 @@ def tile_moe_hib_relu_kernel(
             e = b * P // C2
             late = b * P >= EARLY
             at = b * P - EARLY if late else b * P
+            words = g_w[0][:, b * P : (b + 1) * P] if b * P < FIRST else g_w[1][:, b * P - FIRST : (b + 1) * P - FIRST]
             sums = bank(b, "sums")[:].rearrange("m a c -> m (a c)")
             nc.tensor.matmul_mx(
                 out=sums,
-                lhsT=g_w[:, b * P : (b + 1) * P].bitcast(FP8X4),
+                lhsT=words.bitcast(FP8X4),
                 lhsT_scale=g_s[1 if late else 0][:, at : at + P],
                 rhs=wet_w[:, e, :].bitcast(FP4X4),
                 rhs_scale=wet_s[:, e, :],
@@ -152,6 +153,8 @@ def tile_moe_hib_relu_kernel(
             return psum_t.tile([P, PACK, P], F32, name="turned")
 
         by_plane = [first_product(b) for b in range(2)]
+        g_s.append(reuse.tile([P, T - EARLY], U8, name="g_s1", tag="first_words", align_bytes=64))
+        gather_scales(g_s[1], EARLY, T - EARLY)
         lead = [1, 2, 2, 4]
         for t in range(2):
             turn_plane(t, 0, lead[t], bank(2 + t, "turned_lead"), staging(False))

@@ -100,6 +100,8 @@ def tile_moe_hib_relu_kernel(
 
         gather_scales(g_s[0], 0, EARLY)
         gather_words(g_w[0], 0, FIRST)
+        g_s.append(reuse.tile([P, T - EARLY], U8, name="g_s1", tag="gate", align_bytes=64))
+        gather_scales(g_s[1], EARLY, T - EARLY)
         gather_words(g_w[1], FIRST, T - FIRST)
 
         def bank(b, name):
@@ -131,55 +133,68 @@ def tile_moe_hib_relu_kernel(
                 nc.tensor.transpose(turned[:, n, :], staged[:, n, :], ident[:])
             nc.scalar.copy(z[:, t, first * P : last * P], turned[:, 0:count, :].rearrange("p b m -> p (b m)"))
 
-        def relu_slope(f):
-            slope = [
-                reuse.tile([P, C1], BF16, name="slope", tag="slope%d_%d" % (f, t), align_bytes=64) for t in range(PACK)
-            ]
-            sign = reuse.tile([P, PACK, C1], BF16, name="sign%d" % f, tag="sign")
-            for t in (3, 0, 1, 2) if f == 0 else (2, 0, 1, 3):
-                nc.scalar.activation(sign[:, t, :], a_sb[f][:, t, :], ACT.Sign)
-                if f == 0:
-                    nc.gpsimd.tensor_scalar(slope[t][:], sign[:, t, :], 1.0, 0.0, ALU.min, ALU.max)
-                else:
-                    nc.scalar.activation(slope[t][:], sign[:, t, :], ACT.Relu)
-            return slope
-
-        def staging(last_of_group):
-            if last_of_group:
-                return reuse.tile([P, PACK, P], F32, name="staged_last", tag="sign")
-            return ring.tile([P, PACK, P], F32, name="staged")
-
         def turning():
             return psum_t.tile([P, PACK, P], F32, name="turned")
 
+        def staging(tag=None):
+            if tag:
+                return reuse.tile([P, PACK, P], F32, name="staged_" + tag, tag=tag, align_bytes=64)
+            return ring.tile([P, PACK, P], F32, name="staged")
+
+        def take_sign(f, t):
+            nc.scalar.activation(sign[:, PACK * f + t, :], a_sb[f][:, t, :], ACT.Sign)
+
+        def clamp(f, t, tag):
+            slope = reuse.tile([P, C1], BF16, name="slope", tag=tag, align_bytes=64)
+            if f == 0:
+                nc.gpsimd.tensor_scalar(slope[:], sign[:, t, :], 1.0, 0.0, ALU.min, ALU.max)
+            else:
+                nc.scalar.activation(slope[:], sign[:, PACK + t, :], ACT.Relu)
+            slopes[f, t] = slope
+
+        def relu_slope(f, t):
+            take_sign(f, t)
+            clamp(f, t, "slope%d_%d" % (f, t))
+
         by_plane = [first_product(b) for b in range(2)]
-        g_s.append(reuse.tile([P, T - EARLY], U8, name="g_s1", tag="first_words", align_bytes=64))
-        gather_scales(g_s[1], EARLY, T - EARLY)
-        lead = [1, 2, 2, 4]
-        for t in range(2):
-            turn_plane(t, 0, lead[t], bank(2 + t, "turned_lead"), staging(False))
-        turn_plane(2, 0, lead[2], turning(), staging(False))
+        lead = [2, 2, 1, 4]
+        turn_plane(2, 0, lead[2], bank(2, "turned_lead"), staging())
+        turn_plane(0, 0, lead[0], bank(3, "turned_lead"), staging())
+        turn_plane(1, 0, lead[1], turning(), staging())
         by_plane.extend(first_product(b) for b in range(2, 4))
-        turn_plane(3, 0, lead[3], turning(), staging(False))
-        for t in range(PACK - 1):
-            turn_plane(t, lead[t], 4, turning(), staging(t == PACK - 2))
-        slopes = [relu_slope(0)]
+        turn_plane(3, 0, lead[3], turning(), staging())
+        turn_plane(2, lead[2], 4, turning(), staging())
+        turn_plane(0, lead[0], 4, turning(), staging())
+        turn_plane(1, lead[1], 4, turning(), staging("sign"))
         by_plane.extend(first_product(b) for b in range(4, 8))
-        for t in (2, 0, 1, 3):
-            turn_plane(t, 4, 8, turning(), staging(t == PACK - 1))
-        slopes.append(relu_slope(1))
+        sign = reuse.tile([P, G * PACK, C1], BF16, name="sign", tag="sign", align_bytes=64)
+        slopes = {}
+        turn_plane(0, 4, 8, turning(), staging())
+        relu_slope(0, 3)
+        relu_slope(0, 2)
+        turn_plane(1, 4, 8, turning(), staging())
+        relu_slope(0, 0)
+        relu_slope(1, 0)
+        take_sign(1, 1)
+        slope_head = reuse.tile([P, P], BF16, name="slope_head", tag="last", align_bytes=64)
+        nc.scalar.activation(slope_head[:], sign[:, PACK + 1, 0:P], ACT.Relu)
+        take_sign(0, 1)
+        turn_plane(2, 4, 8, turning(), staging("codes0"))
+        turn_plane(3, 4, 8, turning(), staging("codes0"))
+        take_sign(1, 2)
+        take_sign(1, 3)
 
         def window(tag):
-            return reuse.tile([P, T], F32, name="window", tag=tag)
+            return reuse.tile([P, T], F32, name="window", tag=tag, align_bytes=64)
 
         def scatter_z(win, t, first, count):
             nc.vector.tensor_copy(win[:].indirect(entries(offs2_sb, first, count)), z[:, t, first : first + count])
 
         def mask_plane(da, f, t, win):
-            nc.gpsimd.tensor_tensor(da[:, :, t], win[:, f * C1 : (f + 1) * C1], slopes[f][t][:], ALU.mult)
+            nc.gpsimd.tensor_tensor(da[:, :, t], win[:, f * C1 : (f + 1) * C1], slopes[f, t][:], ALU.mult)
 
         def second_product(f, da):
-            da_w = reuse.tile([P, C1], U32, name="da_w%d" % f, tag="slope1_2" if f == 0 else "codes1", align_bytes=64)
+            da_w = reuse.tile([P, C1], U32, name="da_w%d" % f, tag="codes%d" % f, align_bytes=64)
             da_s = keep.tile([P, C1], U8, name="da_s%d" % f, align_bytes=64)
             nc.vector.quantize_mx(out=da_w[:].bitcast(FP8X4), scales=da_s[:], in_=da[:].rearrange("p j t -> p (j t)"))
             dx = []
@@ -203,31 +218,36 @@ def tile_moe_hib_relu_kernel(
         def scatter_dx(out_tile, f, dx_sb):
             nc.vector.tensor_copy(out_tile[:].indirect(entries(offs_sb, f * C1, C1)), dx_sb[:])
 
-        da = [keep.tile([P, C1, PACK], BF16, name="da%d" % f, align_bytes=64) for f in range(G)]
+        da = [reuse.tile([P, C1, PACK], BF16, name="da", tag="da%d" % f, align_bytes=64) for f in range(G)]
         wins = [window("plane%d" % t) for t in range(PACK)]
-        for t in range(PACK):
+        for t in (2, 0, 1, 3):
             scatter_z(wins[t], t, 0, lead[t] * P)
-        mask_plane(da[0], 0, 3, wins[3])
-        for t in range(2):
-            scatter_z(wins[t], t, lead[t] * P, C1 - lead[t] * P)
+        scatter_z(wins[2], 2, lead[2] * P, C1 - lead[2] * P)
+        for t in (3, 2):
             mask_plane(da[0], 0, t, wins[t])
-        scatter_z(wins[2], 2, lead[2] * P, T - lead[2] * P)
+        scatter_z(wins[0], 0, lead[0] * P, T - lead[0] * P)
         for f in range(G):
-            mask_plane(da[f], f, 2, wins[2])
-
-        late = [window("late%d" % t) for t in range(2)]
-        for t in range(2):
-            scatter_z(late[t], t, C1, C1)
-            mask_plane(da[1], 1, t, late[t])
+            mask_plane(da[f], f, 0, wins[0])
+        clamp(0, 1, "slope1_0")
+        scatter_z(wins[1], 1, lead[1] * P, T - lead[1] * P)
+        mask_plane(da[0], 0, 1, wins[1])
+        nc.gpsimd.tensor_tensor(da[1][:, 0:P, 1], wins[1][:, C1 : C1 + P], slope_head[:], ALU.mult)
+        scatter_z(wins[2], 2, C1, C1)
         dx_first = second_product(0, da[0])
-        last = window("plane2")
+        held = reuse.tile([P, 2, C1], BF16, name="held", tag="da0", align_bytes=64)
+        nc.scalar.activation(held[:, 0, P:C1], sign[:, PACK + 1, P:C1], ACT.Relu)
+        nc.scalar.activation(held[:, 1, :], sign[:, PACK + 2, :], ACT.Relu)
+        nc.gpsimd.tensor_tensor(da[1][:, P:C1, 1], wins[1][:, C1 + P : T], held[:, 0, P:C1], ALU.mult)
+        nc.gpsimd.tensor_tensor(da[1][:, :, 2], wins[2][:, C1:T], held[:, 1, :], ALU.mult)
+        clamp(1, 3, "codes0")
+        last = window("last")
         scatter_z(last, 3, C1, C1)
         mask_plane(da[1], 1, 3, last)
 
-        out_low = window("late1")
+        out_low = window("out_low")
         scatter_dx(out_low, 0, dx_first[0])
         dx_second = second_product(1, da[1])
-        out_high = window("plane2")
+        out_high = window("last")
         scatter_dx(out_high, 0, dx_first[1])
         scatter_dx(out_low, 1, dx_second[0])
         nc.sync.dma_start(out[0:P, :], out_low[:])

@@ -69,15 +69,16 @@ def tile_moe_hib_relu_kernel(
 
         nc.sync.dma_start(dst_sb[:], dst)
         for q in range(4):
-            nc.sync.dma_start(dy_s[32 * q : 32 * q + 4, :].bitcast(I32), dy_scales[0, 4 * q : 4 * q + 4, :].bitcast(I32))
+            queue = nc.sync if q < 3 else nc.scalar
+            queue.dma_start(dy_s[32 * q : 32 * q + 4, :].bitcast(I32), dy_scales[0, 4 * q : 4 * q + 4, :].bitcast(I32))
         nc.sync.dma_start(dy_w[:], dy_words[0].rearrange("p n d -> p (n d)").bitcast(I32))
+        nc.sync.dma_start(offs2_sb[:], offs2)
         nc.sync.dma_start(gate_rows[0:BLOCKS, :], gate[0].rearrange("(b c) -> b c", c=P))
         wet_src = wet_words.rearrange("e s p c -> p (e s) c").bitcast(I32)
         nc.sync.dma_start(wet_w[:, 0:1, :].bitcast(I32), wet_src[:, 0:1, :])
         wet_s_src = wet_scales.rearrange("e s r h -> r (e s) h").bitcast(I32)
         for q in range(4):
             nc.sync.dma_start(wet_s[32 * q : 32 * q + 4, :, :].bitcast(I32), wet_s_src[4 * q : 4 * q + 4, :, :])
-        nc.sync.dma_start(offs2_sb[:], offs2)
         nc.sync.dma_start(wet_w[:, 1:4, :].bitcast(I32), wet_src[:, 1:4, :])
         a_src = a.rearrange("(p t) j -> p t j", t=PACK)
         for f in range(G):

@@ -61,7 +61,10 @@ def tile_moe_hib_relu_kernel(
         z = keep.tile([P, PACK, T], F32, name="z")
         a_sb = [keep.tile([P, PACK, C1], F32, name="a_sb%d" % f) for f in range(G)]
 
-        nc.gpsimd.memset(dy_s[:].bitcast(I32), 0)
+        dy_s_words = dy_s[:].bitcast(I32)
+        nc.gpsimd.memset(dy_s_words[:, 0:P], 0)
+        nc.vector.memset(dy_s_words[:, P : 2 * P - 1], 0)
+        nc.vector.memset(dy_s_words[:, 2 * P - 1 : 2 * P], 0)
         nc.gpsimd.memset(gate_rows[:], 0.0)
         nc.gpsimd.memset(wet_s[:].rearrange("p e h -> p (e h)").bitcast(I32), 0)
         make_identity(nc, ident[:])

@@ -62,20 +62,19 @@ def tile_moe_hib_relu_kernel(
         a_sb = [keep.tile([P, PACK, C1], F32, name="a_sb%d" % f) for f in range(G)]
 
         dy_s_words = dy_s[:].bitcast(I32)
-        nc.gpsimd.memset(dy_s_words[:, 0:P], 0)
-        nc.vector.memset(dy_s_words[:, P : 2 * P - 1], 0)
-        nc.vector.memset(dy_s_words[:, 2 * P - 1 : 2 * P], 0)
-        nc.gpsimd.memset(gate_rows[:], 0.0)
-        nc.gpsimd.memset(wet_s[:].rearrange("p e h -> p (e h)").bitcast(I32), 0)
-        make_identity(nc, ident[:])
-        nc.gpsimd.memset(wgt_s[:].rearrange("p f k -> p (f k)").bitcast(I32), 0)
+        nc.vector.memset(dy_s_words, 0)
+        nc.vector.memset(gate_rows[:], 0.0)
+        nc.vector.memset(wet_s[:].rearrange("p e h -> p (e h)").bitcast(I32), 0)
+        nc.vector.memset(wgt_s[:].rearrange("p f k -> p (f k)").bitcast(I32), 0)
+        nc.vector.memset(ident[:], 0.0)
+        make_identity(nc, ident[:], nomemset=True)
 
         nc.sync.dma_start(dst_sb[:], dst)
+        nc.sync.dma_start(offs2_sb[:], offs2)
         for q in range(4):
             queue = nc.sync if q < 3 else nc.scalar
             queue.dma_start(dy_s[32 * q : 32 * q + 4, :].bitcast(I32), dy_scales[0, 4 * q : 4 * q + 4, :].bitcast(I32))
         nc.sync.dma_start(dy_w[:], dy_words[0].rearrange("p n d -> p (n d)").bitcast(I32))
-        nc.sync.dma_start(offs2_sb[:], offs2)
         nc.sync.dma_start(gate_rows[0:BLOCKS, :], gate[0].rearrange("(b c) -> b c", c=P))
         wet_src = wet_words.rearrange("e s p c -> p (e s) c").bitcast(I32)
         nc.sync.dma_start(wet_w[:, 0:1, :].bitcast(I32), wet_src[:, 0:1, :])

@@ -21,13 +21,15 @@ P = 128
 PACK = 4
 PER_COL = 16
 BLOCKS = T // P
-HALF = C1 // 2
-EARLY = 4 * P
 FIRST = 2 * P
 
 
 def entries(list_tile, first, count):
     return list_tile[:, first // PER_COL : (first + count) // PER_COL]
+
+
+def words_of(plane):
+    return plane[:].rearrange("p e h -> p (e h)").bitcast(I32)
 
 
 def tile_moe_hib_relu_kernel(
@@ -37,7 +39,6 @@ def tile_moe_hib_relu_kernel(
     with ExitStack() as ctx:
         keep = ctx.enter_context(tc.tile_pool(name="keep", bufs=1))
         reuse = ctx.enter_context(tc.tile_pool(name="reuse", bufs=1))
-        ring = ctx.enter_context(tc.tile_pool(name="ring", bufs=3))
         psum_z = ctx.enter_context(tc.psum_pool(name="psum_z", bufs=1))
         psum_t = ctx.enter_context(tc.psum_pool(name="psum_t", bufs=4))
 
@@ -47,10 +48,10 @@ def tile_moe_hib_relu_kernel(
         dy_w = keep.tile([P, T], I32, name="dy_w", align_bytes=64)
         dy_s = keep.tile([P, T], U8, name="dy_s", align_bytes=64)
         g_w = [
-            reuse.tile([P, FIRST], U32, name="g_w0", tag="first_words", align_bytes=64),
+            keep.tile([P, FIRST], U32, name="g_w0", align_bytes=64),
             keep.tile([P, T - FIRST], U32, name="g_w1", align_bytes=64),
         ]
-        g_s = [keep.tile([P, EARLY], U8, name="g_s0", align_bytes=64)]
+        g_s = [keep.tile([P, C1], U8, name="g_s0", align_bytes=64)]
         wet_w = keep.tile([P, E, 2 * H], U8, name="wet_w", align_bytes=64)
         wet_s = keep.tile([P, E, H], U8, name="wet_s", align_bytes=64)
         wgt_w = keep.tile([P, G, K], I32, name="wgt_w", align_bytes=64)
@@ -62,145 +63,110 @@ def tile_moe_hib_relu_kernel(
         a_sb = [keep.tile([P, PACK, C1], F32, name="a_sb%d" % f) for f in range(G)]
 
         dy_s_words = dy_s[:].bitcast(I32)
-        nc.vector.memset(dy_s_words, 0)
-        nc.vector.memset(gate_rows[:], 0.0)
-        nc.vector.memset(wet_s[:].rearrange("p e h -> p (e h)").bitcast(I32), 0)
-        nc.vector.memset(wgt_s[:].rearrange("p f k -> p (f k)").bitcast(I32), 0)
-        nc.vector.memset(ident[:], 0.0)
-        make_identity(nc, ident[:], nomemset=True)
+        nc.gpsimd.memset(dy_s_words[:, 0:P], 0)
+        nc.vector.memset(dy_s_words[:, P : 2 * P - 1], 0)
+        nc.vector.memset(dy_s_words[:, 2 * P - 1 : 2 * P], 0)
+        nc.gpsimd.memset(gate_rows[:], 0.0)
+        nc.gpsimd.memset(words_of(wet_s), 0)
+        make_identity(nc, ident[:])
+        nc.gpsimd.memset(words_of(wgt_s), 0)
 
+        def load_scale_rows(plane, rows):
+            for q in range(4):
+                nc.sync.dma_start(plane[32 * q : 32 * q + 4, :, :].bitcast(I32), rows[4 * q : 4 * q + 4, :, :])
+
+        def gather_scales(tile, window, first, count):
+            nc.vector.tensor_copy(tile[:], window[:].indirect(entries(dst_sb, first, count)))
+
+        def gather_words(tile, first, count):
+            nc.vector.tensor_copy(tile[:], dy_w[:].bitcast(U32).indirect(entries(dst_sb, first, count)))
+
+        wet_src = wet_words.rearrange("e s p c -> p (e s) c").bitcast(I32)
+        wet_s_src = wet_scales.rearrange("e s r h -> r (e s) h").bitcast(I32)
+        a_src = a.rearrange("(p t) j -> p t j", t=PACK)
         nc.sync.dma_start(dst_sb[:], dst)
-        nc.sync.dma_start(offs2_sb[:], offs2)
         for q in range(4):
             queue = nc.sync if q < 3 else nc.scalar
             queue.dma_start(dy_s[32 * q : 32 * q + 4, :].bitcast(I32), dy_scales[0, 4 * q : 4 * q + 4, :].bitcast(I32))
         nc.sync.dma_start(dy_w[:], dy_words[0].rearrange("p n d -> p (n d)").bitcast(I32))
+        nc.sync.dma_start(offs2_sb[:], offs2)
         nc.sync.dma_start(gate_rows[0:BLOCKS, :], gate[0].rearrange("(b c) -> b c", c=P))
-        wet_src = wet_words.rearrange("e s p c -> p (e s) c").bitcast(I32)
         nc.sync.dma_start(wet_w[:, 0:1, :].bitcast(I32), wet_src[:, 0:1, :])
-        wet_s_src = wet_scales.rearrange("e s r h -> r (e s) h").bitcast(I32)
-        for q in range(4):
-            nc.sync.dma_start(wet_s[32 * q : 32 * q + 4, :, :].bitcast(I32), wet_s_src[4 * q : 4 * q + 4, :, :])
-        nc.sync.dma_start(wet_w[:, 1:4, :].bitcast(I32), wet_src[:, 1:4, :])
-        a_src = a.rearrange("(p t) j -> p t j", t=PACK)
+        load_scale_rows(wet_s, wet_s_src)
+        nc.sync.dma_start(wet_w[:, 1:E, :].bitcast(I32), wet_src[:, 1:E, :])
         for f in range(G):
             nc.sync.dma_start(a_sb[f][:], a_src[:, :, f * C1 : (f + 1) * C1])
         nc.sync.dma_start(wgt_w[:], wgt_words.rearrange("f s p k d -> p (f s) (k d)").bitcast(I32))
-        wgt_s_src = wgt_scales.rearrange("f s r k -> r (f s) k").bitcast(I32)
-        for q in range(4):
-            nc.sync.dma_start(wgt_s[32 * q : 32 * q + 4, :, :].bitcast(I32), wgt_s_src[4 * q : 4 * q + 4, :, :])
+        load_scale_rows(wgt_s, wgt_scales.rearrange("f s r k -> r (f s) k").bitcast(I32))
         nc.sync.dma_start(offs_sb[:], offs)
 
         gate_t = psum_t.tile([P, PACK, P], F32, name="turned")
         nc.tensor.transpose(gate_t[:, 0, :], gate_rows[:], ident[:])
         nc.scalar.copy(gate_cols[:], gate_t[:, 0, 0:BLOCKS])
 
-        def gather_scales(tile, first, count):
-            nc.vector.tensor_copy(tile[:], dy_s[:].indirect(entries(dst_sb, first, count)))
-
-        def gather_words(tile, first, count):
-            nc.vector.tensor_copy(tile[:], dy_w[:].bitcast(U32).indirect(entries(dst_sb, first, count)))
-
-        gather_scales(g_s[0], 0, EARLY)
+        gather_scales(g_s[0], dy_s, 0, C1)
         gather_words(g_w[0], 0, FIRST)
-        g_s.append(reuse.tile([P, T - EARLY], U8, name="g_s1", tag="gate", align_bytes=64))
-        gather_scales(g_s[1], EARLY, T - EARLY)
+        g_s.append(reuse.tile([P, C1], U8, name="g_s1", tag="gate", align_bytes=64))
+        gather_scales(g_s[1], dy_s, C1, C1)
         gather_words(g_w[1], FIRST, T - FIRST)
 
-        def bank(b, name):
-            return psum_z.tile([P, PACK, P], F32, name=name, tag="bank%d" % (b % PACK))
+        def bank(n, name):
+            return psum_z.tile([P, PACK, P], F32, name=name, tag="bank%d" % n)
+
+        sums = {}
 
         def first_product(b):
             e = b * P // C2
-            late = b * P >= EARLY
-            at = b * P - EARLY if late else b * P
             words = g_w[0][:, b * P : (b + 1) * P] if b * P < FIRST else g_w[1][:, b * P - FIRST : (b + 1) * P - FIRST]
-            sums = bank(b, "sums")[:].rearrange("m a c -> m (a c)")
+            scales = g_s[b // PACK][:, b % PACK * P : (b % PACK + 1) * P]
+            acc = bank(b % PACK, "sums")[:].rearrange("m a c -> m (a c)")
             nc.tensor.matmul_mx(
-                out=sums,
+                out=acc,
                 lhsT=words.bitcast(FP8X4),
-                lhsT_scale=g_s[1 if late else 0][:, at : at + P],
+                lhsT_scale=scales,
                 rhs=wet_w[:, e, :].bitcast(FP4X4),
                 rhs_scale=wet_s[:, e, :],
                 start=True,
                 stop=True,
             )
-            return sums.rearrange("m (p t) -> m t p", t=PACK)
+            sums[b] = acc.rearrange("m (p t) -> m t p", t=PACK)
 
-        def turn_plane(t, first, last, turned, staged):
-            count = last - first
-            for n in range(count):
-                b = first + n
-                nc.scalar.activation(staged[:, n, :], by_plane[b][:, t, :], ACT.Copy, scale=gate_cols[:, b : b + 1])
-            for n in range(count):
-                nc.tensor.transpose(turned[:, n, :], staged[:, n, :], ident[:])
-            nc.scalar.copy(z[:, t, first * P : last * P], turned[:, 0:count, :].rearrange("p b m -> p (b m)"))
+        staged = {}
 
-        def turning():
-            return psum_t.tile([P, PACK, P], F32, name="turned")
+        def stage(blocks, planes, tag):
+            tile = reuse.tile([P, len(blocks), len(planes), P], F32, name="staged", tag=tag, align_bytes=64)
+            for n, b in enumerate(blocks):
+                nc.scalar.activation(
+                    tile[:, n, :, :], sums[b][:, planes.start : planes.stop, :], ACT.Copy, scale=gate_cols[:, b : b + 1]
+                )
+                for t in planes:
+                    staged[b, t] = tile[:, n, t - planes.start, :]
 
-        def staging(tag=None):
-            if tag:
-                return reuse.tile([P, PACK, P], F32, name="staged_" + tag, tag=tag, align_bytes=64)
-            return ring.tile([P, PACK, P], F32, name="staged")
+        def turn(pieces, into, turned=None):
+            if turned is None:
+                turned = psum_t.tile([P, PACK, P], F32, name="turned")
+            for n, piece in enumerate(pieces):
+                nc.tensor.transpose(turned[:, n, :], staged[piece], ident[:])
+            nc.scalar.copy(into, turned[:, 0 : len(pieces), :])
+
+        def turn_plane(t, blocks, turned=None):
+            into = z[:, t, blocks.start * P : blocks.stop * P].rearrange("p (b m) -> p b m", m=P)
+            turn([(b, t) for b in blocks], into, turned)
 
         def take_sign(f, t):
-            nc.scalar.activation(sign[:, PACK * f + t, :], a_sb[f][:, t, :], ACT.Sign)
+            nc.scalar.activation(sign[f][:, t, :], a_sb[f][:, t, :], ACT.Sign)
 
-        def clamp(f, t, tag):
-            slope = reuse.tile([P, C1], BF16, name="slope", tag=tag, align_bytes=64)
-            if f == 0:
-                nc.gpsimd.tensor_scalar(slope[:], sign[:, t, :], 1.0, 0.0, ALU.min, ALU.max)
-            else:
-                nc.scalar.activation(slope[:], sign[:, PACK + t, :], ACT.Relu)
-            slopes[f, t] = slope
+        def scatter_z(win, source, first, count):
+            nc.vector.tensor_copy(win[:].indirect(entries(offs2_sb, first, count)), source)
 
-        def relu_slope(f, t):
-            take_sign(f, t)
-            clamp(f, t, "slope%d_%d" % (f, t))
+        def mask_plane(f, t, slope, first=0, last=C1):
+            nc.gpsimd.tensor_tensor(da[f][:, first:last, t], wins[t][:, f * C1 + first : f * C1 + last], slope, ALU.mult)
 
-        by_plane = [first_product(b) for b in range(2)]
-        lead = [2, 2, 1, 4]
-        turn_plane(2, 0, lead[2], bank(2, "turned_lead"), staging())
-        turn_plane(0, 0, lead[0], bank(3, "turned_lead"), staging())
-        turn_plane(1, 0, lead[1], turning(), staging())
-        by_plane.extend(first_product(b) for b in range(2, 4))
-        turn_plane(3, 0, lead[3], turning(), staging())
-        turn_plane(2, lead[2], 4, turning(), staging())
-        turn_plane(0, lead[0], 4, turning(), staging())
-        turn_plane(1, lead[1], 4, turning(), staging("sign"))
-        by_plane.extend(first_product(b) for b in range(4, 8))
-        sign = reuse.tile([P, G * PACK, C1], BF16, name="sign", tag="sign", align_bytes=64)
-        slopes = {}
-        turn_plane(0, 4, 8, turning(), staging())
-        relu_slope(0, 3)
-        relu_slope(0, 2)
-        turn_plane(1, 4, 8, turning(), staging())
-        relu_slope(0, 0)
-        relu_slope(1, 0)
-        take_sign(1, 1)
-        slope_head = reuse.tile([P, P], BF16, name="slope_head", tag="last", align_bytes=64)
-        nc.scalar.activation(slope_head[:], sign[:, PACK + 1, 0:P], ACT.Relu)
-        take_sign(0, 1)
-        turn_plane(2, 4, 8, turning(), staging("codes0"))
-        turn_plane(3, 4, 8, turning(), staging("codes0"))
-        take_sign(1, 2)
-        take_sign(1, 3)
-
-        def window(tag):
-            return reuse.tile([P, T], F32, name="window", tag=tag, align_bytes=64)
-
-        def scatter_z(win, t, first, count):
-            nc.vector.tensor_copy(win[:].indirect(entries(offs2_sb, first, count)), z[:, t, first : first + count])
-
-        def mask_plane(da, f, t, win):
-            nc.gpsimd.tensor_tensor(da[:, :, t], win[:, f * C1 : (f + 1) * C1], slopes[f, t][:], ALU.mult)
-
-        def second_product(f, da):
-            da_w = reuse.tile([P, C1], U32, name="da_w%d" % f, tag="codes%d" % f, align_bytes=64)
+        def second_product(f):
+            da_w = keep.tile([P, C1], U32, name="da_w%d" % f, align_bytes=64)
             da_s = keep.tile([P, C1], U8, name="da_s%d" % f, align_bytes=64)
-            nc.vector.quantize_mx(out=da_w[:].bitcast(FP8X4), scales=da_s[:], in_=da[:].rearrange("p j t -> p (j t)"))
-            dx = []
+            nc.vector.quantize_mx(out=da_w[:].bitcast(FP8X4), scales=da_s[:], in_=da[f][:].rearrange("p j t -> p (j t)"))
+            accs = []
             for kb in range(K // P):
                 k_cols = slice(kb * P, (kb + 1) * P)
                 acc = bank(G * f + kb, "acc")[:].rearrange("k a c -> k (a c)")
@@ -213,44 +179,93 @@ def tile_moe_hib_relu_kernel(
                     start=True,
                     stop=True,
                 )
-                dx_sb = keep.tile([P, C1], F32, name="dx%d_%d" % (f, kb))
-                nc.scalar.copy(dx_sb[:], acc)
-                dx.append(dx_sb)
-            return dx
+                accs.append(acc)
+            return accs
+
+        def leave_psum(acc, name):
+            dx_sb = keep.tile([P, C1], F32, name=name)
+            nc.scalar.copy(dx_sb[:], acc)
+            return dx_sb
 
         def scatter_dx(out_tile, f, dx_sb):
             nc.vector.tensor_copy(out_tile[:].indirect(entries(offs_sb, f * C1, C1)), dx_sb[:])
 
+        lead, pair, rest, late = range(0, 1), range(0, 2), range(2, 4), range(4, 8)
+        wins = [reuse.tile([P, T], F32, name="win", tag="win%d" % t, align_bytes=64) for t in range(PACK)]
         da = [reuse.tile([P, C1, PACK], BF16, name="da", tag="da%d" % f, align_bytes=64) for f in range(G)]
-        wins = [window("plane%d" % t) for t in range(PACK)]
-        for t in (2, 0, 1, 3):
-            scatter_z(wins[t], t, 0, lead[t] * P)
-        scatter_z(wins[2], 2, lead[2] * P, C1 - lead[2] * P)
-        for t in (3, 2):
-            mask_plane(da[0], 0, t, wins[t])
-        scatter_z(wins[0], 0, lead[0] * P, T - lead[0] * P)
-        for f in range(G):
-            mask_plane(da[f], f, 0, wins[0])
-        clamp(0, 1, "slope1_0")
-        scatter_z(wins[1], 1, lead[1] * P, T - lead[1] * P)
-        mask_plane(da[0], 0, 1, wins[1])
-        nc.gpsimd.tensor_tensor(da[1][:, 0:P, 1], wins[1][:, C1 : C1 + P], slope_head[:], ALU.mult)
-        scatter_z(wins[2], 2, C1, C1)
-        dx_first = second_product(0, da[0])
-        held = reuse.tile([P, 2, C1], BF16, name="held", tag="da0", align_bytes=64)
-        nc.scalar.activation(held[:, 0, P:C1], sign[:, PACK + 1, P:C1], ACT.Relu)
-        nc.scalar.activation(held[:, 1, :], sign[:, PACK + 2, :], ACT.Relu)
-        nc.gpsimd.tensor_tensor(da[1][:, P:C1, 1], wins[1][:, C1 + P : T], held[:, 0, P:C1], ALU.mult)
-        nc.gpsimd.tensor_tensor(da[1][:, :, 2], wins[2][:, C1:T], held[:, 1, :], ALU.mult)
-        clamp(1, 3, "codes0")
-        last = window("last")
-        scatter_z(last, 3, C1, C1)
-        mask_plane(da[1], 1, 3, last)
 
-        out_low = window("out_low")
+        first_product(0)
+        first_product(1)
+        stage(lead, range(3, 4), "lead3")
+        turn_plane(3, lead, bank(2, "turned_lead"))
+        scatter_z(wins[3], z[:, 3, 0:P], 0, P)
+        stage(lead, range(2, 3), "lead2")
+        turn_plane(2, lead, bank(3, "turned_lead"))
+        scatter_z(wins[2], z[:, 2, 0:P], 0, P)
+        for t in (0, 1):
+            stage(pair, range(t, t + 1), "pair%d" % t)
+            turn_plane(t, pair)
+            scatter_z(wins[t], z[:, t, 0:FIRST], 0, FIRST)
+
+        first_product(2)
+        first_product(3)
+        stage(range(1, 2), range(2, 4), "second")
+        stage(rest, range(0, 4), "rest")
+        for t in (3, 2):
+            turn_plane(t, range(1, 4), bank(3 - t, "turned_rest"))
+            scatter_z(wins[t], z[:, t, P:C1], P, C1 - P)
+        turn_plane(0, rest)
+        for b in late:
+            first_product(b)
+        stage(late, range(0, 1), "sign0")
+        turn_plane(0, late)
+        scatter_z(wins[0], z[:, 0, FIRST:T], FIRST, T - FIRST)
+
+        sign = [reuse.tile([P, PACK, C1], BF16, name="sign", tag="sign0", align_bytes=64)]
+        slope_first = {}
+        for t in (3, 2, 0, 1):
+            take_sign(0, t)
+            slope_first[t] = reuse.tile([P, C1], BF16, name="slope", tag="slope%d" % t, align_bytes=64)
+            nc.gpsimd.tensor_scalar(slope_first[t][:], sign[0][:, t, :], 1.0, 0.0, ALU.min, ALU.max)
+            if t != 1:
+                mask_plane(0, t, slope_first[t][:])
+        turn_plane(1, rest)
+        stage(late, range(1, 4), "late123")
+        turn_plane(1, late)
+        scatter_z(wins[1], z[:, 1, FIRST:T], FIRST, T - FIRST)
+        turn_plane(3, late)
+
+        sign.append(reuse.tile([P, PACK, C1], BF16, name="sign", tag="rest", align_bytes=64))
+        take_sign(1, 0)
+        slope_early = keep.tile([P, C1 + P], BF16, name="slope_early", align_bytes=64)
+        nc.scalar.activation(slope_early[:, 0:C1], sign[1][:, 0, :], ACT.Relu)
+        mask_plane(1, 0, slope_early[:, 0:C1])
+        take_sign(1, 1)
+        nc.scalar.activation(slope_early[:, C1 : C1 + P], sign[1][:, 1, 0:P], ACT.Relu)
+        take_sign(1, 3)
+        take_sign(1, 2)
+        mask_plane(0, 1, slope_first[1][:])
+        mask_plane(1, 1, slope_early[:, C1 : C1 + P], 0, P)
+        scatter_z(wins[3], z[:, 3, C1:T], C1, C1)
+
+        accs = second_product(0)
+        z_last = reuse.tile([P, PACK, P], F32, name="z_last", tag="slope1", align_bytes=64)
+        turn([(b, 2) for b in late], z_last[:])
+        scatter_z(wins[2], z_last[:].rearrange("p b m -> p (b m)"), C1, C1)
+        held = reuse.tile([P, 3, C1], BF16, name="held", tag="da0", align_bytes=64)
+        nc.scalar.activation(held[:, 0, P:C1], sign[1][:, 1, P:C1], ACT.Relu)
+        mask_plane(1, 1, held[:, 0, P:C1], P, C1)
+        nc.scalar.activation(held[:, 1, :], sign[1][:, 3, :], ACT.Relu)
+        mask_plane(1, 3, held[:, 1, :])
+        dx_first = [leave_psum(accs[0], "dx00")]
+        nc.scalar.activation(held[:, 2, :], sign[1][:, 2, :], ACT.Relu)
+        mask_plane(1, 2, held[:, 2, :])
+        dx_first.append(leave_psum(accs[1], "dx01"))
+
+        out_low = keep.tile([P, T], F32, name="out_low", align_bytes=64)
         scatter_dx(out_low, 0, dx_first[0])
-        dx_second = second_product(1, da[1])
-        out_high = window("last")
+        dx_second = [leave_psum(acc, "dx1%d" % kb) for kb, acc in enumerate(second_product(1))]
+        out_high = reuse.tile([P, T], F32, name="out_high", tag="win2", align_bytes=64)
         scatter_dx(out_high, 0, dx_first[1])
         scatter_dx(out_low, 1, dx_second[0])
         nc.sync.dma_start(out[0:P, :], out_low[:])

@@ -47,13 +47,16 @@ def tile_moe_hib_relu_kernel(
         offs_sb = keep.tile([P, T // PER_COL], U16, name="offs_sb")
         dy_w = keep.tile([P, T], I32, name="dy_w", align_bytes=64)
         dy_s = keep.tile([P, T], U8, name="dy_s", align_bytes=64)
+        dy_s_spread = keep.tile([P, T], U8, name="dy_s_spread", align_bytes=64)
         g_w = [
             keep.tile([P, FIRST], U32, name="g_w0", align_bytes=64),
             keep.tile([P, T - FIRST], U32, name="g_w1", align_bytes=64),
         ]
-        g_s = [keep.tile([P, C1], U8, name="g_s0", align_bytes=64)]
+        g_s_first = keep.tile([P, FIRST], U8, name="g_s_first", align_bytes=64)
+        g_s_spread = keep.tile([P, C1], U8, name="g_s_spread", align_bytes=64)
+        g_s_late = keep.tile([P, C1], U8, name="g_s_late", align_bytes=64)
         wet_w = keep.tile([P, E, 2 * H], U8, name="wet_w", align_bytes=64)
-        wet_s = keep.tile([P, E, H], U8, name="wet_s", align_bytes=64)
+        wet_s = [keep.tile([P, E // G, H], U8, name="wet_s%d" % f, align_bytes=64) for f in range(G)]
         wgt_w = keep.tile([P, G, K], I32, name="wgt_w", align_bytes=64)
         wgt_s = keep.tile([P, G, K], U8, name="wgt_s", align_bytes=64)
         gate_rows = reuse.tile([P, P], F32, name="gate_rows", tag="gate", align_bytes=64)
@@ -63,12 +66,14 @@ def tile_moe_hib_relu_kernel(
         a_sb = [keep.tile([P, PACK, C1], F32, name="a_sb%d" % f) for f in range(G)]
 
         dy_s_words = dy_s[:].bitcast(I32)
-        nc.gpsimd.memset(dy_s_words[:, 0:P], 0)
-        nc.vector.memset(dy_s_words[:, P : 2 * P - 1], 0)
+        nc.gpsimd.memset(dy_s_spread[:].bitcast(I32), 0)
+        nc.vector.memset(dy_s_words[:, 0 : 2 * P - 1], 0)
         nc.vector.memset(dy_s_words[:, 2 * P - 1 : 2 * P], 0)
         nc.gpsimd.memset(gate_rows[:], 0.0)
-        nc.gpsimd.memset(words_of(wet_s), 0)
+        nc.gpsimd.memset(words_of(wet_s[0]), 0)
         make_identity(nc, ident[:])
+        nc.gpsimd.memset(words_of(wet_s[1]), 0)
+        nc.gpsimd.memset(g_s_late[:].bitcast(I32), 0)
         nc.gpsimd.memset(words_of(wgt_s), 0)
 
         def load_scale_rows(plane, rows):
@@ -85,15 +90,21 @@ def tile_moe_hib_relu_kernel(
         wet_s_src = wet_scales.rearrange("e s r h -> r (e s) h").bitcast(I32)
         a_src = a.rearrange("(p t) j -> p t j", t=PACK)
         nc.sync.dma_start(dst_sb[:], dst)
+        nc.sync.dma_start(dy_s_spread[0:P:8, :].bitcast(I32), dy_scales[0].bitcast(I32))
         for q in range(4):
             queue = nc.sync if q < 3 else nc.scalar
             queue.dma_start(dy_s[32 * q : 32 * q + 4, :].bitcast(I32), dy_scales[0, 4 * q : 4 * q + 4, :].bitcast(I32))
         nc.sync.dma_start(dy_w[:], dy_words[0].rearrange("p n d -> p (n d)").bitcast(I32))
-        nc.sync.dma_start(offs2_sb[:], offs2)
         nc.sync.dma_start(gate_rows[0:BLOCKS, :], gate[0].rearrange("(b c) -> b c", c=P))
         nc.sync.dma_start(wet_w[:, 0:1, :].bitcast(I32), wet_src[:, 0:1, :])
-        load_scale_rows(wet_s, wet_s_src)
+        load_scale_rows(wet_s[0], wet_s_src[:, 0:2, :])
+        nc.sync.dma_start(offs2_sb[:], offs2)
         nc.sync.dma_start(wet_w[:, 1:E, :].bitcast(I32), wet_src[:, 1:E, :])
+        load_scale_rows(wet_s[1], wet_s_src[:, 2:4, :])
+        gather_scales(g_s_spread, dy_s_spread, C1, C1)
+        for q in range(4):
+            rows = g_s_spread[32 * q : 32 * q + 32 : 8, :].bitcast(I32)
+            nc.sync.dma_start(g_s_late[32 * q : 32 * q + 4, :].bitcast(I32), rows)
         for f in range(G):
             nc.sync.dma_start(a_sb[f][:], a_src[:, :, f * C1 : (f + 1) * C1])
         nc.sync.dma_start(wgt_w[:], wgt_words.rearrange("f s p k d -> p (f s) (k d)").bitcast(I32))
@@ -104,11 +115,11 @@ def tile_moe_hib_relu_kernel(
         nc.tensor.transpose(gate_t[:, 0, :], gate_rows[:], ident[:])
         nc.scalar.copy(gate_cols[:], gate_t[:, 0, 0:BLOCKS])
 
-        gather_scales(g_s[0], dy_s, 0, C1)
+        gather_scales(g_s_first, dy_s, 0, FIRST)
         gather_words(g_w[0], 0, FIRST)
-        g_s.append(reuse.tile([P, C1], U8, name="g_s1", tag="gate", align_bytes=64))
-        gather_scales(g_s[1], dy_s, C1, C1)
         gather_words(g_w[1], FIRST, T - FIRST)
+        g_s_next = reuse.tile([P, C1 - FIRST], U8, name="g_s_next", tag="gate", align_bytes=64)
+        gather_scales(g_s_next, dy_s, FIRST, C1 - FIRST)
 
         def bank(n, name):
             return psum_z.tile([P, PACK, P], F32, name=name, tag="bank%d" % n)
@@ -117,15 +128,21 @@ def tile_moe_hib_relu_kernel(
 
         def first_product(b):
             e = b * P // C2
-            words = g_w[0][:, b * P : (b + 1) * P] if b * P < FIRST else g_w[1][:, b * P - FIRST : (b + 1) * P - FIRST]
-            scales = g_s[b // PACK][:, b % PACK * P : (b % PACK + 1) * P]
+            if b * P < FIRST:
+                words, scales = g_w[0][:, b * P : (b + 1) * P], g_s_first[:, b * P : (b + 1) * P]
+            else:
+                words = g_w[1][:, b * P - FIRST : (b + 1) * P - FIRST]
+                if b * P < C1:
+                    scales = g_s_next[:, b * P - FIRST : (b + 1) * P - FIRST]
+                else:
+                    scales = g_s_late[:, b * P - C1 : (b + 1) * P - C1]
             acc = bank(b % PACK, "sums")[:].rearrange("m a c -> m (a c)")
             nc.tensor.matmul_mx(
                 out=acc,
                 lhsT=words.bitcast(FP8X4),
                 lhsT_scale=scales,
                 rhs=wet_w[:, e, :].bitcast(FP4X4),
-                rhs_scale=wet_s[:, e, :],
+                rhs_scale=wet_s[e // 2][:, e % 2, :],
                 start=True,
                 stop=True,
             )
@@ -223,29 +240,31 @@ def tile_moe_hib_relu_kernel(
 
         sign = [reuse.tile([P, PACK, C1], BF16, name="sign", tag="sign0", align_bytes=64)]
         slope_first = {}
-        for t in (3, 2, 0, 1):
+        for t in (3, 2, 0):
             take_sign(0, t)
-            slope_first[t] = reuse.tile([P, C1], BF16, name="slope", tag="slope%d" % t, align_bytes=64)
+            slope_first[t] = keep.tile([P, C1], BF16, name="slope%d" % t, align_bytes=64)
             nc.gpsimd.tensor_scalar(slope_first[t][:], sign[0][:, t, :], 1.0, 0.0, ALU.min, ALU.max)
-            if t != 1:
-                mask_plane(0, t, slope_first[t][:])
+            mask_plane(0, t, slope_first[t][:])
+        take_sign(0, 1)
         turn_plane(1, rest)
+        sign.append(reuse.tile([P, PACK, C1], BF16, name="sign", tag="rest", align_bytes=64))
+        take_sign(1, 0)
+        slope_early = reuse.tile([P, C1], BF16, name="slope_early", tag="slope1", align_bytes=64)
+        nc.scalar.activation(slope_early[:], sign[1][:, 0, :], ACT.Relu)
+        mask_plane(1, 0, slope_early[:])
         stage(late, range(1, 4), "late123")
         turn_plane(1, late)
         scatter_z(wins[1], z[:, 1, FIRST:T], FIRST, T - FIRST)
         turn_plane(3, late)
-
-        sign.append(reuse.tile([P, PACK, C1], BF16, name="sign", tag="rest", align_bytes=64))
-        take_sign(1, 0)
-        slope_early = keep.tile([P, C1 + P], BF16, name="slope_early", align_bytes=64)
-        nc.scalar.activation(slope_early[:, 0:C1], sign[1][:, 0, :], ACT.Relu)
-        mask_plane(1, 0, slope_early[:, 0:C1])
         take_sign(1, 1)
-        nc.scalar.activation(slope_early[:, C1 : C1 + P], sign[1][:, 1, 0:P], ACT.Relu)
+        slope_short = keep.tile([P, P], BF16, name="slope_short", align_bytes=64)
+        nc.scalar.activation(slope_short[:], sign[1][:, 1, 0:P], ACT.Relu)
         take_sign(1, 3)
         take_sign(1, 2)
-        mask_plane(0, 1, slope_first[1][:])
-        mask_plane(1, 1, slope_early[:, C1 : C1 + P], 0, P)
+        slope_last = reuse.tile([P, C1], BF16, name="slope_last", tag="slope1", align_bytes=64)
+        nc.scalar.activation(slope_last[:], sign[0][:, 1, :], ACT.Relu)
+        mask_plane(0, 1, slope_last[:])
+        mask_plane(1, 1, slope_short[:], 0, P)
         scatter_z(wins[3], z[:, 3, C1:T], C1, C1)
 
         accs = second_product(0)

@@ -56,23 +56,29 @@ def tile_moe_hib_relu_kernel(
         g_s_spread = keep.tile([P, C1], U8, name="g_s_spread", align_bytes=64)
         g_s_late = keep.tile([P, C1], U8, name="g_s_late", align_bytes=64)
         wet_w = keep.tile([P, E, 2 * H], U8, name="wet_w", align_bytes=64)
-        wet_s = [keep.tile([P, E // G, H], U8, name="wet_s%d" % f, align_bytes=64) for f in range(G)]
+        wet_s = keep.tile([P, E, H], U8, name="wet_s", align_bytes=64)
+        lead_w = keep.tile([P, P, 2], U8, name="lead_w", align_bytes=64)
+        lead_s = reuse.tile([P, P], U8, name="lead_s", tag="pinned", align_bytes=64)
         wgt_w = keep.tile([P, G, K], I32, name="wgt_w", align_bytes=64)
         wgt_s = keep.tile([P, G, K], U8, name="wgt_s", align_bytes=64)
-        gate_rows = reuse.tile([P, P], F32, name="gate_rows", tag="gate", align_bytes=64)
+        gate_rows = keep.tile([P, P], F32, name="gate_rows", align_bytes=64)
+        gate_lead = keep.tile([P, FIRST], F32, name="gate_lead", align_bytes=64)
         gate_cols = keep.tile([P, BLOCKS], F32, name="gate_cols")
         ident = keep.tile([P, P], F32, name="ident")
         z = keep.tile([P, PACK, T], F32, name="z")
         a_sb = [keep.tile([P, PACK, C1], F32, name="a_sb%d" % f) for f in range(G)]
 
-        dy_s_words = dy_s[:].bitcast(I32)
-        nc.gpsimd.memset(dy_s_spread[:].bitcast(I32), 0)
-        nc.vector.memset(dy_s_words[:, 0 : 2 * P - 1], 0)
-        nc.vector.memset(dy_s_words[:, 2 * P - 1 : 2 * P], 0)
+        def zero_on_vector(words):
+            last = words.shape[1] - 1
+            nc.vector.memset(words[:, 0:last], 0)
+            nc.vector.memset(words[:, last : last + 1], 0)
+
+        for window in (dy_s_spread, dy_s):
+            nc.gpsimd.memset(window[:].bitcast(I32)[:, 0:P], 0)
+            zero_on_vector(window[:].bitcast(I32)[:, P : 2 * P])
+        zero_on_vector(words_of(wet_s))
         nc.gpsimd.memset(gate_rows[:], 0.0)
-        nc.gpsimd.memset(words_of(wet_s[0]), 0)
         make_identity(nc, ident[:])
-        nc.gpsimd.memset(words_of(wet_s[1]), 0)
         nc.gpsimd.memset(g_s_late[:].bitcast(I32), 0)
         nc.gpsimd.memset(words_of(wgt_s), 0)
 
@@ -95,31 +101,25 @@ def tile_moe_hib_relu_kernel(
             queue = nc.sync if q < 3 else nc.scalar
             queue.dma_start(dy_s[32 * q : 32 * q + 4, :].bitcast(I32), dy_scales[0, 4 * q : 4 * q + 4, :].bitcast(I32))
         nc.sync.dma_start(dy_w[:], dy_words[0].rearrange("p n d -> p (n d)").bitcast(I32))
-        nc.sync.dma_start(gate_rows[0:BLOCKS, :], gate[0].rearrange("(b c) -> b c", c=P))
         nc.sync.dma_start(wet_w[:, 0:1, :].bitcast(I32), wet_src[:, 0:1, :])
-        load_scale_rows(wet_s[0], wet_s_src[:, 0:2, :])
+        load_scale_rows(wet_s, wet_s_src)
+        nc.sync.dma_start(gate_rows[0:BLOCKS, :], gate[0].rearrange("(b c) -> b c", c=P))
         nc.sync.dma_start(offs2_sb[:], offs2)
+        nc.sync.dma_start(gate_lead[:], gate[:, 0:FIRST])
         nc.sync.dma_start(wet_w[:, 1:E, :].bitcast(I32), wet_src[:, 1:E, :])
-        load_scale_rows(wet_s[1], wet_s_src[:, 2:4, :])
         gather_scales(g_s_spread, dy_s_spread, C1, C1)
         for q in range(4):
             rows = g_s_spread[32 * q : 32 * q + 32 : 8, :].bitcast(I32)
             nc.sync.dma_start(g_s_late[32 * q : 32 * q + 4, :].bitcast(I32), rows)
-        for f in range(G):
-            nc.sync.dma_start(a_sb[f][:], a_src[:, :, f * C1 : (f + 1) * C1])
+        for f, planes in ((0, slice(2, 4)), (0, slice(0, 2)), (1, slice(0, 2)), (1, slice(2, 4))):
+            nc.sync.dma_start(a_sb[f][:, planes, :], a_src[:, planes, f * C1 : (f + 1) * C1])
         nc.sync.dma_start(wgt_w[:], wgt_words.rearrange("f s p k d -> p (f s) (k d)").bitcast(I32))
         load_scale_rows(wgt_s, wgt_scales.rearrange("f s r k -> r (f s) k").bitcast(I32))
         nc.sync.dma_start(offs_sb[:], offs)
 
-        gate_t = psum_t.tile([P, PACK, P], F32, name="turned")
-        nc.tensor.transpose(gate_t[:, 0, :], gate_rows[:], ident[:])
-        nc.scalar.copy(gate_cols[:], gate_t[:, 0, 0:BLOCKS])
-
         gather_scales(g_s_first, dy_s, 0, FIRST)
         gather_words(g_w[0], 0, FIRST)
         gather_words(g_w[1], FIRST, T - FIRST)
-        g_s_next = reuse.tile([P, C1 - FIRST], U8, name="g_s_next", tag="gate", align_bytes=64)
-        gather_scales(g_s_next, dy_s, FIRST, C1 - FIRST)
 
         def bank(n, name):
             return psum_z.tile([P, PACK, P], F32, name=name, tag="bank%d" % n)
@@ -142,7 +142,7 @@ def tile_moe_hib_relu_kernel(
                 lhsT=words.bitcast(FP8X4),
                 lhsT_scale=scales,
                 rhs=wet_w[:, e, :].bitcast(FP4X4),
-                rhs_scale=wet_s[e // 2][:, e % 2, :],
+                rhs_scale=wet_s[:, e, :],
                 start=True,
                 stop=True,
             )
@@ -153,9 +153,8 @@ def tile_moe_hib_relu_kernel(
         def stage(blocks, planes, tag):
             tile = reuse.tile([P, len(blocks), len(planes), P], F32, name="staged", tag=tag, align_bytes=64)
             for n, b in enumerate(blocks):
-                nc.scalar.activation(
-                    tile[:, n, :, :], sums[b][:, planes.start : planes.stop, :], ACT.Copy, scale=gate_cols[:, b : b + 1]
-                )
+                source = sums[b][:, planes.start : planes.stop, :]
+                nc.scalar.activation(tile[:, n, :, :], source, ACT.Copy, scale=gate_cols[:, b : b + 1])
                 for t in planes:
                     staged[b, t] = tile[:, n, t - planes.start, :]
 
@@ -175,6 +174,11 @@ def tile_moe_hib_relu_kernel(
 
         def scatter_z(win, source, first, count):
             nc.vector.tensor_copy(win[:].indirect(entries(offs2_sb, first, count)), source)
+
+        def scatter_lead(t, count):
+            nc.vector.tensor_tensor(
+                wins[t][:].indirect(entries(offs2_sb, 0, count)), z[:, t, 0:count], gate_lead[:, 0:count], ALU.mult
+            )
 
         def mask_plane(f, t, slope, first=0, last=C1):
             nc.gpsimd.tensor_tensor(da[f][:, first:last, t], wins[t][:, f * C1 + first : f * C1 + last], slope, ALU.mult)
@@ -211,26 +215,43 @@ def tile_moe_hib_relu_kernel(
         wins = [reuse.tile([P, T], F32, name="win", tag="win%d" % t, align_bytes=64) for t in range(PACK)]
         da = [reuse.tile([P, C1, PACK], BF16, name="da", tag="da%d" % f, align_bytes=64) for f in range(G)]
 
+        nc.gpsimd.tensor_copy(lead_w[:], wet_w[:, 0, :].rearrange("p (m t b) -> p m t b", t=PACK, b=2)[:, :, 3, :])
+        nc.gpsimd.tensor_copy(lead_s[:], wet_s[:, 0, :].rearrange("p (m t) -> p m t", t=PACK)[:, :, 3])
+        lead_sums = bank(1, "lead_sums")[:].rearrange("m a c -> m (a c)")[:, 0:FIRST]
+        nc.tensor.matmul_mx(
+            out=lead_sums,
+            lhsT=lead_w[:].rearrange("p m b -> p (m b)").bitcast(FP4X4),
+            lhsT_scale=lead_s[:],
+            rhs=g_w[0][:].bitcast(FP8X4),
+            rhs_scale=g_s_first[:],
+            start=True,
+            stop=True,
+        )
+        nc.scalar.copy(z[:, 3, 0:FIRST], lead_sums)
+        scatter_lead(3, FIRST)
+
+        gate_t = psum_t.tile([P, PACK, P], F32, name="turned")
+        nc.tensor.transpose(gate_t[:, 0, :], gate_rows[:], ident[:])
+        nc.scalar.copy(gate_cols[:], gate_t[:, 0, 0:BLOCKS])
         first_product(0)
         first_product(1)
-        stage(lead, range(3, 4), "lead3")
-        turn_plane(3, lead, bank(2, "turned_lead"))
-        scatter_z(wins[3], z[:, 3, 0:P], 0, P)
+        g_s_next = reuse.tile([P, C1 - FIRST], U8, name="g_s_next", tag="pinned", align_bytes=64)
+        gather_scales(g_s_next, dy_s, FIRST, C1 - FIRST)
         stage(lead, range(2, 3), "lead2")
-        turn_plane(2, lead, bank(3, "turned_lead"))
+        turn_plane(2, lead, bank(2, "turned_lead"))
         scatter_z(wins[2], z[:, 2, 0:P], 0, P)
         for t in (0, 1):
             stage(pair, range(t, t + 1), "pair%d" % t)
-            turn_plane(t, pair)
+            turn_plane(t, pair, bank(3, "turned_lead") if t == 0 else None)
             scatter_z(wins[t], z[:, t, 0:FIRST], 0, FIRST)
+        stage(range(1, 2), range(2, 3), "second")
 
         first_product(2)
         first_product(3)
-        stage(range(1, 2), range(2, 4), "second")
         stage(rest, range(0, 4), "rest")
-        for t in (3, 2):
-            turn_plane(t, range(1, 4), bank(3 - t, "turned_rest"))
-            scatter_z(wins[t], z[:, t, P:C1], P, C1 - P)
+        for t, blocks in ((3, rest), (2, range(1, 4))):
+            turn_plane(t, blocks, bank(3 - t, "turned_rest"))
+            scatter_z(wins[t], z[:, t, blocks.start * P : C1], blocks.start * P, C1 - blocks.start * P)
         turn_plane(0, rest)
         for b in late:
             first_product(b)
@@ -289,5 +310,4 @@ def tile_moe_hib_relu_kernel(
         scatter_dx(out_low, 1, dx_second[0])
         nc.sync.dma_start(out[0:P, :], out_low[:])
         scatter_dx(out_high, 1, dx_second[1])
-        nc.sync.dma_start(out[P : 2 * P, 0 : T // 2], out_high[:, 0 : T // 2])
-        nc.scalar.dma_start(out[P : 2 * P, T // 2 : T], out_high[:, T // 2 : T])
+        nc.sync.dma_start(out[P : 2 * P, :], out_high[:])

@@ -1,7 +1,6 @@
 from contextlib import ExitStack
 
 import concourse.mybir as mybir
-from concourse.masks import make_identity
 
 K, T, G, C1, E, C2, H, N = 256, 1024, 2, 512, 4, 256, 512, 512
 FLOPS = 2 * T * N * H + 2 * T * H * K
@@ -20,8 +19,9 @@ ALU = mybir.AluOpType
 P = 128
 PACK = 4
 PER_COL = 16
-BLOCKS = T // P
-FIRST = 2 * P
+BANKS = 8
+TINY = 2.0**-126
+HALF_UP = 2.0**63
 
 
 def entries(list_tile, first, count):
@@ -39,149 +39,139 @@ def tile_moe_hib_relu_kernel(
     with ExitStack() as ctx:
         keep = ctx.enter_context(tc.tile_pool(name="keep", bufs=1))
         reuse = ctx.enter_context(tc.tile_pool(name="reuse", bufs=1))
-        psum_z = ctx.enter_context(tc.psum_pool(name="psum_z", bufs=1))
-        psum_t = ctx.enter_context(tc.psum_pool(name="psum_t", bufs=4))
+        psum = ctx.enter_context(tc.psum_pool(name="psum", bufs=1))
 
         dst_sb = keep.tile([P, T // PER_COL], U16, name="dst_sb")
         offs2_sb = keep.tile([P, T // PER_COL], U16, name="offs2_sb")
         offs_sb = keep.tile([P, T // PER_COL], U16, name="offs_sb")
         dy_w = keep.tile([P, T], I32, name="dy_w", align_bytes=64)
         dy_s = keep.tile([P, T], U8, name="dy_s", align_bytes=64)
-        dy_s_spread = keep.tile([P, T], U8, name="dy_s_spread", align_bytes=64)
-        g_w = [
-            keep.tile([P, FIRST], U32, name="g_w0", align_bytes=64),
-            keep.tile([P, T - FIRST], U32, name="g_w1", align_bytes=64),
-        ]
-        g_s_first = keep.tile([P, FIRST], U8, name="g_s_first", align_bytes=64)
-        g_s_spread = keep.tile([P, C1], U8, name="g_s_spread", align_bytes=64)
-        g_s_late = keep.tile([P, C1], U8, name="g_s_late", align_bytes=64)
-        wet_w = keep.tile([P, E, 2 * H], U8, name="wet_w", align_bytes=64)
+        wet_w = [keep.tile([P, E // G, 2 * H], U8, name="wet_w%d" % f, align_bytes=64) for f in range(G)]
         wet_s = keep.tile([P, E, H], U8, name="wet_s", align_bytes=64)
-        lead_w = keep.tile([P, P, 2], U8, name="lead_w", align_bytes=64)
-        lead_s = reuse.tile([P, P], U8, name="lead_s", tag="pinned", align_bytes=64)
         wgt_w = keep.tile([P, G, K], I32, name="wgt_w", align_bytes=64)
         wgt_s = keep.tile([P, G, K], U8, name="wgt_s", align_bytes=64)
-        gate_rows = keep.tile([P, P], F32, name="gate_rows", align_bytes=64)
-        gate_lead = keep.tile([P, FIRST], F32, name="gate_lead", align_bytes=64)
-        gate_cols = keep.tile([P, BLOCKS], F32, name="gate_cols")
-        ident = keep.tile([P, P], F32, name="ident")
-        z = keep.tile([P, PACK, T], F32, name="z")
-        a_sb = [keep.tile([P, PACK, C1], F32, name="a_sb%d" % f) for f in range(G)]
+        gate_first = reuse.tile([P, C2], F32, name="gate_first", tag="gate_first", align_bytes=64)
+        gate_rest = keep.tile([P, T - C2], F32, name="gate_rest", align_bytes=64)
+        a_sb = {}
+        for f in range(G):
+            for u in range(2):
+                a_sb[f, u] = reuse.tile([P, 2, C1], F32, name="a_sb", tag="a%d%d" % (f, u), align_bytes=64)
 
         def zero_on_vector(words):
             last = words.shape[1] - 1
             nc.vector.memset(words[:, 0:last], 0)
             nc.vector.memset(words[:, last : last + 1], 0)
 
-        for window in (dy_s_spread, dy_s):
-            nc.gpsimd.memset(window[:].bitcast(I32)[:, 0:P], 0)
-            zero_on_vector(window[:].bitcast(I32)[:, P : 2 * P])
+        nc.gpsimd.memset(dy_s[:].bitcast(I32)[:, 0:P], 0)
+        zero_on_vector(dy_s[:].bitcast(I32)[:, P : 2 * P])
         zero_on_vector(words_of(wet_s))
-        nc.gpsimd.memset(gate_rows[:], 0.0)
-        make_identity(nc, ident[:])
-        nc.gpsimd.memset(g_s_late[:].bitcast(I32), 0)
         nc.gpsimd.memset(words_of(wgt_s), 0)
 
         def load_scale_rows(plane, rows):
             for q in range(4):
                 nc.sync.dma_start(plane[32 * q : 32 * q + 4, :, :].bitcast(I32), rows[4 * q : 4 * q + 4, :, :])
 
-        def gather_scales(tile, window, first, count):
-            nc.vector.tensor_copy(tile[:], window[:].indirect(entries(dst_sb, first, count)))
-
-        def gather_words(tile, first, count):
-            nc.vector.tensor_copy(tile[:], dy_w[:].bitcast(U32).indirect(entries(dst_sb, first, count)))
-
-        wet_src = wet_words.rearrange("e s p c -> p (e s) c").bitcast(I32)
-        wet_s_src = wet_scales.rearrange("e s r h -> r (e s) h").bitcast(I32)
         a_src = a.rearrange("(p t) j -> p t j", t=PACK)
         nc.sync.dma_start(dst_sb[:], dst)
-        nc.sync.dma_start(dy_s_spread[0:P:8, :].bitcast(I32), dy_scales[0].bitcast(I32))
         for q in range(4):
             queue = nc.sync if q < 3 else nc.scalar
             queue.dma_start(dy_s[32 * q : 32 * q + 4, :].bitcast(I32), dy_scales[0, 4 * q : 4 * q + 4, :].bitcast(I32))
+        wet_src = wet_words.rearrange("e s p c -> p (e s) c").bitcast(I32)
         nc.sync.dma_start(dy_w[:], dy_words[0].rearrange("p n d -> p (n d)").bitcast(I32))
-        nc.sync.dma_start(wet_w[:, 0:1, :].bitcast(I32), wet_src[:, 0:1, :])
-        load_scale_rows(wet_s, wet_s_src)
-        nc.sync.dma_start(gate_rows[0:BLOCKS, :], gate[0].rearrange("(b c) -> b c", c=P))
+        nc.sync.dma_start(wet_w[0][:].bitcast(I32), wet_src[:, 0:2, :])
         nc.sync.dma_start(offs2_sb[:], offs2)
-        nc.sync.dma_start(gate_lead[:], gate[:, 0:FIRST])
-        nc.sync.dma_start(wet_w[:, 1:E, :].bitcast(I32), wet_src[:, 1:E, :])
-        gather_scales(g_s_spread, dy_s_spread, C1, C1)
-        for q in range(4):
-            rows = g_s_spread[32 * q : 32 * q + 32 : 8, :].bitcast(I32)
-            nc.sync.dma_start(g_s_late[32 * q : 32 * q + 4, :].bitcast(I32), rows)
-        for f, planes in ((0, slice(2, 4)), (0, slice(0, 2)), (1, slice(0, 2)), (1, slice(2, 4))):
-            nc.sync.dma_start(a_sb[f][:, planes, :], a_src[:, planes, f * C1 : (f + 1) * C1])
+        load_scale_rows(wet_s, wet_scales.rearrange("e s r h -> r (e s) h").bitcast(I32))
+        nc.sync.dma_start(gate_first[:], gate[:, 0:C2])
+        nc.sync.dma_start(wet_w[1][:].bitcast(I32), wet_src[:, 2:4, :])
+        nc.sync.dma_start(gate_rest[:], gate[:, C2:T])
+        for f in range(G):
+            for u in range(2):
+                nc.sync.dma_start(a_sb[f, u][:], a_src[:, 2 * u : 2 * u + 2, f * C1 : (f + 1) * C1])
         nc.sync.dma_start(wgt_w[:], wgt_words.rearrange("f s p k d -> p (f s) (k d)").bitcast(I32))
         load_scale_rows(wgt_s, wgt_scales.rearrange("f s r k -> r (f s) k").bitcast(I32))
         nc.sync.dma_start(offs_sb[:], offs)
 
-        gather_scales(g_s_first, dy_s, 0, FIRST)
-        gather_words(g_w[0], 0, FIRST)
-        gather_words(g_w[1], FIRST, T - FIRST)
+        def gather_scales(f, tag):
+            tile = reuse.tile([P, C1], U8, name="g_s", tag=tag, align_bytes=64)
+            nc.vector.tensor_copy(tile[:], dy_s[:].indirect(entries(dst_sb, f * C1, C1)))
+            return tile
 
-        def bank(n, name):
-            return psum_z.tile([P, PACK, P], F32, name=name, tag="bank%d" % n)
+        def gather_words(first, count, tag):
+            tile = reuse.tile([P, count], U32, name="g_w", tag=tag, align_bytes=64)
+            nc.vector.tensor_copy(tile[:], dy_w[:].bitcast(U32).indirect(entries(dst_sb, first, count)))
+            return tile
 
-        sums = {}
+        plane_w, plane_s = {}, {}
 
-        def first_product(b):
-            e = b * P // C2
-            if b * P < FIRST:
-                words, scales = g_w[0][:, b * P : (b + 1) * P], g_s_first[:, b * P : (b + 1) * P]
-            else:
-                words = g_w[1][:, b * P - FIRST : (b + 1) * P - FIRST]
-                if b * P < C1:
-                    scales = g_s_next[:, b * P - FIRST : (b + 1) * P - FIRST]
-                else:
-                    scales = g_s_late[:, b * P - C1 : (b + 1) * P - C1]
-            acc = bank(b % PACK, "sums")[:].rearrange("m a c -> m (a c)")
-            nc.tensor.matmul_mx(
-                out=acc,
-                lhsT=words.bitcast(FP8X4),
-                lhsT_scale=scales,
-                rhs=wet_w[:, e, :].bitcast(FP4X4),
-                rhs_scale=wet_s[:, e, :],
-                start=True,
-                stop=True,
-            )
-            sums[b] = acc.rearrange("m (p t) -> m t p", t=PACK)
+        def order_words(e, planes, tag):
+            tile = reuse.tile([P, len(planes), 2 * P], U8, name="plane_w", tag=tag, align_bytes=64)
+            source = wet_w[0][:, e, :].bitcast(U16).rearrange("p (m t) -> p t m", t=PACK)
+            nc.scalar.copy(tile[:].bitcast(U16), source[:, planes.start : planes.stop, :])
+            for n, t in enumerate(planes):
+                plane_w[e, t] = tile[:, n, :]
 
-        staged = {}
+        def order_late_words(tag):
+            tile = reuse.tile([P, E // G, PACK, 2 * P], U8, name="late_w", tag=tag, align_bytes=64)
+            source = wet_w[1][:].bitcast(U16).rearrange("p e (m t) -> p e t m", t=PACK)
+            nc.vector.tensor_copy(tile[:].bitcast(U16), source)
+            for m in range(E // G):
+                for t in range(PACK):
+                    plane_w[E // G + m, t] = tile[:, m, t, :]
 
-        def stage(blocks, planes, tag):
-            tile = reuse.tile([P, len(blocks), len(planes), P], F32, name="staged", tag=tag, align_bytes=64)
-            for n, b in enumerate(blocks):
-                source = sums[b][:, planes.start : planes.stop, :]
-                nc.scalar.activation(tile[:, n, :, :], source, ACT.Copy, scale=gate_cols[:, b : b + 1])
-                for t in planes:
-                    staged[b, t] = tile[:, n, t - planes.start, :]
+        def order_scales(experts, planes, tag):
+            tile = reuse.tile([P, len(experts), len(planes), P], U8, name="plane_s", tag=tag, align_bytes=64)
+            source = wet_s[:].rearrange("p e (m t) -> p e t m", t=PACK)
+            nc.vector.tensor_copy(tile[:], source[:, experts.start : experts.stop, planes.start : planes.stop, :])
+            for m, e in enumerate(experts):
+                for n, t in enumerate(planes):
+                    plane_s[e, t] = tile[:, m, n, :]
 
-        def turn(pieces, into, turned=None):
-            if turned is None:
-                turned = psum_t.tile([P, PACK, P], F32, name="turned")
-            for n, piece in enumerate(pieces):
-                nc.tensor.transpose(turned[:, n, :], staged[piece], ident[:])
-            nc.scalar.copy(into, turned[:, 0 : len(pieces), :])
+        banks_taken = []
 
-        def turn_plane(t, blocks, turned=None):
-            into = z[:, t, blocks.start * P : blocks.stop * P].rearrange("p (b m) -> p b m", m=P)
-            turn([(b, t) for b in blocks], into, turned)
+        def next_bank(shape):
+            tile = psum.tile(shape, F32, name="bank", tag="bank%d" % (len(banks_taken) % BANKS))
+            banks_taken.append(tile)
+            return tile
 
-        def take_sign(f, t):
-            nc.scalar.activation(sign[f][:, t, :], a_sb[f][:, t, :], ACT.Sign)
+        z = [keep.tile([P, PACK, C1], F32, name="z%d" % f, align_bytes=64) for f in range(G)]
 
-        def scatter_z(win, source, first, count):
-            nc.vector.tensor_copy(win[:].indirect(entries(offs2_sb, first, count)), source)
+        def first_product(e, planes, words, scales):
+            f, place = divmod(e, E // G)
+            acc = next_bank([P, len(planes), C2])
+            for n, t in enumerate(planes):
+                nc.tensor.matmul_mx(
+                    out=acc[:, n, :],
+                    lhsT=plane_w[e, t].bitcast(FP4X4),
+                    lhsT_scale=plane_s[e, t],
+                    rhs=words.bitcast(FP8X4),
+                    rhs_scale=scales,
+                    start=True,
+                    stop=True,
+                )
+            weights = gate_first[:] if e == 0 else gate_rest[:, (e - 1) * C2 : e * C2]
+            weights = weights.unsqueeze(1).to_broadcast([P, len(planes), C2])
+            into = z[f][:, planes.start : planes.stop, place * C2 : (place + 1) * C2]
+            nc.vector.tensor_tensor(into, acc[:], weights, ALU.mult)
 
-        def scatter_lead(t, count):
-            nc.vector.tensor_tensor(
-                wins[t][:].indirect(entries(offs2_sb, 0, count)), z[:, t, 0:count], gate_lead[:, 0:count], ALU.mult
-            )
+        def scatter_on_scalar(window, list_tile, first, source):
+            nc.scalar.activation(window[:].indirect(entries(list_tile, first, C2)), source, ACT.Copy)
 
-        def mask_plane(f, t, slope, first=0, last=C1):
-            nc.gpsimd.tensor_tensor(da[f][:, first:last, t], wins[t][:, f * C1 + first : f * C1 + last], slope, ALU.mult)
+        def scatter_on_vector(window, list_tile, first, count, source):
+            nc.vector.tensor_copy(window[:].indirect(entries(list_tile, first, count)), source)
+
+        def z_on_scalar(e, t):
+            f, place = divmod(e, E // G)
+            scatter_on_scalar(win[f, t], offs2_sb, e * C2, z[f][:, t, place * C2 : (place + 1) * C2])
+
+        def mask_plane(f, t, slope):
+            nc.gpsimd.tensor_tensor(da[f][:, :, t], win[f, t][:, f * C1 : (f + 1) * C1], slope, ALU.mult)
+
+        def slope_on_gpsimd(t):
+            spread = keep.tile([P, C1], F32, name="spread%d" % t, align_bytes=64)
+            slope = keep.tile([P, C1], BF16, name="slope%d" % t, align_bytes=64)
+            nc.gpsimd.tensor_scalar(spread[:], a_sb[0, t // 2][:, t % 2, :], TINY, 0.0, ALU.min, ALU.max)
+            nc.gpsimd.tensor_scalar(slope[:], spread[:], HALF_UP, HALF_UP, ALU.mult, ALU.mult)
+            return slope
 
         def second_product(f):
             da_w = keep.tile([P, C1], U32, name="da_w%d" % f, align_bytes=64)
@@ -190,9 +180,9 @@ def tile_moe_hib_relu_kernel(
             accs = []
             for kb in range(K // P):
                 k_cols = slice(kb * P, (kb + 1) * P)
-                acc = bank(G * f + kb, "acc")[:].rearrange("k a c -> k (a c)")
+                acc = next_bank([P, C1])
                 nc.tensor.matmul_mx(
-                    out=acc,
+                    out=acc[:],
                     lhsT=wgt_w[:, f, k_cols].bitcast(FP8X4),
                     lhsT_scale=wgt_s[:, f, k_cols],
                     rhs=da_w[:].bitcast(FP8X4),
@@ -203,111 +193,67 @@ def tile_moe_hib_relu_kernel(
                 accs.append(acc)
             return accs
 
-        def leave_psum(acc, name):
-            dx_sb = keep.tile([P, C1], F32, name=name)
-            nc.scalar.copy(dx_sb[:], acc)
-            return dx_sb
+        order_words(0, range(0, 1), "lead_w")
+        order_words(0, range(1, 4), "first_w")
+        order_words(1, range(0, 4), "plane_w1")
+        g_s = [gather_scales(0, "g_s0")]
+        g_w0 = gather_words(0, C2, "g_w0")
+        order_scales(range(0, 1), range(0, 1), "lead_s")
+        order_scales(range(0, 1), range(1, 4), "first_s")
+        for planes in (range(0, 1), range(1, 2), range(2, 4)):
+            first_product(0, planes, g_w0[:], g_s[0][:, 0:C2])
+        g_w1 = gather_words(C2, C2, "g_w1")
+        order_scales(range(1, E), range(0, 4), "gate_first")
+        for planes in (range(0, 2), range(2, 4)):
+            first_product(1, planes, g_w1[:], g_s[0][:, C2:C1])
+        order_late_words("first_w")
+        g_s.append(gather_scales(1, "first_s"))
+        g_w_late = {2: gather_words(2 * C2, C2, "g_w0"), 3: gather_words(3 * C2, C2, "g_w1")}
+        for e in (2, 3):
+            columns = slice((e - 2) * C2, (e - 1) * C2)
+            for planes in (range(0, 2), range(2, 4)):
+                first_product(e, planes, g_w_late[e][:], g_s[1][:, columns])
 
-        def scatter_dx(out_tile, f, dx_sb):
-            nc.vector.tensor_copy(out_tile[:].indirect(entries(offs_sb, f * C1, C1)), dx_sb[:])
-
-        lead, pair, rest, late = range(0, 1), range(0, 2), range(2, 4), range(4, 8)
-        wins = [reuse.tile([P, T], F32, name="win", tag="win%d" % t, align_bytes=64) for t in range(PACK)]
         da = [reuse.tile([P, C1, PACK], BF16, name="da", tag="da%d" % f, align_bytes=64) for f in range(G)]
+        win = {}
+        for f, t in ((0, 0), (0, 1), (0, 2), (0, 3), (1, 0), (1, 3)):
+            win[f, t] = keep.tile([P, T], F32, name="win%d%d" % (f, t), align_bytes=64)
 
-        nc.gpsimd.tensor_copy(lead_w[:], wet_w[:, 0, :].rearrange("p (m t b) -> p m t b", t=PACK, b=2)[:, :, 3, :])
-        nc.gpsimd.tensor_copy(lead_s[:], wet_s[:, 0, :].rearrange("p (m t) -> p m t", t=PACK)[:, :, 3])
-        lead_sums = bank(1, "lead_sums")[:].rearrange("m a c -> m (a c)")[:, 0:FIRST]
-        nc.tensor.matmul_mx(
-            out=lead_sums,
-            lhsT=lead_w[:].rearrange("p m b -> p (m b)").bitcast(FP4X4),
-            lhsT_scale=lead_s[:],
-            rhs=g_w[0][:].bitcast(FP8X4),
-            rhs_scale=g_s_first[:],
-            start=True,
-            stop=True,
-        )
-        nc.scalar.copy(z[:, 3, 0:FIRST], lead_sums)
-        scatter_lead(3, FIRST)
+        for e, t in ((0, 0), (0, 1), (0, 2), (0, 3), (1, 0), (1, 1), (1, 2), (1, 3)):
+            z_on_scalar(e, t)
+        slopes = [slope_on_gpsimd(t) for t in range(PACK)]
+        for t in range(PACK):
+            mask_plane(0, t, slopes[t][:])
 
-        gate_t = psum_t.tile([P, PACK, P], F32, name="turned")
-        nc.tensor.transpose(gate_t[:, 0, :], gate_rows[:], ident[:])
-        nc.scalar.copy(gate_cols[:], gate_t[:, 0, 0:BLOCKS])
-        first_product(0)
-        first_product(1)
-        g_s_next = reuse.tile([P, C1 - FIRST], U8, name="g_s_next", tag="pinned", align_bytes=64)
-        gather_scales(g_s_next, dy_s, FIRST, C1 - FIRST)
-        stage(lead, range(2, 3), "lead2")
-        turn_plane(2, lead, bank(2, "turned_lead"))
-        scatter_z(wins[2], z[:, 2, 0:P], 0, P)
-        for t in (0, 1):
-            stage(pair, range(t, t + 1), "pair%d" % t)
-            turn_plane(t, pair, bank(3, "turned_lead") if t == 0 else None)
-            scatter_z(wins[t], z[:, t, 0:FIRST], 0, FIRST)
-        stage(range(1, 2), range(2, 3), "second")
-
-        first_product(2)
-        first_product(3)
-        stage(rest, range(0, 4), "rest")
-        for t, blocks in ((3, rest), (2, range(1, 4))):
-            turn_plane(t, blocks, bank(3 - t, "turned_rest"))
-            scatter_z(wins[t], z[:, t, blocks.start * P : C1], blocks.start * P, C1 - blocks.start * P)
-        turn_plane(0, rest)
-        for b in late:
-            first_product(b)
-        stage(late, range(0, 1), "sign0")
-        turn_plane(0, late)
-        scatter_z(wins[0], z[:, 0, FIRST:T], FIRST, T - FIRST)
-
-        sign = [reuse.tile([P, PACK, C1], BF16, name="sign", tag="sign0", align_bytes=64)]
-        slope_first = {}
-        for t in (3, 2, 0):
-            take_sign(0, t)
-            slope_first[t] = keep.tile([P, C1], BF16, name="slope%d" % t, align_bytes=64)
-            nc.gpsimd.tensor_scalar(slope_first[t][:], sign[0][:, t, :], 1.0, 0.0, ALU.min, ALU.max)
-            mask_plane(0, t, slope_first[t][:])
-        take_sign(0, 1)
-        turn_plane(1, rest)
-        sign.append(reuse.tile([P, PACK, C1], BF16, name="sign", tag="rest", align_bytes=64))
-        take_sign(1, 0)
-        slope_early = reuse.tile([P, C1], BF16, name="slope_early", tag="slope1", align_bytes=64)
-        nc.scalar.activation(slope_early[:], sign[1][:, 0, :], ACT.Relu)
-        mask_plane(1, 0, slope_early[:])
-        stage(late, range(1, 4), "late123")
-        turn_plane(1, late)
-        scatter_z(wins[1], z[:, 1, FIRST:T], FIRST, T - FIRST)
-        turn_plane(3, late)
-        take_sign(1, 1)
-        slope_short = keep.tile([P, P], BF16, name="slope_short", align_bytes=64)
-        nc.scalar.activation(slope_short[:], sign[1][:, 1, 0:P], ACT.Relu)
-        take_sign(1, 3)
-        take_sign(1, 2)
-        slope_last = reuse.tile([P, C1], BF16, name="slope_last", tag="slope1", align_bytes=64)
-        nc.scalar.activation(slope_last[:], sign[0][:, 1, :], ACT.Relu)
-        mask_plane(0, 1, slope_last[:])
-        mask_plane(1, 1, slope_short[:], 0, P)
-        scatter_z(wins[3], z[:, 3, C1:T], C1, C1)
-
+        scatter_on_vector(win[1, 0], offs2_sb, C1, C1, z[1][:, 0, :])
+        slope_late = keep.tile([P, PACK, C1], BF16, name="slope_late", align_bytes=64)
+        for u in range(2):
+            nc.vector.tensor_scalar(slope_late[:, 2 * u : 2 * u + 2, :], a_sb[1, u][:], 0.0, None, ALU.is_gt)
+        win[1, 2] = reuse.tile([P, T], F32, name="win", tag="a11", align_bytes=64)
+        scatter_on_vector(win[1, 2], offs2_sb, C1, C2, z[1][:, 2, 0:C2])
+        z_on_scalar(2, 3)
+        z_on_scalar(3, 3)
+        z_on_scalar(3, 2)
         accs = second_product(0)
-        z_last = reuse.tile([P, PACK, P], F32, name="z_last", tag="slope1", align_bytes=64)
-        turn([(b, 2) for b in late], z_last[:])
-        scatter_z(wins[2], z_last[:].rearrange("p b m -> p (b m)"), C1, C1)
-        held = reuse.tile([P, 3, C1], BF16, name="held", tag="da0", align_bytes=64)
-        nc.scalar.activation(held[:, 0, P:C1], sign[1][:, 1, P:C1], ACT.Relu)
-        mask_plane(1, 1, held[:, 0, P:C1], P, C1)
-        nc.scalar.activation(held[:, 1, :], sign[1][:, 3, :], ACT.Relu)
-        mask_plane(1, 3, held[:, 1, :])
-        dx_first = [leave_psum(accs[0], "dx00")]
-        nc.scalar.activation(held[:, 2, :], sign[1][:, 2, :], ACT.Relu)
-        mask_plane(1, 2, held[:, 2, :])
-        dx_first.append(leave_psum(accs[1], "dx01"))
+        win[1, 1] = reuse.tile([P, T], F32, name="win", tag="da0", align_bytes=64)
+        scatter_on_vector(win[1, 1], offs2_sb, C1, C1, z[1][:, 1, :])
+        for t in (0, 3, 2, 1):
+            mask_plane(1, t, slope_late[:, t, :])
 
-        out_low = keep.tile([P, T], F32, name="out_low", align_bytes=64)
-        scatter_dx(out_low, 0, dx_first[0])
-        dx_second = [leave_psum(acc, "dx1%d" % kb) for kb, acc in enumerate(second_product(1))]
-        out_high = reuse.tile([P, T], F32, name="out_high", tag="win2", align_bytes=64)
-        scatter_dx(out_high, 0, dx_first[1])
-        scatter_dx(out_low, 1, dx_second[0])
-        nc.sync.dma_start(out[0:P, :], out_low[:])
-        scatter_dx(out_high, 1, dx_second[1])
-        nc.sync.dma_start(out[P : 2 * P, :], out_high[:])
+        out_sb = [keep.tile([P, T], F32, name="out%d" % kb, align_bytes=64) for kb in range(K // P)]
+        dx = [keep.tile([P, C1], F32, name="dx0%d" % kb, align_bytes=64) for kb in range(K // P)]
+        nc.scalar.copy(dx[1][:], accs[1][:])
+        nc.scalar.copy(dx[0][:], accs[0][:])
+        for place in range(2):
+            scatter_on_scalar(out_sb[1], offs_sb, place * C2, dx[1][:, place * C2 : (place + 1) * C2])
+        scatter_on_vector(out_sb[0], offs_sb, 0, C1, dx[0][:])
+
+        accs = second_product(1)
+        dx = [keep.tile([P, C1], F32, name="dx1%d" % kb, align_bytes=64) for kb in range(K // P)]
+        nc.vector.tensor_copy(dx[0][:], accs[0][:])
+        nc.scalar.copy(dx[1][:], accs[1][:])
+        scatter_on_vector(out_sb[0], offs_sb, C1, C1, dx[0][:])
+        for place in range(2):
+            scatter_on_scalar(out_sb[1], offs_sb, C1 + place * C2, dx[1][:, place * C2 : (place + 1) * C2])
+        for kb in range(K // P):
+            nc.sync.dma_start(out[kb * P : (kb + 1) * P, :], out_sb[kb][:])

@@ -20,8 +20,7 @@ P = 128
 PACK = 4
 PER_COL = 16
 BANKS = 8
-TINY = 2.0**-126
-HALF_UP = 2.0**63
+SHORT = 128
 
 
 def entries(list_tile, first, count):
@@ -39,6 +38,7 @@ def tile_moe_hib_relu_kernel(
     with ExitStack() as ctx:
         keep = ctx.enter_context(tc.tile_pool(name="keep", bufs=1))
         reuse = ctx.enter_context(tc.tile_pool(name="reuse", bufs=1))
+        placed = ctx.enter_context(tc.tile_pool(name="placed", bufs=1))
         psum = ctx.enter_context(tc.psum_pool(name="psum", bufs=1))
 
         dst_sb = keep.tile([P, T // PER_COL], U16, name="dst_sb")
@@ -51,11 +51,10 @@ def tile_moe_hib_relu_kernel(
         wgt_w = keep.tile([P, G, K], I32, name="wgt_w", align_bytes=64)
         wgt_s = keep.tile([P, G, K], U8, name="wgt_s", align_bytes=64)
         gate_first = reuse.tile([P, C2], F32, name="gate_first", tag="gate_first", align_bytes=64)
-        gate_rest = keep.tile([P, T - C2], F32, name="gate_rest", align_bytes=64)
-        a_sb = {}
-        for f in range(G):
-            for u in range(2):
-                a_sb[f, u] = reuse.tile([P, 2, C1], F32, name="a_sb", tag="a%d%d" % (f, u), align_bytes=64)
+        gate_second = keep.tile([P, C2], F32, name="gate_second", align_bytes=64)
+        gate_late = keep.tile([P, C1], F32, name="gate_late", align_bytes=64)
+        gates = [gate_first[:], gate_second[:], gate_late[:, 0:C2], gate_late[:, C2:C1]]
+        a_sb = [reuse.tile([P, PACK, C1], F32, name="a_sb", tag="a%d" % f, align_bytes=64) for f in range(G)]
 
         def zero_on_vector(words):
             last = words.shape[1] - 1
@@ -72,21 +71,21 @@ def tile_moe_hib_relu_kernel(
                 nc.sync.dma_start(plane[32 * q : 32 * q + 4, :, :].bitcast(I32), rows[4 * q : 4 * q + 4, :, :])
 
         a_src = a.rearrange("(p t) j -> p t j", t=PACK)
+        wet_src = wet_words.rearrange("e s p c -> p (e s) c").bitcast(I32)
         nc.sync.dma_start(dst_sb[:], dst)
         for q in range(4):
             queue = nc.sync if q < 3 else nc.scalar
             queue.dma_start(dy_s[32 * q : 32 * q + 4, :].bitcast(I32), dy_scales[0, 4 * q : 4 * q + 4, :].bitcast(I32))
-        wet_src = wet_words.rearrange("e s p c -> p (e s) c").bitcast(I32)
         nc.sync.dma_start(dy_w[:], dy_words[0].rearrange("p n d -> p (n d)").bitcast(I32))
         nc.sync.dma_start(wet_w[0][:].bitcast(I32), wet_src[:, 0:2, :])
         nc.sync.dma_start(offs2_sb[:], offs2)
         load_scale_rows(wet_s, wet_scales.rearrange("e s r h -> r (e s) h").bitcast(I32))
         nc.sync.dma_start(gate_first[:], gate[:, 0:C2])
+        nc.sync.dma_start(gate_second[:], gate[:, C2:C1])
         nc.sync.dma_start(wet_w[1][:].bitcast(I32), wet_src[:, 2:4, :])
-        nc.sync.dma_start(gate_rest[:], gate[:, C2:T])
-        for f in range(G):
-            for u in range(2):
-                nc.sync.dma_start(a_sb[f, u][:], a_src[:, 2 * u : 2 * u + 2, f * C1 : (f + 1) * C1])
+        for f in (1, 0):
+            nc.sync.dma_start(a_sb[f][:], a_src[:, :, f * C1 : (f + 1) * C1])
+        nc.sync.dma_start(gate_late[:], gate[:, C1:T])
         nc.sync.dma_start(wgt_w[:], wgt_words.rearrange("f s p k d -> p (f s) (k d)").bitcast(I32))
         load_scale_rows(wgt_s, wgt_scales.rearrange("f s r k -> r (f s) k").bitcast(I32))
         nc.sync.dma_start(offs_sb[:], offs)
@@ -96,9 +95,9 @@ def tile_moe_hib_relu_kernel(
             nc.vector.tensor_copy(tile[:], dy_s[:].indirect(entries(dst_sb, f * C1, C1)))
             return tile
 
-        def gather_words(first, count, tag):
-            tile = reuse.tile([P, count], U32, name="g_w", tag=tag, align_bytes=64)
-            nc.vector.tensor_copy(tile[:], dy_w[:].bitcast(U32).indirect(entries(dst_sb, first, count)))
+        def gather_words(e, tag):
+            tile = reuse.tile([P, C2], U32, name="g_w", tag=tag, align_bytes=64)
+            nc.vector.tensor_copy(tile[:], dy_w[:].bitcast(U32).indirect(entries(dst_sb, e * C2, C2)))
             return tile
 
         plane_w, plane_s = {}, {}
@@ -133,45 +132,39 @@ def tile_moe_hib_relu_kernel(
             banks_taken.append(tile)
             return tile
 
-        z = [keep.tile([P, PACK, C1], F32, name="z%d" % f, align_bytes=64) for f in range(G)]
-
-        def first_product(e, planes, words, scales):
+        def first_product(e, planes):
             f, place = divmod(e, E // G)
+            columns = slice(place * C2, (place + 1) * C2)
             acc = next_bank([P, len(planes), C2])
             for n, t in enumerate(planes):
                 nc.tensor.matmul_mx(
                     out=acc[:, n, :],
                     lhsT=plane_w[e, t].bitcast(FP4X4),
                     lhsT_scale=plane_s[e, t],
-                    rhs=words.bitcast(FP8X4),
-                    rhs_scale=scales,
+                    rhs=g_w[e][:].bitcast(FP8X4),
+                    rhs_scale=g_s[f][:, columns],
                     start=True,
                     stop=True,
                 )
-            weights = gate_first[:] if e == 0 else gate_rest[:, (e - 1) * C2 : e * C2]
-            weights = weights.unsqueeze(1).to_broadcast([P, len(planes), C2])
-            into = z[f][:, planes.start : planes.stop, place * C2 : (place + 1) * C2]
-            nc.vector.tensor_tensor(into, acc[:], weights, ALU.mult)
+            weights = gates[e].unsqueeze(1).to_broadcast([P, len(planes), C2])
+            nc.vector.tensor_tensor(z[f][:, planes.start : planes.stop, columns], acc[:], weights, ALU.mult)
 
         def scatter_on_scalar(window, list_tile, first, source):
-            nc.scalar.activation(window[:].indirect(entries(list_tile, first, C2)), source, ACT.Copy)
+            nc.scalar.activation(window[:].indirect(entries(list_tile, first, source.shape[1])), source, ACT.Copy)
 
-        def scatter_on_vector(window, list_tile, first, count, source):
-            nc.vector.tensor_copy(window[:].indirect(entries(list_tile, first, count)), source)
+        def scatter_on_vector(window, list_tile, first, source):
+            nc.vector.tensor_copy(window[:].indirect(entries(list_tile, first, source.shape[1])), source)
 
-        def z_on_scalar(e, t):
-            f, place = divmod(e, E // G)
-            scatter_on_scalar(win[f, t], offs2_sb, e * C2, z[f][:, t, place * C2 : (place + 1) * C2])
+        def scatter_z(scatter, f, t, first, last):
+            scatter(win[f, t], offs2_sb, f * C1 + first, z[f][:, t, first:last])
 
-        def mask_plane(f, t, slope):
-            nc.gpsimd.tensor_tensor(da[f][:, :, t], win[f, t][:, f * C1 : (f + 1) * C1], slope, ALU.mult)
+        def take_slope(f):
+            tile = keep.tile([P, PACK, C1], BF16, name="slope%d" % f, align_bytes=64)
+            nc.vector.tensor_scalar(tile[:], a_sb[f][:], 0.0, None, ALU.is_gt)
+            return tile
 
-        def slope_on_gpsimd(t):
-            spread = keep.tile([P, C1], F32, name="spread%d" % t, align_bytes=64)
-            slope = keep.tile([P, C1], BF16, name="slope%d" % t, align_bytes=64)
-            nc.gpsimd.tensor_scalar(spread[:], a_sb[0, t // 2][:, t % 2, :], TINY, 0.0, ALU.min, ALU.max)
-            nc.gpsimd.tensor_scalar(slope[:], spread[:], HALF_UP, HALF_UP, ALU.mult, ALU.mult)
-            return slope
+        def mask_plane(f, t):
+            nc.gpsimd.tensor_tensor(da[f][:, :, t], win[f, t][:, f * C1 : (f + 1) * C1], slope[f][:, t, :], ALU.mult)
 
         def second_product(f):
             da_w = keep.tile([P, C1], U32, name="da_w%d" % f, align_bytes=64)
@@ -196,63 +189,69 @@ def tile_moe_hib_relu_kernel(
         order_words(0, range(0, 1), "lead_w")
         order_words(0, range(1, 4), "first_w")
         order_words(1, range(0, 4), "plane_w1")
+        z = [keep.tile([P, PACK, C1], F32, name="z0", align_bytes=64)]
         g_s = [gather_scales(0, "g_s0")]
-        g_w0 = gather_words(0, C2, "g_w0")
+        g_w = [gather_words(0, "g_w0"), gather_words(1, "g_w1")]
         order_scales(range(0, 1), range(0, 1), "lead_s")
         order_scales(range(0, 1), range(1, 4), "first_s")
-        for planes in (range(0, 1), range(1, 2), range(2, 4)):
-            first_product(0, planes, g_w0[:], g_s[0][:, 0:C2])
-        g_w1 = gather_words(C2, C2, "g_w1")
-        order_scales(range(1, E), range(0, 4), "gate_first")
-        for planes in (range(0, 2), range(2, 4)):
-            first_product(1, planes, g_w1[:], g_s[0][:, C2:C1])
+        first_product(0, range(0, 1))
+        order_scales(range(1, 2), range(0, 4), "lead_s")
+        for e, planes in ((0, range(1, 2)), (1, range(0, 2)), (0, range(2, 4)), (1, range(2, 4))):
+            first_product(e, planes)
         order_late_words("first_w")
-        g_s.append(gather_scales(1, "first_s"))
-        g_w_late = {2: gather_words(2 * C2, C2, "g_w0"), 3: gather_words(3 * C2, C2, "g_w1")}
-        for e in (2, 3):
-            columns = slice((e - 2) * C2, (e - 1) * C2)
-            for planes in (range(0, 2), range(2, 4)):
-                first_product(e, planes, g_w_late[e][:], g_s[1][:, columns])
+        order_scales(range(2, 4), range(0, 4), "first_s")
+        g_s.append(gather_scales(1, "gate_first"))
+        g_w.append(gather_words(2, "g_w0"))
+        g_w.append(gather_words(3, "g_w1"))
+        slope = {f: take_slope(f) for f in (1, 0)}
+        z.append(reuse.tile([P, PACK, C1], F32, name="z1", tag="a0", align_bytes=64))
+        for planes in (range(0, 2), range(2, 4)):
+            for e in (2, 3):
+                first_product(e, planes)
 
-        da = [reuse.tile([P, C1, PACK], BF16, name="da", tag="da%d" % f, align_bytes=64) for f in range(G)]
+        half = 2 * C1 * 2
+        da = [placed.tile([P, C1, PACK], BF16, name="da0", offset=half, align_bytes=64)]
         win = {}
-        for f, t in ((0, 0), (0, 1), (0, 2), (0, 3), (1, 0), (1, 3)):
+        for f, t in ((0, 0), (0, 1), (0, 2), (0, 3), (1, 0), (1, 2), (1, 3)):
             win[f, t] = keep.tile([P, T], F32, name="win%d%d" % (f, t), align_bytes=64)
 
-        for e, t in ((0, 0), (0, 1), (0, 2), (0, 3), (1, 0), (1, 1), (1, 2), (1, 3)):
-            z_on_scalar(e, t)
-        slopes = [slope_on_gpsimd(t) for t in range(PACK)]
+        scatter_z(scatter_on_scalar, 0, 0, 0, SHORT)
         for t in range(PACK):
-            mask_plane(0, t, slopes[t][:])
+            if t + 1 < PACK:
+                scatter_z(scatter_on_scalar, 0, t + 1, 0, SHORT)
+            scatter_z(scatter_on_scalar, 0, t, SHORT, C1)
+            mask_plane(0, t)
 
-        scatter_on_vector(win[1, 0], offs2_sb, C1, C1, z[1][:, 0, :])
-        slope_late = keep.tile([P, PACK, C1], BF16, name="slope_late", align_bytes=64)
-        for u in range(2):
-            nc.vector.tensor_scalar(slope_late[:, 2 * u : 2 * u + 2, :], a_sb[1, u][:], 0.0, None, ALU.is_gt)
-        win[1, 2] = reuse.tile([P, T], F32, name="win", tag="a11", align_bytes=64)
-        scatter_on_vector(win[1, 2], offs2_sb, C1, C2, z[1][:, 2, 0:C2])
-        z_on_scalar(2, 3)
-        z_on_scalar(3, 3)
-        z_on_scalar(3, 2)
+        scatter_z(scatter_on_vector, 1, 0, 0, C1)
+        scatter_z(scatter_on_vector, 1, 2, 0, C1 - SHORT)
+        scatter_z(scatter_on_scalar, 1, 3, 0, C2)
+        scatter_z(scatter_on_scalar, 1, 2, C1 - SHORT, C1)
+        scatter_z(scatter_on_scalar, 1, 3, C2, C1)
         accs = second_product(0)
-        win[1, 1] = reuse.tile([P, T], F32, name="win", tag="da0", align_bytes=64)
-        scatter_on_vector(win[1, 1], offs2_sb, C1, C1, z[1][:, 1, :])
-        for t in (0, 3, 2, 1):
-            mask_plane(1, t, slope_late[:, t, :])
+        win[1, 1] = placed.tile([P, T], F32, name="win11", offset=0, align_bytes=64)
+        da.append(placed.tile([P, C1, PACK], BF16, name="da1", offset=2 * half, align_bytes=64))
+        scatter_z(scatter_on_vector, 1, 1, 0, C1)
+        for t in (0, 2, 3, 1):
+            mask_plane(1, t)
 
         out_sb = [keep.tile([P, T], F32, name="out%d" % kb, align_bytes=64) for kb in range(K // P)]
-        dx = [keep.tile([P, C1], F32, name="dx0%d" % kb, align_bytes=64) for kb in range(K // P)]
-        nc.scalar.copy(dx[1][:], accs[1][:])
-        nc.scalar.copy(dx[0][:], accs[0][:])
+        dx_low = keep.tile([P, C1 - SHORT], F32, name="dx_low", align_bytes=64)
+        dx_high = keep.tile([P, C1], F32, name="dx_high", align_bytes=64)
+        nc.scalar.copy(dx_low[:], accs[0][:, 0 : C1 - SHORT])
+        nc.scalar.copy(dx_high[:], accs[1][:])
         for place in range(2):
-            scatter_on_scalar(out_sb[1], offs_sb, place * C2, dx[1][:, place * C2 : (place + 1) * C2])
-        scatter_on_vector(out_sb[0], offs_sb, 0, C1, dx[0][:])
+            scatter_on_scalar(out_sb[1], offs_sb, place * C2, dx_high[:, place * C2 : (place + 1) * C2])
+        scatter_on_vector(out_sb[0], offs_sb, 0, dx_low[:])
 
+        held = accs[0]
         accs = second_product(1)
+        dx_held = placed.tile([P, SHORT], F32, name="dx_held", offset=3 * half, align_bytes=64)
+        nc.scalar.copy(dx_held[:], held[:, C1 - SHORT : C1])
+        scatter_on_vector(out_sb[0], offs_sb, C1 - SHORT, dx_held[:])
         dx = [keep.tile([P, C1], F32, name="dx1%d" % kb, align_bytes=64) for kb in range(K // P)]
-        nc.vector.tensor_copy(dx[0][:], accs[0][:])
-        nc.scalar.copy(dx[1][:], accs[1][:])
-        scatter_on_vector(out_sb[0], offs_sb, C1, C1, dx[0][:])
+        for kb in range(K // P):
+            nc.scalar.copy(dx[kb][:], accs[kb][:])
+        scatter_on_vector(out_sb[0], offs_sb, C1, dx[0][:])
         for place in range(2):
             scatter_on_scalar(out_sb[1], offs_sb, C1 + place * C2, dx[1][:, place * C2 : (place + 1) * C2])
         for kb in range(K // P):

@@ -19,8 +19,8 @@ ALU = mybir.AluOpType
 P = 128
 PACK = 4
 PER_COL = 16
-BANKS = 8
 SHORT = 128
+KIB = 1024
 
 
 def entries(list_tile, first, count):
@@ -54,7 +54,9 @@ def tile_moe_hib_relu_kernel(
         gate_second = keep.tile([P, C2], F32, name="gate_second", align_bytes=64)
         gate_late = keep.tile([P, C1], F32, name="gate_late", align_bytes=64)
         gates = [gate_first[:], gate_second[:], gate_late[:, 0:C2], gate_late[:, C2:C1]]
-        a_sb = [reuse.tile([P, PACK, C1], F32, name="a_sb", tag="a%d" % f, align_bytes=64) for f in range(G)]
+        a_lead = placed.tile([P, 1, C1], F32, name="a_lead", offset=30 * KIB, align_bytes=64)
+        a_rest = reuse.tile([P, PACK - 1, C1], F32, name="a_rest", tag="a_rest", align_bytes=64)
+        a_late = placed.tile([P, PACK, C1], F32, name="a_late", offset=20 * KIB, align_bytes=64)
 
         def zero_on_vector(words):
             last = words.shape[1] - 1
@@ -83,20 +85,19 @@ def tile_moe_hib_relu_kernel(
         nc.sync.dma_start(gate_first[:], gate[:, 0:C2])
         nc.sync.dma_start(gate_second[:], gate[:, C2:C1])
         nc.sync.dma_start(wet_w[1][:].bitcast(I32), wet_src[:, 2:4, :])
-        for f in (1, 0):
-            nc.sync.dma_start(a_sb[f][:], a_src[:, :, f * C1 : (f + 1) * C1])
+        nc.sync.dma_start(a_lead[:], a_src[:, 0:1, 0:C1])
+        nc.sync.dma_start(a_late[:], a_src[:, :, C1:T])
+        nc.sync.dma_start(a_rest[:], a_src[:, 1:PACK, 0:C1])
         nc.sync.dma_start(gate_late[:], gate[:, C1:T])
         nc.sync.dma_start(wgt_w[:], wgt_words.rearrange("f s p k d -> p (f s) (k d)").bitcast(I32))
         load_scale_rows(wgt_s, wgt_scales.rearrange("f s r k -> r (f s) k").bitcast(I32))
         nc.sync.dma_start(offs_sb[:], offs)
 
-        def gather_scales(f, tag):
-            tile = reuse.tile([P, C1], U8, name="g_s", tag=tag, align_bytes=64)
+        def gather_scales(f, tile):
             nc.vector.tensor_copy(tile[:], dy_s[:].indirect(entries(dst_sb, f * C1, C1)))
             return tile
 
-        def gather_words(e, tag):
-            tile = reuse.tile([P, C2], U32, name="g_w", tag=tag, align_bytes=64)
+        def gather_words(e, tile):
             nc.vector.tensor_copy(tile[:], dy_w[:].bitcast(U32).indirect(entries(dst_sb, e * C2, C2)))
             return tile
 
@@ -125,17 +126,13 @@ def tile_moe_hib_relu_kernel(
                 for n, t in enumerate(planes):
                     plane_s[e, t] = tile[:, m, n, :]
 
-        banks_taken = []
+        def bank(n, shape):
+            return psum.tile(shape, F32, name="bank", tag="bank%d" % n)
 
-        def next_bank(shape):
-            tile = psum.tile(shape, F32, name="bank", tag="bank%d" % (len(banks_taken) % BANKS))
-            banks_taken.append(tile)
-            return tile
-
-        def first_product(e, planes):
+        def first_product(e, planes, n_bank):
             f, place = divmod(e, E // G)
             columns = slice(place * C2, (place + 1) * C2)
-            acc = next_bank([P, len(planes), C2])
+            acc = bank(n_bank, [P, len(planes), C2])
             for n, t in enumerate(planes):
                 nc.tensor.matmul_mx(
                     out=acc[:, n, :],
@@ -158,22 +155,24 @@ def tile_moe_hib_relu_kernel(
         def scatter_z(scatter, f, t, first, last):
             scatter(win[f, t], offs2_sb, f * C1 + first, z[f][:, t, first:last])
 
-        def take_slope(f):
-            tile = keep.tile([P, PACK, C1], BF16, name="slope%d" % f, align_bytes=64)
-            nc.vector.tensor_scalar(tile[:], a_sb[f][:], 0.0, None, ALU.is_gt)
-            return tile
+        def take_slope(tile, source, f, planes):
+            nc.vector.tensor_scalar(tile[:], source[:], 0.0, None, ALU.is_gt)
+            for n, t in enumerate(planes):
+                slope[f, t] = tile[:, n, :]
 
         def mask_plane(f, t):
-            nc.gpsimd.tensor_tensor(da[f][:, :, t], win[f, t][:, f * C1 : (f + 1) * C1], slope[f][:, t, :], ALU.mult)
+            nc.gpsimd.tensor_tensor(da[f][:, :, t], win[f, t][:, f * C1 : (f + 1) * C1], slope[f, t], ALU.mult)
 
-        def second_product(f):
-            da_w = keep.tile([P, C1], U32, name="da_w%d" % f, align_bytes=64)
-            da_s = keep.tile([P, C1], U8, name="da_s%d" % f, align_bytes=64)
-            nc.vector.quantize_mx(out=da_w[:].bitcast(FP8X4), scales=da_s[:], in_=da[f][:].rearrange("p j t -> p (j t)"))
+        def second_product(f, first, last, banks):
+            count = last - first
+            da_w = keep.tile([P, count], U32, name="da_w%d_%d" % (f, first), align_bytes=64)
+            da_s = keep.tile([P, count], U8, name="da_s%d_%d" % (f, first), align_bytes=64)
+            values = da[f][:, first:last, :].rearrange("p j t -> p (j t)")
+            nc.vector.quantize_mx(out=da_w[:].bitcast(FP8X4), scales=da_s[:], in_=values)
             accs = []
             for kb in range(K // P):
                 k_cols = slice(kb * P, (kb + 1) * P)
-                acc = next_bank([P, C1])
+                acc = bank(banks[kb], [P, count])
                 nc.tensor.matmul_mx(
                     out=acc[:],
                     lhsT=wgt_w[:, f, k_cols].bitcast(FP8X4),
@@ -190,69 +189,72 @@ def tile_moe_hib_relu_kernel(
         order_words(0, range(1, 4), "first_w")
         order_words(1, range(0, 4), "plane_w1")
         z = [keep.tile([P, PACK, C1], F32, name="z0", align_bytes=64)]
-        g_s = [gather_scales(0, "g_s0")]
-        g_w = [gather_words(0, "g_w0"), gather_words(1, "g_w1")]
+        g_s = [gather_scales(0, keep.tile([P, C1], U8, name="g_s0", align_bytes=64))]
+        g_w = [gather_words(e, keep.tile([P, C2], U32, name="g_w%d" % e, align_bytes=64)) for e in range(2)]
         order_scales(range(0, 1), range(0, 1), "lead_s")
         order_scales(range(0, 1), range(1, 4), "first_s")
-        first_product(0, range(0, 1))
+        first_product(0, range(0, 1), 0)
         order_scales(range(1, 2), range(0, 4), "lead_s")
-        for e, planes in ((0, range(1, 2)), (1, range(0, 2)), (0, range(2, 4)), (1, range(2, 4))):
-            first_product(e, planes)
+        for e, planes, n in ((0, range(1, 2), 1), (1, range(0, 2), 2), (0, range(2, 4), 2), (1, range(2, 4), 3)):
+            first_product(e, planes, n)
         order_late_words("first_w")
         order_scales(range(2, 4), range(0, 4), "first_s")
-        g_s.append(gather_scales(1, "gate_first"))
-        g_w.append(gather_words(2, "g_w0"))
-        g_w.append(gather_words(3, "g_w1"))
-        slope = {f: take_slope(f) for f in (1, 0)}
-        z.append(reuse.tile([P, PACK, C1], F32, name="z1", tag="a0", align_bytes=64))
-        for planes in (range(0, 2), range(2, 4)):
-            for e in (2, 3):
-                first_product(e, planes)
 
-        half = 2 * C1 * 2
-        da = [placed.tile([P, C1, PACK], BF16, name="da0", offset=half, align_bytes=64)]
-        win = {}
-        for f, t in ((0, 0), (0, 1), (0, 2), (0, 3), (1, 0), (1, 2), (1, 3)):
+        half = 2 * KIB
+        win, slope = {}, {}
+        take_slope(keep.tile([P, 1, C1], BF16, name="slope_lead", align_bytes=64), a_lead, 0, range(0, 1))
+        g_s.append(gather_scales(1, placed.tile([P, C1], U8, name="g_s1", offset=30 * KIB, align_bytes=64)))
+        for e, offset in ((2, 30 * KIB + 512), (3, 31 * KIB + 512)):
+            g_w.append(gather_words(e, placed.tile([P, C2], U32, name="g_w%d" % e, offset=offset, align_bytes=64)))
+        win[0, 0] = placed.tile([P, T], F32, name="win00", offset=5 * half, align_bytes=64)
+        for f, t in ((0, 1), (0, 2), (1, 0), (1, 1), (1, 3)):
             win[f, t] = keep.tile([P, T], F32, name="win%d%d" % (f, t), align_bytes=64)
-
+        da = [placed.tile([P, C1, PACK], BF16, name="da0", offset=half, align_bytes=64)]
         scatter_z(scatter_on_scalar, 0, 0, 0, SHORT)
-        for t in range(PACK):
-            if t + 1 < PACK:
-                scatter_z(scatter_on_scalar, 0, t + 1, 0, SHORT)
+        scatter_z(scatter_on_scalar, 0, 1, 0, SHORT)
+        scatter_z(scatter_on_scalar, 0, 0, SHORT, C1)
+        mask_plane(0, 0)
+        take_slope(placed.tile([P, PACK, C1], BF16, name="slope_late", offset=4 * half, align_bytes=64), a_late, 1, range(0, 4))
+        take_slope(placed.tile([P, 3, C1], BF16, name="slope_rest", offset=26 * KIB, align_bytes=64), a_rest, 0, range(1, 4))
+        scatter_z(scatter_on_scalar, 0, 2, 0, SHORT)
+        for t in (1, 2):
             scatter_z(scatter_on_scalar, 0, t, SHORT, C1)
             mask_plane(0, t)
 
-        scatter_z(scatter_on_vector, 1, 0, 0, C1)
-        scatter_z(scatter_on_vector, 1, 2, 0, C1 - SHORT)
-        scatter_z(scatter_on_scalar, 1, 3, 0, C2)
-        scatter_z(scatter_on_scalar, 1, 2, C1 - SHORT, C1)
-        scatter_z(scatter_on_scalar, 1, 3, C2, C1)
-        accs = second_product(0)
-        win[1, 1] = placed.tile([P, T], F32, name="win11", offset=0, align_bytes=64)
+        z.append(placed.tile([P, PACK, C1], F32, name="z1", offset=14 * KIB, align_bytes=64))
+        first_product(2, range(0, 2), 4)
+        win[0, 3] = reuse.tile([P, T], F32, name="win03", tag="a_rest", align_bytes=64)
+        scatter_z(scatter_on_vector, 0, 3, 0, C1)
+        mask_plane(0, 3)
+        for e, planes, n in ((3, range(0, 2), 5), (2, range(2, 4), 6), (3, range(2, 4), 7)):
+            first_product(e, planes, n)
+        for t, first, last in ((0, 0, C2), (1, 0, SHORT), (0, C2, C1), (1, SHORT, C1), (3, 0, C2), (3, C2, C1)):
+            scatter_z(scatter_on_scalar, 1, t, first, last)
+
+        low, high = second_product(0, 0, C1, (0, 1))
+        win[1, 2] = placed.tile([P, T], F32, name="win12", offset=0, align_bytes=64)
         da.append(placed.tile([P, C1, PACK], BF16, name="da1", offset=2 * half, align_bytes=64))
-        scatter_z(scatter_on_vector, 1, 1, 0, C1)
-        for t in (0, 2, 3, 1):
+        scatter_z(scatter_on_vector, 1, 2, 0, C1)
+        for t in range(PACK):
             mask_plane(1, t)
 
-        out_sb = [keep.tile([P, T], F32, name="out%d" % kb, align_bytes=64) for kb in range(K // P)]
-        dx_low = keep.tile([P, C1 - SHORT], F32, name="dx_low", align_bytes=64)
-        dx_high = keep.tile([P, C1], F32, name="dx_high", align_bytes=64)
-        nc.scalar.copy(dx_low[:], accs[0][:, 0 : C1 - SHORT])
-        nc.scalar.copy(dx_high[:], accs[1][:])
-        for place in range(2):
-            scatter_on_scalar(out_sb[1], offs_sb, place * C2, dx_high[:, place * C2 : (place + 1) * C2])
-        scatter_on_vector(out_sb[0], offs_sb, 0, dx_low[:])
+        def leave_psum(copy, acc, name):
+            tile = keep.tile([P, acc.shape[1]], F32, name=name, align_bytes=64)
+            copy(tile[:], acc)
+            return tile
 
-        held = accs[0]
-        accs = second_product(1)
-        dx_held = placed.tile([P, SHORT], F32, name="dx_held", offset=3 * half, align_bytes=64)
-        nc.scalar.copy(dx_held[:], held[:, C1 - SHORT : C1])
-        scatter_on_vector(out_sb[0], offs_sb, C1 - SHORT, dx_held[:])
-        dx = [keep.tile([P, C1], F32, name="dx1%d" % kb, align_bytes=64) for kb in range(K // P)]
-        for kb in range(K // P):
-            nc.scalar.copy(dx[kb][:], accs[kb][:])
-        scatter_on_vector(out_sb[0], offs_sb, C1, dx[0][:])
-        for place in range(2):
-            scatter_on_scalar(out_sb[1], offs_sb, C1 + place * C2, dx[1][:, place * C2 : (place + 1) * C2])
-        for kb in range(K // P):
-            nc.sync.dma_start(out[kb * P : (kb + 1) * P, :], out_sb[kb][:])
+        out_low = keep.tile([P, T], F32, name="out_low", align_bytes=64)
+        out_high = keep.tile([P, T], F32, name="out_high", align_bytes=64)
+        dx_high = leave_psum(nc.vector.tensor_copy, high[:], "dx0_high")
+        dx_low = leave_psum(nc.vector.tensor_copy, low[:], "dx0_low")
+        for first in (0, C2):
+            scatter_on_scalar(out_high, offs_sb, first, dx_high[:, first : first + C2])
+        scatter_on_vector(out_low, offs_sb, 0, dx_low[:])
+
+        late = [second_product(1, 0, C2, (2, 3)), second_product(1, C2, C1, (4, 5))]
+        for place, (low, high) in enumerate(late):
+            first = C1 + place * C2
+            scatter_on_vector(out_low, offs_sb, first, leave_psum(nc.vector.tensor_copy, low[:], "dx1_low%d" % place)[:])
+            scatter_on_scalar(out_high, offs_sb, first, leave_psum(nc.scalar.copy, high[:], "dx1_high%d" % place)[:])
+        nc.sync.dma_start(out[0:P, :], out_low[:])
+        nc.sync.dma_start(out[P : 2 * P, :], out_high[:])

@@ -46,17 +46,16 @@ def tile_moe_hib_relu_kernel(
         offs_sb = keep.tile([P, T // PER_COL], U16, name="offs_sb")
         dy_w = keep.tile([P, T], I32, name="dy_w", align_bytes=64)
         dy_s = keep.tile([P, T], U8, name="dy_s", align_bytes=64)
-        wet_w = [keep.tile([P, E // G, 2 * H], U8, name="wet_w%d" % f, align_bytes=64) for f in range(G)]
+        wet_early = keep.tile([P, E // G, 2 * H], U8, name="wet_early", align_bytes=64)
+        wet_late = keep.tile([P, E // G, 2 * H], U8, name="wet_late", align_bytes=64)
         wet_s = keep.tile([P, E, H], U8, name="wet_s", align_bytes=64)
         wgt_w = keep.tile([P, G, K], I32, name="wgt_w", align_bytes=64)
         wgt_s = keep.tile([P, G, K], U8, name="wgt_s", align_bytes=64)
-        gate_first = reuse.tile([P, C2], F32, name="gate_first", tag="gate_first", align_bytes=64)
-        gate_second = keep.tile([P, C2], F32, name="gate_second", align_bytes=64)
+        gate_lead = reuse.tile([P, SHORT], F32, name="gate_lead", tag="gate_lead", align_bytes=64)
+        gate_rest = placed.tile([P, C1], F32, name="gate_rest", offset=24 * KIB, align_bytes=64)
         gate_late = keep.tile([P, C1], F32, name="gate_late", align_bytes=64)
-        gates = [gate_first[:], gate_second[:], gate_late[:, 0:C2], gate_late[:, C2:C1]]
-        a_lead = placed.tile([P, 1, C1], F32, name="a_lead", offset=30 * KIB, align_bytes=64)
-        a_rest = reuse.tile([P, PACK - 1, C1], F32, name="a_rest", tag="a_rest", align_bytes=64)
-        a_late = placed.tile([P, PACK, C1], F32, name="a_late", offset=20 * KIB, align_bytes=64)
+        a_first = placed.tile([P, PACK, C1], F32, name="a_first", offset=12 * KIB, align_bytes=64)
+        a_late = keep.tile([P, PACK, C1], F32, name="a_late", align_bytes=64)
 
         def zero_on_vector(words):
             last = words.shape[1] - 1
@@ -65,7 +64,8 @@ def tile_moe_hib_relu_kernel(
 
         nc.gpsimd.memset(dy_s[:].bitcast(I32)[:, 0:P], 0)
         zero_on_vector(dy_s[:].bitcast(I32)[:, P : 2 * P])
-        zero_on_vector(words_of(wet_s))
+        nc.gpsimd.memset(words_of(wet_s)[:, 0:P], 0)
+        zero_on_vector(words_of(wet_s)[:, P : E * P])
         nc.gpsimd.memset(words_of(wgt_s), 0)
 
         def load_scale_rows(plane, rows):
@@ -78,48 +78,46 @@ def tile_moe_hib_relu_kernel(
         for q in range(4):
             queue = nc.sync if q < 3 else nc.scalar
             queue.dma_start(dy_s[32 * q : 32 * q + 4, :].bitcast(I32), dy_scales[0, 4 * q : 4 * q + 4, :].bitcast(I32))
-        nc.sync.dma_start(dy_w[:], dy_words[0].rearrange("p n d -> p (n d)").bitcast(I32))
-        nc.sync.dma_start(wet_w[0][:].bitcast(I32), wet_src[:, 0:2, :])
-        nc.sync.dma_start(offs2_sb[:], offs2)
         load_scale_rows(wet_s, wet_scales.rearrange("e s r h -> r (e s) h").bitcast(I32))
-        nc.sync.dma_start(gate_first[:], gate[:, 0:C2])
-        nc.sync.dma_start(gate_second[:], gate[:, C2:C1])
-        nc.sync.dma_start(wet_w[1][:].bitcast(I32), wet_src[:, 2:4, :])
-        nc.sync.dma_start(a_lead[:], a_src[:, 0:1, 0:C1])
+        nc.sync.dma_start(wet_early[:].bitcast(I32), wet_src[:, 0:2, :])
+        nc.sync.dma_start(dy_w[:], dy_words[0].rearrange("p n d -> p (n d)").bitcast(I32))
+        nc.sync.dma_start(offs2_sb[:], offs2)
+        nc.sync.dma_start(gate_lead[:], gate[:, 0:SHORT])
+        nc.sync.dma_start(gate_rest[:], gate[:, 0:C1])
+        nc.sync.dma_start(wet_late[:].bitcast(I32), wet_src[:, 2:4, :])
         nc.sync.dma_start(a_late[:], a_src[:, :, C1:T])
-        nc.sync.dma_start(a_rest[:], a_src[:, 1:PACK, 0:C1])
+        nc.sync.dma_start(a_first[:], a_src[:, :, 0:C1])
         nc.sync.dma_start(gate_late[:], gate[:, C1:T])
         nc.sync.dma_start(wgt_w[:], wgt_words.rearrange("f s p k d -> p (f s) (k d)").bitcast(I32))
         load_scale_rows(wgt_s, wgt_scales.rearrange("f s r k -> r (f s) k").bitcast(I32))
         nc.sync.dma_start(offs_sb[:], offs)
 
-        def gather_scales(f, tile):
+        def gather_scales(f):
+            tile = keep.tile([P, C1], U8, name="g_s%d" % f, align_bytes=64)
             nc.vector.tensor_copy(tile[:], dy_s[:].indirect(entries(dst_sb, f * C1, C1)))
             return tile
 
-        def gather_words(e, tile):
-            nc.vector.tensor_copy(tile[:], dy_w[:].bitcast(U32).indirect(entries(dst_sb, e * C2, C2)))
+        def gather_words(first, tile):
+            nc.vector.tensor_copy(tile[:], dy_w[:].bitcast(U32).indirect(entries(dst_sb, first, tile.shape[1])))
             return tile
 
         plane_w, plane_s = {}, {}
 
         def order_words(e, planes, tag):
             tile = reuse.tile([P, len(planes), 2 * P], U8, name="plane_w", tag=tag, align_bytes=64)
-            source = wet_w[0][:, e, :].bitcast(U16).rearrange("p (m t) -> p t m", t=PACK)
+            source = wet_early[:, e, :].bitcast(U16).rearrange("p (m t) -> p t m", t=PACK)
             nc.scalar.copy(tile[:].bitcast(U16), source[:, planes.start : planes.stop, :])
             for n, t in enumerate(planes):
                 plane_w[e, t] = tile[:, n, :]
 
-        def order_late_words(tag):
-            tile = reuse.tile([P, E // G, PACK, 2 * P], U8, name="late_w", tag=tag, align_bytes=64)
-            source = wet_w[1][:].bitcast(U16).rearrange("p e (m t) -> p e t m", t=PACK)
+        def order_late_words(tile):
+            source = wet_late[:].bitcast(U16).rearrange("p e (m t) -> p e t m", t=PACK)
             nc.vector.tensor_copy(tile[:].bitcast(U16), source)
             for m in range(E // G):
                 for t in range(PACK):
                     plane_w[E // G + m, t] = tile[:, m, t, :]
 
-        def order_scales(experts, planes, tag):
-            tile = reuse.tile([P, len(experts), len(planes), P], U8, name="plane_s", tag=tag, align_bytes=64)
+        def order_scales(experts, planes, tile):
             source = wet_s[:].rearrange("p e (m t) -> p e t m", t=PACK)
             nc.vector.tensor_copy(tile[:], source[:, experts.start : experts.stop, planes.start : planes.stop, :])
             for m, e in enumerate(experts):
@@ -129,22 +127,24 @@ def tile_moe_hib_relu_kernel(
         def bank(n, shape):
             return psum.tile(shape, F32, name="bank", tag="bank%d" % n)
 
-        def first_product(e, planes, n_bank):
-            f, place = divmod(e, E // G)
-            columns = slice(place * C2, (place + 1) * C2)
-            acc = bank(n_bank, [P, len(planes), C2])
+        def first_product(first, words, planes, n_bank):
+            count = words.shape[1]
+            e, f = first // C2, first // C1
+            acc = bank(n_bank, [P, len(planes), count])
             for n, t in enumerate(planes):
                 nc.tensor.matmul_mx(
                     out=acc[:, n, :],
                     lhsT=plane_w[e, t].bitcast(FP4X4),
                     lhsT_scale=plane_s[e, t],
-                    rhs=g_w[e][:].bitcast(FP8X4),
-                    rhs_scale=g_s[f][:, columns],
+                    rhs=words.bitcast(FP8X4),
+                    rhs_scale=g_s[f][:, first - f * C1 : first - f * C1 + count],
                     start=True,
                     stop=True,
                 )
-            weights = gates[e].unsqueeze(1).to_broadcast([P, len(planes), C2])
-            nc.vector.tensor_tensor(z[f][:, planes.start : planes.stop, columns], acc[:], weights, ALU.mult)
+            return acc
+
+        def times_gate(into, acc, weights):
+            nc.vector.tensor_tensor(into, acc[:], weights.unsqueeze(1).to_broadcast(list(acc.shape)), ALU.mult)
 
         def scatter_on_scalar(window, list_tile, first, source):
             nc.scalar.activation(window[:].indirect(entries(list_tile, first, source.shape[1])), source, ACT.Copy)
@@ -153,15 +153,15 @@ def tile_moe_hib_relu_kernel(
             nc.vector.tensor_copy(window[:].indirect(entries(list_tile, first, source.shape[1])), source)
 
         def scatter_z(scatter, f, t, first, last):
-            scatter(win[f, t], offs2_sb, f * C1 + first, z[f][:, t, first:last])
+            scatter(win[f, t], offs2_sb, f * C1 + first, z[f, t][:, first:last])
 
-        def take_slope(tile, source, f, planes):
+        def take_slope(source, name):
+            tile = keep.tile([P, PACK, C1], BF16, name=name, align_bytes=64)
             nc.vector.tensor_scalar(tile[:], source[:], 0.0, None, ALU.is_gt)
-            for n, t in enumerate(planes):
-                slope[f, t] = tile[:, n, :]
+            return tile
 
         def mask_plane(f, t):
-            nc.gpsimd.tensor_tensor(da[f][:, :, t], win[f, t][:, f * C1 : (f + 1) * C1], slope[f, t], ALU.mult)
+            nc.gpsimd.tensor_tensor(da[f][:, :, t], win[f, t][:, f * C1 : (f + 1) * C1], slope[f][:, t, :], ALU.mult)
 
         def second_product(f, first, last, banks):
             count = last - first
@@ -188,52 +188,57 @@ def tile_moe_hib_relu_kernel(
         order_words(0, range(0, 1), "lead_w")
         order_words(0, range(1, 4), "first_w")
         order_words(1, range(0, 4), "plane_w1")
-        z = [keep.tile([P, PACK, C1], F32, name="z0", align_bytes=64)]
-        g_s = [gather_scales(0, keep.tile([P, C1], U8, name="g_s0", align_bytes=64))]
-        g_w = [gather_words(e, keep.tile([P, C2], U32, name="g_w%d" % e, align_bytes=64)) for e in range(2)]
-        order_scales(range(0, 1), range(0, 1), "lead_s")
-        order_scales(range(0, 1), range(1, 4), "first_s")
-        first_product(0, range(0, 1), 0)
-        order_scales(range(1, 2), range(0, 4), "lead_s")
-        for e, planes, n in ((0, range(1, 2), 1), (1, range(0, 2), 2), (0, range(2, 4), 2), (1, range(2, 4), 3)):
-            first_product(e, planes, n)
-        order_late_words("first_w")
-        order_scales(range(2, 4), range(0, 4), "first_s")
+        z_first = keep.tile([P, PACK, C1], F32, name="z_first", align_bytes=64)
+        z = {(0, t): z_first[:, t, :] for t in range(PACK)}
+        g_s = [gather_scales(f) for f in range(G)]
+        order_scales(range(0, 1), range(0, 4), keep.tile([P, 1, PACK, P], U8, name="first_s", align_bytes=64))
+        w_lead = gather_words(0, keep.tile([P, SHORT], U32, name="w_lead", align_bytes=64))
+        w_rest = gather_words(SHORT, keep.tile([P, C1 - SHORT], U32, name="w_rest", align_bytes=64))
+        times_gate(z_first[:, 0:1, 0:SHORT], first_product(0, w_lead[:], range(0, 1), 0), gate_lead[:])
+        order_scales(range(1, 2), range(0, 4), reuse.tile([P, 1, PACK, P], U8, name="second_s", tag="gate_lead", align_bytes=64))
+        times_gate(z_first[:, 1:4, 0:SHORT], first_product(0, w_lead[:], range(1, 4), 1), gate_rest[:, 0:SHORT])
+        times_gate(z_first[:, :, SHORT:C2], first_product(SHORT, w_rest[:, 0:SHORT], range(0, 4), 2), gate_rest[:, SHORT:C2])
+        for planes, n in ((range(0, 2), 3), (range(2, 4), 0)):
+            acc = first_product(C2, w_rest[:, SHORT:], planes, n)
+            times_gate(z_first[:, planes.start : planes.stop, C2:C1], acc, gate_rest[:, C2:C1])
 
-        half = 2 * KIB
-        win, slope = {}, {}
-        take_slope(keep.tile([P, 1, C1], BF16, name="slope_lead", align_bytes=64), a_lead, 0, range(0, 1))
-        g_s.append(gather_scales(1, placed.tile([P, C1], U8, name="g_s1", offset=30 * KIB, align_bytes=64)))
-        for e, offset in ((2, 30 * KIB + 512), (3, 31 * KIB + 512)):
-            g_w.append(gather_words(e, placed.tile([P, C2], U32, name="g_w%d" % e, offset=offset, align_bytes=64)))
-        win[0, 0] = placed.tile([P, T], F32, name="win00", offset=5 * half, align_bytes=64)
-        for f, t in ((0, 1), (0, 2), (1, 0), (1, 1), (1, 3)):
+        order_late_words(placed.tile([P, E // G, PACK, 2 * P], U8, name="late_w", offset=25 * KIB + 512, align_bytes=64))
+        order_scales(range(2, 4), range(0, 4), placed.tile([P, E // G, PACK, P], U8, name="late_s", offset=24 * KIB + 256, align_bytes=64))
+        w_late = gather_words(C1, placed.tile([P, C1], U32, name="w_late", offset=22 * KIB + 128, align_bytes=64))
+        late_sums = {}
+        for u in range(2):
+            for e in (2, 3):
+                words = w_late[:, e * C2 - C1 : (e + 1) * C2 - C1]
+                late_sums[e, u] = first_product(e * C2, words, range(2 * u, 2 * u + 2), 4 + 2 * u + e % 2)
+        slope = {1: take_slope(a_late, "slope_late"), 0: take_slope(a_first, "slope_first")}
+        win = {(0, 3): placed.tile([P, T], F32, name="win03", offset=9 * KIB, align_bytes=64)}
+        scatter_z(scatter_on_vector, 0, 3, 0, C2)
+        for u in range(2):
+            tile = placed.tile([P, 2, C1], F32, name="z_late%d" % u, offset=(13 + 4 * u) * KIB, align_bytes=64)
+            for e in (2, 3):
+                columns = slice(e * C2 - C1, (e + 1) * C2 - C1)
+                times_gate(tile[:, :, columns], late_sums[e, u], gate_late[:, columns])
+            for n in range(2):
+                z[1, 2 * u + n] = tile[:, n, :]
+
+        for f, t in ((0, 0), (0, 1), (0, 2), (1, 0), (1, 1), (1, 3)):
             win[f, t] = keep.tile([P, T], F32, name="win%d%d" % (f, t), align_bytes=64)
-        da = [placed.tile([P, C1, PACK], BF16, name="da0", offset=half, align_bytes=64)]
-        scatter_z(scatter_on_scalar, 0, 0, 0, SHORT)
-        scatter_z(scatter_on_scalar, 0, 1, 0, SHORT)
-        scatter_z(scatter_on_scalar, 0, 0, SHORT, C1)
-        mask_plane(0, 0)
-        take_slope(placed.tile([P, PACK, C1], BF16, name="slope_late", offset=4 * half, align_bytes=64), a_late, 1, range(0, 4))
-        take_slope(placed.tile([P, 3, C1], BF16, name="slope_rest", offset=26 * KIB, align_bytes=64), a_rest, 0, range(1, 4))
-        scatter_z(scatter_on_scalar, 0, 2, 0, SHORT)
-        for t in (1, 2):
+        da = [placed.tile([P, C1, PACK], BF16, name="da0", offset=2 * KIB, align_bytes=64)]
+        for t in range(3):
+            scatter_z(scatter_on_scalar, 0, t, 0, SHORT)
+        for t in range(3):
             scatter_z(scatter_on_scalar, 0, t, SHORT, C1)
             mask_plane(0, t)
-
-        z.append(placed.tile([P, PACK, C1], F32, name="z1", offset=14 * KIB, align_bytes=64))
-        first_product(2, range(0, 2), 4)
-        win[0, 3] = reuse.tile([P, T], F32, name="win03", tag="a_rest", align_bytes=64)
-        scatter_z(scatter_on_vector, 0, 3, 0, C1)
+        scatter_z(scatter_on_scalar, 0, 3, C2, C1)
         mask_plane(0, 3)
-        for e, planes, n in ((3, range(0, 2), 5), (2, range(2, 4), 6), (3, range(2, 4), 7)):
-            first_product(e, planes, n)
-        for t, first, last in ((0, 0, C2), (1, 0, SHORT), (0, C2, C1), (1, SHORT, C1), (3, 0, C2), (3, C2, C1)):
-            scatter_z(scatter_on_scalar, 1, t, first, last)
 
+        scatter_z(scatter_on_vector, 1, 0, 0, C1)
+        for t in (1, 3):
+            for first in (0, C2):
+                scatter_z(scatter_on_scalar, 1, t, first, first + C2)
         low, high = second_product(0, 0, C1, (0, 1))
         win[1, 2] = placed.tile([P, T], F32, name="win12", offset=0, align_bytes=64)
-        da.append(placed.tile([P, C1, PACK], BF16, name="da1", offset=2 * half, align_bytes=64))
+        da.append(placed.tile([P, C1, PACK], BF16, name="da1", offset=4 * KIB, align_bytes=64))
         scatter_z(scatter_on_vector, 1, 2, 0, C1)
         for t in range(PACK):
             mask_plane(1, t)
@@ -245,7 +250,7 @@ def tile_moe_hib_relu_kernel(
 
         out_low = keep.tile([P, T], F32, name="out_low", align_bytes=64)
         out_high = keep.tile([P, T], F32, name="out_high", align_bytes=64)
-        dx_high = leave_psum(nc.vector.tensor_copy, high[:], "dx0_high")
+        dx_high = leave_psum(nc.scalar.copy, high[:], "dx0_high")
         dx_low = leave_psum(nc.vector.tensor_copy, low[:], "dx0_low")
         for first in (0, C2):
             scatter_on_scalar(out_high, offs_sb, first, dx_high[:, first : first + C2])

@@ -48,14 +48,14 @@ def tile_moe_hib_relu_kernel(
         dy_s = keep.tile([P, T], U8, name="dy_s", align_bytes=64)
         wet_early = keep.tile([P, E // G, 2 * H], U8, name="wet_early", align_bytes=64)
         wet_late = keep.tile([P, E // G, 2 * H], U8, name="wet_late", align_bytes=64)
-        wet_s = keep.tile([P, E, H], U8, name="wet_s", align_bytes=64)
+        wet_s = placed.tile([P, E, H], U8, name="wet_s", offset=32 * KIB, align_bytes=64)
         wgt_w = keep.tile([P, G, K], I32, name="wgt_w", align_bytes=64)
         wgt_s = keep.tile([P, G, K], U8, name="wgt_s", align_bytes=64)
-        gate_lead = reuse.tile([P, SHORT], F32, name="gate_lead", tag="gate_lead", align_bytes=64)
-        gate_rest = placed.tile([P, C1], F32, name="gate_rest", offset=24 * KIB, align_bytes=64)
+        gate_lead = reuse.tile([P, C2], F32, name="gate_lead", tag="gate_lead", align_bytes=64)
+        gate_rest = reuse.tile([P, C1], F32, name="gate_rest", tag="gate_rest", align_bytes=64)
         gate_late = keep.tile([P, C1], F32, name="gate_late", align_bytes=64)
-        a_first = placed.tile([P, PACK, C1], F32, name="a_first", offset=12 * KIB, align_bytes=64)
-        a_late = keep.tile([P, PACK, C1], F32, name="a_late", align_bytes=64)
+        a_first = keep.tile([P, PACK, C1], F32, name="a_first", align_bytes=64)
+        a_late = placed.tile([P, PACK, C1], F32, name="a_late", offset=5 * KIB, align_bytes=64)
 
         def zero_on_vector(words):
             last = words.shape[1] - 1
@@ -82,11 +82,11 @@ def tile_moe_hib_relu_kernel(
         nc.sync.dma_start(wet_early[:].bitcast(I32), wet_src[:, 0:2, :])
         nc.sync.dma_start(dy_w[:], dy_words[0].rearrange("p n d -> p (n d)").bitcast(I32))
         nc.sync.dma_start(offs2_sb[:], offs2)
-        nc.sync.dma_start(gate_lead[:], gate[:, 0:SHORT])
+        nc.sync.dma_start(gate_lead[:], gate[:, 0:C2])
         nc.sync.dma_start(gate_rest[:], gate[:, 0:C1])
         nc.sync.dma_start(wet_late[:].bitcast(I32), wet_src[:, 2:4, :])
-        nc.sync.dma_start(a_late[:], a_src[:, :, C1:T])
         nc.sync.dma_start(a_first[:], a_src[:, :, 0:C1])
+        nc.sync.dma_start(a_late[:], a_src[:, :, C1:T])
         nc.sync.dma_start(gate_late[:], gate[:, C1:T])
         nc.sync.dma_start(wgt_w[:], wgt_words.rearrange("f s p k d -> p (f s) (k d)").bitcast(I32))
         load_scale_rows(wgt_s, wgt_scales.rearrange("f s r k -> r (f s) k").bitcast(I32))
@@ -97,9 +97,8 @@ def tile_moe_hib_relu_kernel(
             nc.vector.tensor_copy(tile[:], dy_s[:].indirect(entries(dst_sb, f * C1, C1)))
             return tile
 
-        def gather_words(first, tile):
-            nc.vector.tensor_copy(tile[:], dy_w[:].bitcast(U32).indirect(entries(dst_sb, first, tile.shape[1])))
-            return tile
+        def gather_words(first, into):
+            nc.vector.tensor_copy(into, dy_w[:].bitcast(U32).indirect(entries(dst_sb, first, into.shape[1])))
 
         plane_w, plane_s = {}, {}
 
@@ -117,12 +116,12 @@ def tile_moe_hib_relu_kernel(
                 for t in range(PACK):
                     plane_w[E // G + m, t] = tile[:, m, t, :]
 
-        def order_scales(experts, planes, tile):
-            source = wet_s[:].rearrange("p e (m t) -> p e t m", t=PACK)
-            nc.vector.tensor_copy(tile[:], source[:, experts.start : experts.stop, planes.start : planes.stop, :])
-            for m, e in enumerate(experts):
-                for n, t in enumerate(planes):
-                    plane_s[e, t] = tile[:, m, n, :]
+        def order_scales(e, planes):
+            tile = keep.tile([P, len(planes), P], U8, name="plane_s%d_%d" % (e, planes.start), align_bytes=64)
+            source = wet_s[:, e, :].rearrange("p (m t) -> p t m", t=PACK)
+            nc.gpsimd.tensor_copy(tile[:], source[:, planes.start : planes.stop, :])
+            for n, t in enumerate(planes):
+                plane_s[e, t] = tile[:, n, :]
 
         def bank(n, shape):
             return psum.tile(shape, F32, name="bank", tag="bank%d" % n)
@@ -155,8 +154,8 @@ def tile_moe_hib_relu_kernel(
         def scatter_z(scatter, f, t, first, last):
             scatter(win[f, t], offs2_sb, f * C1 + first, z[f, t][:, first:last])
 
-        def take_slope(source, name):
-            tile = keep.tile([P, PACK, C1], BF16, name=name, align_bytes=64)
+        def take_slope(source, name, offset):
+            tile = placed.tile([P, PACK, C1], BF16, name=name, offset=offset, align_bytes=64)
             nc.vector.tensor_scalar(tile[:], source[:], 0.0, None, ALU.is_gt)
             return tile
 
@@ -165,7 +164,7 @@ def tile_moe_hib_relu_kernel(
 
         def second_product(f, first, last, banks):
             count = last - first
-            da_w = keep.tile([P, count], U32, name="da_w%d_%d" % (f, first), align_bytes=64)
+            da_w = reuse.tile([P, count], U32, name="da_w", tag="da_w%d_%d" % (f, first), align_bytes=64)
             da_s = keep.tile([P, count], U8, name="da_s%d_%d" % (f, first), align_bytes=64)
             values = da[f][:, first:last, :].rearrange("p j t -> p (j t)")
             nc.vector.quantize_mx(out=da_w[:].bitcast(FP8X4), scales=da_s[:], in_=values)
@@ -188,59 +187,70 @@ def tile_moe_hib_relu_kernel(
         order_words(0, range(0, 1), "lead_w")
         order_words(0, range(1, 4), "first_w")
         order_words(1, range(0, 4), "plane_w1")
-        z_first = keep.tile([P, PACK, C1], F32, name="z_first", align_bytes=64)
+        z_first = reuse.tile([P, PACK, C1], F32, name="z_first", tag="z_first", align_bytes=64)
         z = {(0, t): z_first[:, t, :] for t in range(PACK)}
         g_s = [gather_scales(f) for f in range(G)]
-        order_scales(range(0, 1), range(0, 4), keep.tile([P, 1, PACK, P], U8, name="first_s", align_bytes=64))
-        w_lead = gather_words(0, keep.tile([P, SHORT], U32, name="w_lead", align_bytes=64))
-        w_rest = gather_words(SHORT, keep.tile([P, C1 - SHORT], U32, name="w_rest", align_bytes=64))
-        times_gate(z_first[:, 0:1, 0:SHORT], first_product(0, w_lead[:], range(0, 1), 0), gate_lead[:])
-        order_scales(range(1, 2), range(0, 4), reuse.tile([P, 1, PACK, P], U8, name="second_s", tag="gate_lead", align_bytes=64))
-        times_gate(z_first[:, 1:4, 0:SHORT], first_product(0, w_lead[:], range(1, 4), 1), gate_rest[:, 0:SHORT])
-        times_gate(z_first[:, :, SHORT:C2], first_product(SHORT, w_rest[:, 0:SHORT], range(0, 4), 2), gate_rest[:, SHORT:C2])
-        for planes, n in ((range(0, 2), 3), (range(2, 4), 0)):
-            acc = first_product(C2, w_rest[:, SHORT:], planes, n)
-            times_gate(z_first[:, planes.start : planes.stop, C2:C1], acc, gate_rest[:, C2:C1])
+        for e, planes in ((0, range(0, 1)), (0, range(1, 2)), (1, range(0, 2)), (0, range(2, 4)), (1, range(2, 4))):
+            order_scales(e, planes)
+        for e in range(E // G, E):
+            order_scales(e, range(0, PACK))
+        w_first = keep.tile([P, C1], U32, name="w_first", align_bytes=64)
+        gather_words(0, w_first[:, 0:SHORT])
+        gather_words(SHORT, w_first[:, SHORT:C1])
+        for first, last, planes, n_bank, weights in (
+            (0, SHORT, range(0, 1), 0, gate_lead),
+            (0, C2, range(1, 2), 1, gate_lead),
+            (SHORT, C2, range(0, 1), 2, gate_lead),
+            (C2, C1, range(0, 2), 3, gate_rest),
+            (0, C2, range(2, 4), 4, gate_rest),
+            (C2, C1, range(2, 4), 5, gate_rest),
+        ):
+            acc = first_product(first, w_first[:, first:last], planes, n_bank)
+            times_gate(z_first[:, planes.start : planes.stop, first:last], acc, weights[:, first:last])
 
-        order_late_words(placed.tile([P, E // G, PACK, 2 * P], U8, name="late_w", offset=25 * KIB + 512, align_bytes=64))
-        order_scales(range(2, 4), range(0, 4), placed.tile([P, E // G, PACK, P], U8, name="late_s", offset=24 * KIB + 256, align_bytes=64))
-        w_late = gather_words(C1, placed.tile([P, C1], U32, name="w_late", offset=22 * KIB + 128, align_bytes=64))
+        order_late_words(placed.tile([P, E // G, PACK, 2 * P], U8, name="late_w", offset=31 * KIB, align_bytes=64))
+        w_late = reuse.tile([P, C1], U32, name="w_late", tag="gate_lead", align_bytes=64)
+        gather_words(C1, w_late[:])
+        slope = {0: take_slope(a_first, "slope_first", 33 * KIB)}
         late_sums = {}
         for u in range(2):
             for e in (2, 3):
                 words = w_late[:, e * C2 - C1 : (e + 1) * C2 - C1]
-                late_sums[e, u] = first_product(e * C2, words, range(2 * u, 2 * u + 2), 4 + 2 * u + e % 2)
-        slope = {1: take_slope(a_late, "slope_late"), 0: take_slope(a_first, "slope_first")}
-        win = {(0, 3): placed.tile([P, T], F32, name="win03", offset=9 * KIB, align_bytes=64)}
-        scatter_z(scatter_on_vector, 0, 3, 0, C2)
-        for u in range(2):
-            tile = placed.tile([P, 2, C1], F32, name="z_late%d" % u, offset=(13 + 4 * u) * KIB, align_bytes=64)
+                late_sums[e, u] = first_product(e * C2, words, range(2 * u, 2 * u + 2), (6 + 2 * u + e % 2) % 8)
+        slope[1] = take_slope(a_late, "slope_late", 37 * KIB)
+        win = {(0, 3): placed.tile([P, T], F32, name="win03", offset=12 * KIB, align_bytes=64)}
+        scatter_z(scatter_on_vector, 0, 3, 0, C1)
+
+        def late_pair(u, tile):
             for e in (2, 3):
                 columns = slice(e * C2 - C1, (e + 1) * C2 - C1)
                 times_gate(tile[:, :, columns], late_sums[e, u], gate_late[:, columns])
             for n in range(2):
                 z[1, 2 * u + n] = tile[:, n, :]
 
-        for f, t in ((0, 0), (0, 1), (0, 2), (1, 0), (1, 1), (1, 3)):
-            win[f, t] = keep.tile([P, T], F32, name="win%d%d" % (f, t), align_bytes=64)
-        da = [placed.tile([P, C1, PACK], BF16, name="da0", offset=2 * KIB, align_bytes=64)]
-        for t in range(3):
-            scatter_z(scatter_on_scalar, 0, t, 0, SHORT)
-        for t in range(3):
-            scatter_z(scatter_on_scalar, 0, t, SHORT, C1)
-            mask_plane(0, t)
-        scatter_z(scatter_on_scalar, 0, 3, C2, C1)
-        mask_plane(0, 3)
+        late_pair(0, placed.tile([P, 2, C1], F32, name="z_late0", offset=8 * KIB, align_bytes=64))
 
-        scatter_z(scatter_on_vector, 1, 0, 0, C1)
-        for t in (1, 3):
-            for first in (0, C2):
-                scatter_z(scatter_on_scalar, 1, t, first, first + C2)
-        low, high = second_product(0, 0, C1, (0, 1))
-        win[1, 2] = placed.tile([P, T], F32, name="win12", offset=0, align_bytes=64)
+        for f, t in ((0, 0), (0, 1), (1, 0), (1, 2)):
+            win[f, t] = keep.tile([P, T], F32, name="win%d%d" % (f, t), align_bytes=64)
+        win[0, 2] = reuse.tile([P, T], F32, name="win02", tag="gate_rest", align_bytes=64)
+        da = [placed.tile([P, C1, PACK], BF16, name="da0", offset=2 * KIB, align_bytes=64)]
+        for t, first, last in ((0, 0, SHORT), (1, 0, C2), (0, SHORT, C1), (1, C2, C1), (2, 0, C2), (2, C2, C1)):
+            scatter_z(scatter_on_scalar, 0, t, first, last)
+        for t in (0, 1, 3, 2):
+            mask_plane(0, t)
+
+        late_pair(1, reuse.tile([P, 2, C1], F32, name="z_late1", tag="z_first", align_bytes=64))
+        scatter_z(scatter_on_vector, 1, 2, 0, C2)
+        for t, first in ((0, 0), (0, C2), (2, C2)):
+            scatter_z(scatter_on_scalar, 1, t, first, first + C2)
+        low, high = second_product(0, 0, C1, (2, 3))
+        win[1, 3] = placed.tile([P, T], F32, name="win13", offset=0, align_bytes=64)
         da.append(placed.tile([P, C1, PACK], BF16, name="da1", offset=4 * KIB, align_bytes=64))
-        scatter_z(scatter_on_vector, 1, 2, 0, C1)
-        for t in range(PACK):
+        scatter_z(scatter_on_vector, 1, 3, 0, C1)
+        win[1, 1] = reuse.tile([P, T], F32, name="win11", tag="da_w0_0", align_bytes=64)
+        for first in (0, C2):
+            scatter_z(scatter_on_scalar, 1, 1, first, first + C2)
+        for t in (0, 2, 3, 1):
             mask_plane(1, t)
 
         def leave_psum(copy, acc, name):
@@ -256,7 +266,7 @@ def tile_moe_hib_relu_kernel(
             scatter_on_scalar(out_high, offs_sb, first, dx_high[:, first : first + C2])
         scatter_on_vector(out_low, offs_sb, 0, dx_low[:])
 
-        late = [second_product(1, 0, C2, (2, 3)), second_product(1, C2, C1, (4, 5))]
+        late = [second_product(1, 0, C2, (4, 5)), second_product(1, C2, C1, (6, 7))]
         for place, (low, high) in enumerate(late):
             first = C1 + place * C2
             scatter_on_vector(out_low, offs_sb, first, leave_psum(nc.vector.tensor_copy, low[:], "dx1_low%d" % place)[:])

@@ -46,9 +46,9 @@ def tile_moe_hib_relu_kernel(
         offs_sb = keep.tile([P, T // PER_COL], U16, name="offs_sb")
         dy_w = keep.tile([P, T], I32, name="dy_w", align_bytes=64)
         dy_s = keep.tile([P, T], U8, name="dy_s", align_bytes=64)
-        wet_early = keep.tile([P, E // G, 2 * H], U8, name="wet_early", align_bytes=64)
-        wet_late = keep.tile([P, E // G, 2 * H], U8, name="wet_late", align_bytes=64)
-        wet_s = placed.tile([P, E, H], U8, name="wet_s", offset=32 * KIB, align_bytes=64)
+        wet_early = [keep.tile([P, 2 * H], U8, name="wet_w%d" % e, align_bytes=64) for e in range(E // G)]
+        wet_late = reuse.tile([P, E // G, 2 * H], U8, name="wet_late", tag="wet_late", align_bytes=64)
+        wet_s = keep.tile([P, E, H], U8, name="wet_s", align_bytes=64)
         wgt_w = keep.tile([P, G, K], I32, name="wgt_w", align_bytes=64)
         wgt_s = keep.tile([P, G, K], U8, name="wgt_s", align_bytes=64)
         gate_lead = reuse.tile([P, C2], F32, name="gate_lead", tag="gate_lead", align_bytes=64)
@@ -79,8 +79,9 @@ def tile_moe_hib_relu_kernel(
             queue = nc.sync if q < 3 else nc.scalar
             queue.dma_start(dy_s[32 * q : 32 * q + 4, :].bitcast(I32), dy_scales[0, 4 * q : 4 * q + 4, :].bitcast(I32))
         load_scale_rows(wet_s, wet_scales.rearrange("e s r h -> r (e s) h").bitcast(I32))
-        nc.sync.dma_start(wet_early[:].bitcast(I32), wet_src[:, 0:2, :])
         nc.sync.dma_start(dy_w[:], dy_words[0].rearrange("p n d -> p (n d)").bitcast(I32))
+        for e in range(E // G):
+            nc.sync.dma_start(wet_early[e][:].bitcast(I32), wet_src[:, e, :])
         nc.sync.dma_start(offs2_sb[:], offs2)
         nc.sync.dma_start(gate_lead[:], gate[:, 0:C2])
         nc.sync.dma_start(gate_rest[:], gate[:, 0:C1])
@@ -104,17 +105,16 @@ def tile_moe_hib_relu_kernel(
 
         def order_words(e, planes, tag):
             tile = reuse.tile([P, len(planes), 2 * P], U8, name="plane_w", tag=tag, align_bytes=64)
-            source = wet_early[:, e, :].bitcast(U16).rearrange("p (m t) -> p t m", t=PACK)
+            source = wet_early[e][:].bitcast(U16).rearrange("p (m t) -> p t m", t=PACK)
             nc.scalar.copy(tile[:].bitcast(U16), source[:, planes.start : planes.stop, :])
             for n, t in enumerate(planes):
                 plane_w[e, t] = tile[:, n, :]
 
-        def order_late_words(tile):
-            source = wet_late[:].bitcast(U16).rearrange("p e (m t) -> p e t m", t=PACK)
-            nc.vector.tensor_copy(tile[:].bitcast(U16), source)
-            for m in range(E // G):
-                for t in range(PACK):
-                    plane_w[E // G + m, t] = tile[:, m, t, :]
+        def order_late_words(m):
+            tile = keep.tile([P, PACK, P, 2], U8, name="late_w%d" % m, align_bytes=64)
+            nc.gpsimd.tensor_copy(tile[:], wet_late[:, m, :].rearrange("p (m t b) -> p t m b", t=PACK, b=2))
+            for t in range(PACK):
+                plane_w[E // G + m, t] = tile[:, t, :, :].rearrange("p m b -> p (m b)")
 
         def order_scales(e, planes):
             tile = keep.tile([P, len(planes), P], U8, name="plane_s%d_%d" % (e, planes.start), align_bytes=64)
@@ -154,8 +154,8 @@ def tile_moe_hib_relu_kernel(
         def scatter_z(scatter, f, t, first, last):
             scatter(win[f, t], offs2_sb, f * C1 + first, z[f, t][:, first:last])
 
-        def take_slope(source, name, offset):
-            tile = placed.tile([P, PACK, C1], BF16, name=name, offset=offset, align_bytes=64)
+        def take_slope(source, tag):
+            tile = reuse.tile([P, PACK, C1], BF16, name="slope", tag=tag, align_bytes=64)
             nc.vector.tensor_scalar(tile[:], source[:], 0.0, None, ALU.is_gt)
             return tile
 
@@ -208,16 +208,17 @@ def tile_moe_hib_relu_kernel(
             acc = first_product(first, w_first[:, first:last], planes, n_bank)
             times_gate(z_first[:, planes.start : planes.stop, first:last], acc, weights[:, first:last])
 
-        order_late_words(placed.tile([P, E // G, PACK, 2 * P], U8, name="late_w", offset=31 * KIB, align_bytes=64))
+        for m in range(E // G):
+            order_late_words(m)
         w_late = reuse.tile([P, C1], U32, name="w_late", tag="gate_lead", align_bytes=64)
         gather_words(C1, w_late[:])
-        slope = {0: take_slope(a_first, "slope_first", 33 * KIB)}
+        slope = {0: take_slope(a_first, "wet_late")}
         late_sums = {}
         for u in range(2):
             for e in (2, 3):
                 words = w_late[:, e * C2 - C1 : (e + 1) * C2 - C1]
                 late_sums[e, u] = first_product(e * C2, words, range(2 * u, 2 * u + 2), (6 + 2 * u + e % 2) % 8)
-        slope[1] = take_slope(a_late, "slope_late", 37 * KIB)
+        slope[1] = take_slope(a_late, "slope_late")
         win = {(0, 3): placed.tile([P, T], F32, name="win03", offset=12 * KIB, align_bytes=64)}
         scatter_z(scatter_on_vector, 0, 3, 0, C1)
 
@@ -260,7 +261,7 @@ def tile_moe_hib_relu_kernel(
 
         out_low = keep.tile([P, T], F32, name="out_low", align_bytes=64)
         out_high = keep.tile([P, T], F32, name="out_high", align_bytes=64)
-        dx_high = leave_psum(nc.scalar.copy, high[:], "dx0_high")
+        dx_high = leave_psum(nc.vector.tensor_copy, high[:], "dx0_high")
         dx_low = leave_psum(nc.vector.tensor_copy, low[:], "dx0_low")
         for first in (0, C2):
             scatter_on_scalar(out_high, offs_sb, first, dx_high[:, first : first + C2])
@@ -269,7 +270,8 @@ def tile_moe_hib_relu_kernel(
         late = [second_product(1, 0, C2, (4, 5)), second_product(1, C2, C1, (6, 7))]
         for place, (low, high) in enumerate(late):
             first = C1 + place * C2
-            scatter_on_vector(out_low, offs_sb, first, leave_psum(nc.vector.tensor_copy, low[:], "dx1_low%d" % place)[:])
+            copy_low = nc.vector.tensor_copy if place == 0 else nc.scalar.copy
+            scatter_on_vector(out_low, offs_sb, first, leave_psum(copy_low, low[:], "dx1_low%d" % place)[:])
             scatter_on_scalar(out_high, offs_sb, first, leave_psum(nc.scalar.copy, high[:], "dx1_high%d" % place)[:])
         nc.sync.dma_start(out[0:P, :], out_low[:])
         nc.sync.dma_start(out[P : 2 * P, :], out_high[:])

@@ -20,6 +20,7 @@ P = 128
 PACK = 4
 PER_COL = 16
 SHORT = 128
+FILL = 256
 KIB = 1024
 
 
@@ -46,13 +47,12 @@ def tile_moe_hib_relu_kernel(
         offs_sb = keep.tile([P, T // PER_COL], U16, name="offs_sb")
         dy_w = keep.tile([P, T], I32, name="dy_w", align_bytes=64)
         dy_s = keep.tile([P, T], U8, name="dy_s", align_bytes=64)
-        wet_early = [keep.tile([P, 2 * H], U8, name="wet_w%d" % e, align_bytes=64) for e in range(E // G)]
-        wet_late = reuse.tile([P, E // G, 2 * H], U8, name="wet_late", tag="wet_late", align_bytes=64)
+        wet_w = [reuse.tile([P, 2 * H], U8, name="wet_w", tag="wet_w%d" % e, align_bytes=64) for e in range(E)]
         wet_s = keep.tile([P, E, H], U8, name="wet_s", align_bytes=64)
         wgt_w = keep.tile([P, G, K], I32, name="wgt_w", align_bytes=64)
         wgt_s = keep.tile([P, G, K], U8, name="wgt_s", align_bytes=64)
         gate_lead = reuse.tile([P, C2], F32, name="gate_lead", tag="gate_lead", align_bytes=64)
-        gate_rest = reuse.tile([P, C1], F32, name="gate_rest", tag="gate_rest", align_bytes=64)
+        gate_rest = reuse.tile([P, C2], F32, name="gate_rest", tag="gate_rest", align_bytes=64)
         gate_late = keep.tile([P, C1], F32, name="gate_late", align_bytes=64)
         a_first = keep.tile([P, PACK, C1], F32, name="a_first", align_bytes=64)
         a_late = placed.tile([P, PACK, C1], F32, name="a_late", offset=5 * KIB, align_bytes=64)
@@ -62,15 +62,14 @@ def tile_moe_hib_relu_kernel(
             nc.vector.memset(words[:, 0:last], 0)
             nc.vector.memset(words[:, last : last + 1], 0)
 
-        nc.gpsimd.memset(dy_s[:].bitcast(I32)[:, 0:P], 0)
-        zero_on_vector(dy_s[:].bitcast(I32)[:, P : 2 * P])
-        nc.gpsimd.memset(words_of(wet_s)[:, 0:P], 0)
-        zero_on_vector(words_of(wet_s)[:, P : E * P])
-        nc.gpsimd.memset(words_of(wgt_s), 0)
+        nc.gpsimd.memset(words_of(wet_s)[96:P, :], 0)
+        zero_on_vector(dy_s[:].bitcast(I32))
+        zero_on_vector(words_of(wet_s)[0:96, :])
 
-        def load_scale_rows(plane, rows):
+        def load_scale_rows(plane, rows, last_queue):
             for q in range(4):
-                nc.sync.dma_start(plane[32 * q : 32 * q + 4, :, :].bitcast(I32), rows[4 * q : 4 * q + 4, :, :])
+                queue = nc.sync if q < 3 else last_queue
+                queue.dma_start(plane[32 * q : 32 * q + 4, :, :].bitcast(I32), rows[4 * q : 4 * q + 4, :, :])
 
         a_src = a.rearrange("(p t) j -> p t j", t=PACK)
         wet_src = wet_words.rearrange("e s p c -> p (e s) c").bitcast(I32)
@@ -78,19 +77,20 @@ def tile_moe_hib_relu_kernel(
         for q in range(4):
             queue = nc.sync if q < 3 else nc.scalar
             queue.dma_start(dy_s[32 * q : 32 * q + 4, :].bitcast(I32), dy_scales[0, 4 * q : 4 * q + 4, :].bitcast(I32))
-        load_scale_rows(wet_s, wet_scales.rearrange("e s r h -> r (e s) h").bitcast(I32))
+        load_scale_rows(wet_s, wet_scales.rearrange("e s r h -> r (e s) h").bitcast(I32), nc.gpsimd)
+        nc.gpsimd.memset(words_of(wgt_s), 0)
         nc.sync.dma_start(dy_w[:], dy_words[0].rearrange("p n d -> p (n d)").bitcast(I32))
-        for e in range(E // G):
-            nc.sync.dma_start(wet_early[e][:].bitcast(I32), wet_src[:, e, :])
+        for e in (0, 1, 3):
+            nc.sync.dma_start(wet_w[e][:].bitcast(I32), wet_src[:, e, :])
         nc.sync.dma_start(offs2_sb[:], offs2)
         nc.sync.dma_start(gate_lead[:], gate[:, 0:C2])
-        nc.sync.dma_start(gate_rest[:], gate[:, 0:C1])
-        nc.sync.dma_start(wet_late[:].bitcast(I32), wet_src[:, 2:4, :])
+        nc.sync.dma_start(gate_rest[:], gate[:, C2:C1])
+        nc.sync.dma_start(wet_w[2][:].bitcast(I32), wet_src[:, 2, :])
         nc.sync.dma_start(a_first[:], a_src[:, :, 0:C1])
         nc.sync.dma_start(a_late[:], a_src[:, :, C1:T])
         nc.sync.dma_start(gate_late[:], gate[:, C1:T])
         nc.sync.dma_start(wgt_w[:], wgt_words.rearrange("f s p k d -> p (f s) (k d)").bitcast(I32))
-        load_scale_rows(wgt_s, wgt_scales.rearrange("f s r k -> r (f s) k").bitcast(I32))
+        load_scale_rows(wgt_s, wgt_scales.rearrange("f s r k -> r (f s) k").bitcast(I32), nc.sync)
         nc.sync.dma_start(offs_sb[:], offs)
 
         def gather_scales(f):
@@ -105,16 +105,16 @@ def tile_moe_hib_relu_kernel(
 
         def order_words(e, planes, tag):
             tile = reuse.tile([P, len(planes), 2 * P], U8, name="plane_w", tag=tag, align_bytes=64)
-            source = wet_early[e][:].bitcast(U16).rearrange("p (m t) -> p t m", t=PACK)
+            source = wet_w[e][:].bitcast(U16).rearrange("p (m t) -> p t m", t=PACK)
             nc.scalar.copy(tile[:].bitcast(U16), source[:, planes.start : planes.stop, :])
             for n, t in enumerate(planes):
                 plane_w[e, t] = tile[:, n, :]
 
-        def order_late_words(m):
-            tile = keep.tile([P, PACK, P, 2], U8, name="late_w%d" % m, align_bytes=64)
-            nc.gpsimd.tensor_copy(tile[:], wet_late[:, m, :].rearrange("p (m t b) -> p t m b", t=PACK, b=2))
+        def order_words_as_bytes(e):
+            tile = keep.tile([P, PACK, P, 2], U8, name="late_w%d" % e, align_bytes=64)
+            nc.gpsimd.tensor_copy(tile[:], wet_w[e][:].rearrange("p (m t b) -> p t m b", t=PACK, b=2))
             for t in range(PACK):
-                plane_w[E // G + m, t] = tile[:, t, :, :].rearrange("p m b -> p (m b)")
+                plane_w[e, t] = tile[:, t, :, :].rearrange("p m b -> p (m b)")
 
         def order_scales(e, planes):
             tile = keep.tile([P, len(planes), P], U8, name="plane_s%d_%d" % (e, planes.start), align_bytes=64)
@@ -187,6 +187,7 @@ def tile_moe_hib_relu_kernel(
         order_words(0, range(0, 1), "lead_w")
         order_words(0, range(1, 4), "first_w")
         order_words(1, range(0, 4), "plane_w1")
+        order_words(3, range(0, 4), "plane_w3")
         z_first = reuse.tile([P, PACK, C1], F32, name="z_first", tag="z_first", align_bytes=64)
         z = {(0, t): z_first[:, t, :] for t in range(PACK)}
         g_s = [gather_scales(f) for f in range(G)]
@@ -196,29 +197,29 @@ def tile_moe_hib_relu_kernel(
             order_scales(e, range(0, PACK))
         w_first = keep.tile([P, C1], U32, name="w_first", align_bytes=64)
         gather_words(0, w_first[:, 0:SHORT])
-        gather_words(SHORT, w_first[:, SHORT:C1])
-        for first, last, planes, n_bank, weights in (
-            (0, SHORT, range(0, 1), 0, gate_lead),
-            (0, C2, range(1, 2), 1, gate_lead),
-            (SHORT, C2, range(0, 1), 2, gate_lead),
-            (C2, C1, range(0, 2), 3, gate_rest),
-            (0, C2, range(2, 4), 4, gate_rest),
-            (C2, C1, range(2, 4), 5, gate_rest),
+        gather_words(SHORT, w_first[:, SHORT:C2])
+        gather_words(C2, w_first[:, C2:C1])
+        for first, last, planes, n_bank in (
+            (0, SHORT, range(0, 1), 0),
+            (0, C2, range(1, 2), 1),
+            (SHORT, C2, range(0, 1), 2),
+            (C2, C1, range(0, 2), 3),
+            (0, C2, range(2, 4), 4),
+            (C2, C1, range(2, 4), 5),
         ):
             acc = first_product(first, w_first[:, first:last], planes, n_bank)
-            times_gate(z_first[:, planes.start : planes.stop, first:last], acc, weights[:, first:last])
+            weights = gate_lead[:, first:last] if first < C2 else gate_rest[:]
+            times_gate(z_first[:, planes.start : planes.stop, first:last], acc, weights)
 
-        for m in range(E // G):
-            order_late_words(m)
+        order_words_as_bytes(2)
         w_late = reuse.tile([P, C1], U32, name="w_late", tag="gate_lead", align_bytes=64)
         gather_words(C1, w_late[:])
-        slope = {0: take_slope(a_first, "wet_late")}
+        slope = {0: take_slope(a_first, "wet_w2"), 1: take_slope(a_late, "slope_late")}
         late_sums = {}
         for u in range(2):
             for e in (2, 3):
                 words = w_late[:, e * C2 - C1 : (e + 1) * C2 - C1]
                 late_sums[e, u] = first_product(e * C2, words, range(2 * u, 2 * u + 2), (6 + 2 * u + e % 2) % 8)
-        slope[1] = take_slope(a_late, "slope_late")
         win = {(0, 3): placed.tile([P, T], F32, name="win03", offset=12 * KIB, align_bytes=64)}
         scatter_z(scatter_on_vector, 0, 3, 0, C1)
 
@@ -241,9 +242,9 @@ def tile_moe_hib_relu_kernel(
             mask_plane(0, t)
 
         late_pair(1, reuse.tile([P, 2, C1], F32, name="z_late1", tag="z_first", align_bytes=64))
-        scatter_z(scatter_on_vector, 1, 2, 0, C2)
-        for t, first in ((0, 0), (0, C2), (2, C2)):
-            scatter_z(scatter_on_scalar, 1, t, first, first + C2)
+        scatter_z(scatter_on_vector, 1, 2, 0, FILL)
+        for t, first, last in ((0, 0, C2), (0, C2, C1), (2, FILL, C1)):
+            scatter_z(scatter_on_scalar, 1, t, first, last)
         low, high = second_product(0, 0, C1, (2, 3))
         win[1, 3] = placed.tile([P, T], F32, name="win13", offset=0, align_bytes=64)
         da.append(placed.tile([P, C1, PACK], BF16, name="da1", offset=4 * KIB, align_bytes=64))
@@ -261,7 +262,7 @@ def tile_moe_hib_relu_kernel(
 
         out_low = keep.tile([P, T], F32, name="out_low", align_bytes=64)
         out_high = keep.tile([P, T], F32, name="out_high", align_bytes=64)
-        dx_high = leave_psum(nc.vector.tensor_copy, high[:], "dx0_high")
+        dx_high = leave_psum(nc.scalar.copy, high[:], "dx0_high")
         dx_low = leave_psum(nc.vector.tensor_copy, low[:], "dx0_low")
         for first in (0, C2):
             scatter_on_scalar(out_high, offs_sb, first, dx_high[:, first : first + C2])

@@ -47,12 +47,13 @@ def tile_moe_hib_relu_kernel(
         offs_sb = keep.tile([P, T // PER_COL], U16, name="offs_sb")
         dy_w = keep.tile([P, T], I32, name="dy_w", align_bytes=64)
         dy_s = keep.tile([P, T], U8, name="dy_s", align_bytes=64)
-        wet_w = [reuse.tile([P, 2 * H], U8, name="wet_w", tag="wet_w%d" % e, align_bytes=64) for e in range(E)]
+        wet_w = [keep.tile([P, 2 * H], U8, name="wet_w%d" % e, align_bytes=64) for e in range(E // G)]
+        wet_late = reuse.tile([P, E // G, 2 * H], U8, name="wet_late", tag="wet_late", align_bytes=64)
         wet_s = keep.tile([P, E, H], U8, name="wet_s", align_bytes=64)
         wgt_w = keep.tile([P, G, K], I32, name="wgt_w", align_bytes=64)
         wgt_s = keep.tile([P, G, K], U8, name="wgt_s", align_bytes=64)
-        gate_lead = reuse.tile([P, C2], F32, name="gate_lead", tag="gate_lead", align_bytes=64)
-        gate_rest = reuse.tile([P, C2], F32, name="gate_rest", tag="gate_rest", align_bytes=64)
+        gate_lead = keep.tile([P, C2], F32, name="gate_lead", align_bytes=64)
+        gate_rest = keep.tile([P, C2], F32, name="gate_rest", align_bytes=64)
         gate_late = keep.tile([P, C1], F32, name="gate_late", align_bytes=64)
         a_first = keep.tile([P, PACK, C1], F32, name="a_first", align_bytes=64)
         a_late = placed.tile([P, PACK, C1], F32, name="a_late", offset=5 * KIB, align_bytes=64)
@@ -62,14 +63,15 @@ def tile_moe_hib_relu_kernel(
             nc.vector.memset(words[:, 0:last], 0)
             nc.vector.memset(words[:, last : last + 1], 0)
 
-        nc.gpsimd.memset(words_of(wet_s)[96:P, :], 0)
-        zero_on_vector(dy_s[:].bitcast(I32))
-        zero_on_vector(words_of(wet_s)[0:96, :])
+        nc.gpsimd.memset(dy_s[:].bitcast(I32)[:, 0:P], 0)
+        zero_on_vector(dy_s[:].bitcast(I32)[:, P : 2 * P])
+        nc.gpsimd.memset(words_of(wet_s)[:, 0:P], 0)
+        zero_on_vector(words_of(wet_s)[:, P : E * P])
+        nc.gpsimd.memset(words_of(wgt_s), 0)
 
-        def load_scale_rows(plane, rows, last_queue):
+        def load_scale_rows(plane, rows):
             for q in range(4):
-                queue = nc.sync if q < 3 else last_queue
-                queue.dma_start(plane[32 * q : 32 * q + 4, :, :].bitcast(I32), rows[4 * q : 4 * q + 4, :, :])
+                nc.sync.dma_start(plane[32 * q : 32 * q + 4, :, :].bitcast(I32), rows[4 * q : 4 * q + 4, :, :])
 
         a_src = a.rearrange("(p t) j -> p t j", t=PACK)
         wet_src = wet_words.rearrange("e s p c -> p (e s) c").bitcast(I32)
@@ -77,20 +79,19 @@ def tile_moe_hib_relu_kernel(
         for q in range(4):
             queue = nc.sync if q < 3 else nc.scalar
             queue.dma_start(dy_s[32 * q : 32 * q + 4, :].bitcast(I32), dy_scales[0, 4 * q : 4 * q + 4, :].bitcast(I32))
-        load_scale_rows(wet_s, wet_scales.rearrange("e s r h -> r (e s) h").bitcast(I32), nc.gpsimd)
-        nc.gpsimd.memset(words_of(wgt_s), 0)
+        load_scale_rows(wet_s, wet_scales.rearrange("e s r h -> r (e s) h").bitcast(I32))
         nc.sync.dma_start(dy_w[:], dy_words[0].rearrange("p n d -> p (n d)").bitcast(I32))
-        for e in (0, 1, 3):
+        for e in (0, 1):
             nc.sync.dma_start(wet_w[e][:].bitcast(I32), wet_src[:, e, :])
         nc.sync.dma_start(offs2_sb[:], offs2)
         nc.sync.dma_start(gate_lead[:], gate[:, 0:C2])
         nc.sync.dma_start(gate_rest[:], gate[:, C2:C1])
-        nc.sync.dma_start(wet_w[2][:].bitcast(I32), wet_src[:, 2, :])
+        nc.sync.dma_start(wet_late[:].bitcast(I32), wet_src[:, 2:4, :])
         nc.sync.dma_start(a_first[:], a_src[:, :, 0:C1])
         nc.sync.dma_start(a_late[:], a_src[:, :, C1:T])
         nc.sync.dma_start(gate_late[:], gate[:, C1:T])
         nc.sync.dma_start(wgt_w[:], wgt_words.rearrange("f s p k d -> p (f s) (k d)").bitcast(I32))
-        load_scale_rows(wgt_s, wgt_scales.rearrange("f s r k -> r (f s) k").bitcast(I32), nc.sync)
+        load_scale_rows(wgt_s, wgt_scales.rearrange("f s r k -> r (f s) k").bitcast(I32))
         nc.sync.dma_start(offs_sb[:], offs)
 
         def gather_scales(f):
@@ -112,7 +113,7 @@ def tile_moe_hib_relu_kernel(
 
         def order_words_as_bytes(e):
             tile = keep.tile([P, PACK, P, 2], U8, name="late_w%d" % e, align_bytes=64)
-            nc.gpsimd.tensor_copy(tile[:], wet_w[e][:].rearrange("p (m t b) -> p t m b", t=PACK, b=2))
+            nc.gpsimd.tensor_copy(tile[:], wet_late[:, e - E // G, :].rearrange("p (m t b) -> p t m b", t=PACK, b=2))
             for t in range(PACK):
                 plane_w[e, t] = tile[:, t, :, :].rearrange("p m b -> p (m b)")
 
@@ -187,11 +188,10 @@ def tile_moe_hib_relu_kernel(
         order_words(0, range(0, 1), "lead_w")
         order_words(0, range(1, 4), "first_w")
         order_words(1, range(0, 4), "plane_w1")
-        order_words(3, range(0, 4), "plane_w3")
         z_first = reuse.tile([P, PACK, C1], F32, name="z_first", tag="z_first", align_bytes=64)
         z = {(0, t): z_first[:, t, :] for t in range(PACK)}
         g_s = [gather_scales(f) for f in range(G)]
-        for e, planes in ((0, range(0, 1)), (0, range(1, 2)), (1, range(0, 2)), (0, range(2, 4)), (1, range(2, 4))):
+        for e, planes in ((0, range(0, 1)), (0, range(1, 4)), (1, range(0, 2)), (1, range(2, 4))):
             order_scales(e, planes)
         for e in range(E // G, E):
             order_scales(e, range(0, PACK))
@@ -201,20 +201,20 @@ def tile_moe_hib_relu_kernel(
         gather_words(C2, w_first[:, C2:C1])
         for first, last, planes, n_bank in (
             (0, SHORT, range(0, 1), 0),
-            (0, C2, range(1, 2), 1),
-            (SHORT, C2, range(0, 1), 2),
+            (0, SHORT, range(1, 4), 1),
+            (SHORT, C2, range(0, 4), 2),
             (C2, C1, range(0, 2), 3),
-            (0, C2, range(2, 4), 4),
-            (C2, C1, range(2, 4), 5),
+            (C2, C1, range(2, 4), 4),
         ):
             acc = first_product(first, w_first[:, first:last], planes, n_bank)
             weights = gate_lead[:, first:last] if first < C2 else gate_rest[:]
             times_gate(z_first[:, planes.start : planes.stop, first:last], acc, weights)
 
-        order_words_as_bytes(2)
-        w_late = reuse.tile([P, C1], U32, name="w_late", tag="gate_lead", align_bytes=64)
+        for e in range(E // G, E):
+            order_words_as_bytes(e)
+        w_late = reuse.tile([P, C1], U32, name="w_late", tag="plane_w1", align_bytes=64)
         gather_words(C1, w_late[:])
-        slope = {0: take_slope(a_first, "wet_w2"), 1: take_slope(a_late, "slope_late")}
+        slope = {0: take_slope(a_first, "wet_late"), 1: take_slope(a_late, "slope_late")}
         late_sums = {}
         for u in range(2):
             for e in (2, 3):
@@ -234,10 +234,11 @@ def tile_moe_hib_relu_kernel(
 
         for f, t in ((0, 0), (0, 1), (1, 0), (1, 2)):
             win[f, t] = keep.tile([P, T], F32, name="win%d%d" % (f, t), align_bytes=64)
-        win[0, 2] = reuse.tile([P, T], F32, name="win02", tag="gate_rest", align_bytes=64)
+        win[0, 2] = reuse.tile([P, T], F32, name="win02", tag="win02", align_bytes=64)
         da = [placed.tile([P, C1, PACK], BF16, name="da0", offset=2 * KIB, align_bytes=64)]
-        for t, first, last in ((0, 0, SHORT), (1, 0, C2), (0, SHORT, C1), (1, C2, C1), (2, 0, C2), (2, C2, C1)):
-            scatter_z(scatter_on_scalar, 0, t, first, last)
+        for first, last in ((0, SHORT), (SHORT, C1)):
+            for t in range(PACK - 1):
+                scatter_z(scatter_on_scalar, 0, t, first, last)
         for t in (0, 1, 3, 2):
             mask_plane(0, t)
 
@@ -246,7 +247,7 @@ def tile_moe_hib_relu_kernel(
         for t, first, last in ((0, 0, C2), (0, C2, C1), (2, FILL, C1)):
             scatter_z(scatter_on_scalar, 1, t, first, last)
         low, high = second_product(0, 0, C1, (2, 3))
-        win[1, 3] = placed.tile([P, T], F32, name="win13", offset=0, align_bytes=64)
+        win[1, 3] = reuse.tile([P, T], F32, name="win13", tag="win02", align_bytes=64)
         da.append(placed.tile([P, C1, PACK], BF16, name="da1", offset=4 * KIB, align_bytes=64))
         scatter_z(scatter_on_vector, 1, 3, 0, C1)
         win[1, 1] = reuse.tile([P, T], F32, name="win11", tag="da_w0_0", align_bytes=64)

@@ -263,8 +263,8 @@ def tile_moe_hib_relu_kernel(
 
         out_low = keep.tile([P, T], F32, name="out_low", align_bytes=64)
         out_high = keep.tile([P, T], F32, name="out_high", align_bytes=64)
-        dx_high = leave_psum(nc.scalar.copy, high[:], "dx0_high")
         dx_low = leave_psum(nc.vector.tensor_copy, low[:], "dx0_low")
+        dx_high = leave_psum(nc.vector.tensor_copy, high[:], "dx0_high")
         for first in (0, C2):
             scatter_on_scalar(out_high, offs_sb, first, dx_high[:, first : first + C2])
         scatter_on_vector(out_low, offs_sb, 0, dx_low[:])

from contextlib import ExitStack

import concourse.mybir as mybir

K, T, G, C1, E, C2, H, N = 256, 1024, 2, 512, 4, 256, 512, 512
FLOPS = 2 * T * N * H + 2 * T * H * K

F32 = mybir.dt.float32
BF16 = mybir.dt.bfloat16
I32 = mybir.dt.int32
U32 = mybir.dt.uint32
U16 = mybir.dt.uint16
U8 = mybir.dt.uint8
FP8X4 = mybir.dt.float8_e4m3fn_x4
FP4X4 = mybir.dt.float4_e2m1fn_x4
ACT = mybir.ActivationFunctionType
ALU = mybir.AluOpType

P = 128
PACK = 4
PER_COL = 16
SHORT = 128
FILL = 256
KIB = 1024


def entries(list_tile, first, count):
    return list_tile[:, first // PER_COL : (first + count) // PER_COL]


def words_of(plane):
    return plane[:].rearrange("p e h -> p (e h)").bitcast(I32)


def tile_moe_hib_relu_kernel(
    tc, dy_words, dy_scales, wet_words, wet_scales, wgt_words, wgt_scales, a, gate, offs, offs2, dst, out
):
    nc = tc.nc
    with ExitStack() as ctx:
        keep = ctx.enter_context(tc.tile_pool(name="keep", bufs=1))
        reuse = ctx.enter_context(tc.tile_pool(name="reuse", bufs=1))
        placed = ctx.enter_context(tc.tile_pool(name="placed", bufs=1))
        psum = ctx.enter_context(tc.psum_pool(name="psum", bufs=1))

        dst_sb = keep.tile([P, T // PER_COL], U16, name="dst_sb")
        offs2_sb = keep.tile([P, T // PER_COL], U16, name="offs2_sb")
        offs_sb = keep.tile([P, T // PER_COL], U16, name="offs_sb")
        dy_w = keep.tile([P, T], I32, name="dy_w", align_bytes=64)
        dy_s = keep.tile([P, T], U8, name="dy_s", align_bytes=64)
        wet_w = [keep.tile([P, 2 * H], U8, name="wet_w%d" % e, align_bytes=64) for e in range(E // G)]
        wet_late = reuse.tile([P, E // G, 2 * H], U8, name="wet_late", tag="wet_late", align_bytes=64)
        wet_s = keep.tile([P, E, H], U8, name="wet_s", align_bytes=64)
        wgt_w = keep.tile([P, G, K], I32, name="wgt_w", align_bytes=64)
        wgt_s = keep.tile([P, G, K], U8, name="wgt_s", align_bytes=64)
        gate_lead = keep.tile([P, C2], F32, name="gate_lead", align_bytes=64)
        gate_rest = keep.tile([P, C2], F32, name="gate_rest", align_bytes=64)
        gate_late = keep.tile([P, C1], F32, name="gate_late", align_bytes=64)
        a_first = keep.tile([P, PACK, C1], F32, name="a_first", align_bytes=64)
        a_late = placed.tile([P, PACK, C1], F32, name="a_late", offset=5 * KIB, align_bytes=64)

        def zero_on_vector(words):
            last = words.shape[1] - 1
            nc.vector.memset(words[:, 0:last], 0)
            nc.vector.memset(words[:, last : last + 1], 0)

        nc.gpsimd.memset(dy_s[:].bitcast(I32)[:, 0:P], 0)
        zero_on_vector(dy_s[:].bitcast(I32)[:, P : 2 * P])
        nc.gpsimd.memset(words_of(wet_s)[:, 0:P], 0)
        zero_on_vector(words_of(wet_s)[:, P : E * P])
        nc.gpsimd.memset(words_of(wgt_s), 0)

        def load_scale_rows(plane, rows):
            for q in range(4):
                nc.sync.dma_start(plane[32 * q : 32 * q + 4, :, :].bitcast(I32), rows[4 * q : 4 * q + 4, :, :])

        a_src = a.rearrange("(p t) j -> p t j", t=PACK)
        wet_src = wet_words.rearrange("e s p c -> p (e s) c").bitcast(I32)
        nc.sync.dma_start(dst_sb[:], dst)
        for q in range(4):
            queue = nc.sync if q < 3 else nc.scalar
            queue.dma_start(dy_s[32 * q : 32 * q + 4, :].bitcast(I32), dy_scales[0, 4 * q : 4 * q + 4, :].bitcast(I32))
        load_scale_rows(wet_s, wet_scales.rearrange("e s r h -> r (e s) h").bitcast(I32))
        nc.sync.dma_start(dy_w[:], dy_words[0].rearrange("p n d -> p (n d)").bitcast(I32))
        for e in (0, 1):
            nc.sync.dma_start(wet_w[e][:].bitcast(I32), wet_src[:, e, :])
        nc.sync.dma_start(offs2_sb[:], offs2)
        nc.sync.dma_start(gate_lead[:], gate[:, 0:C2])
        nc.sync.dma_start(gate_rest[:], gate[:, C2:C1])
        nc.sync.dma_start(wet_late[:].bitcast(I32), wet_src[:, 2:4, :])
        nc.sync.dma_start(a_first[:], a_src[:, :, 0:C1])
        nc.sync.dma_start(a_late[:], a_src[:, :, C1:T])
        nc.sync.dma_start(gate_late[:], gate[:, C1:T])
        nc.sync.dma_start(wgt_w[:], wgt_words.rearrange("f s p k d -> p (f s) (k d)").bitcast(I32))
        load_scale_rows(wgt_s, wgt_scales.rearrange("f s r k -> r (f s) k").bitcast(I32))
        nc.sync.dma_start(offs_sb[:], offs)

        def gather_scales(f):
            tile = keep.tile([P, C1], U8, name="g_s%d" % f, align_bytes=64)
            nc.vector.tensor_copy(tile[:], dy_s[:].indirect(entries(dst_sb, f * C1, C1)))
            return tile

        def gather_words(first, into):
            nc.vector.tensor_copy(into, dy_w[:].bitcast(U32).indirect(entries(dst_sb, first, into.shape[1])))

        plane_w, plane_s = {}, {}

        def order_words(e, planes, tag):
            tile = reuse.tile([P, len(planes), 2 * P], U8, name="plane_w", tag=tag, align_bytes=64)
            source = wet_w[e][:].bitcast(U16).rearrange("p (m t) -> p t m", t=PACK)
            nc.scalar.copy(tile[:].bitcast(U16), source[:, planes.start : planes.stop, :])
            for n, t in enumerate(planes):
                plane_w[e, t] = tile[:, n, :]

        def order_words_as_bytes(e):
            tile = keep.tile([P, PACK, P, 2], U8, name="late_w%d" % e, align_bytes=64)
            nc.gpsimd.tensor_copy(tile[:], wet_late[:, e - E // G, :].rearrange("p (m t b) -> p t m b", t=PACK, b=2))
            for t in range(PACK):
                plane_w[e, t] = tile[:, t, :, :].rearrange("p m b -> p (m b)")

        def order_scales(e, planes):
            tile = keep.tile([P, len(planes), P], U8, name="plane_s%d_%d" % (e, planes.start), align_bytes=64)
            source = wet_s[:, e, :].rearrange("p (m t) -> p t m", t=PACK)
            nc.gpsimd.tensor_copy(tile[:], source[:, planes.start : planes.stop, :])
            for n, t in enumerate(planes):
                plane_s[e, t] = tile[:, n, :]

        def bank(n, shape):
            return psum.tile(shape, F32, name="bank", tag="bank%d" % n)

        def first_product(first, words, planes, n_bank):
            count = words.shape[1]
            e, f = first // C2, first // C1
            acc = bank(n_bank, [P, len(planes), count])
            for n, t in enumerate(planes):
                nc.tensor.matmul_mx(
                    out=acc[:, n, :],
                    lhsT=plane_w[e, t].bitcast(FP4X4),
                    lhsT_scale=plane_s[e, t],
                    rhs=words.bitcast(FP8X4),
                    rhs_scale=g_s[f][:, first - f * C1 : first - f * C1 + count],
                    start=True,
                    stop=True,
                )
            return acc

        def times_gate(into, acc, weights):
            nc.vector.tensor_tensor(into, acc[:], weights.unsqueeze(1).to_broadcast(list(acc.shape)), ALU.mult)

        def scatter_on_scalar(window, list_tile, first, source):
            nc.scalar.activation(window[:].indirect(entries(list_tile, first, source.shape[1])), source, ACT.Copy)

        def scatter_on_vector(window, list_tile, first, source):
            nc.vector.tensor_copy(window[:].indirect(entries(list_tile, first, source.shape[1])), source)

        def scatter_z(scatter, f, t, first, last):
            scatter(win[f, t], offs2_sb, f * C1 + first, z[f, t][:, first:last])

        def take_slope(source, tag):
            tile = reuse.tile([P, PACK, C1], BF16, name="slope", tag=tag, align_bytes=64)
            nc.vector.tensor_scalar(tile[:], source[:], 0.0, None, ALU.is_gt)
            return tile

        def mask_plane(f, t):
            nc.gpsimd.tensor_tensor(da[f][:, :, t], win[f, t][:, f * C1 : (f + 1) * C1], slope[f][:, t, :], ALU.mult)

        def second_product(f, first, last, banks):
            count = last - first
            da_w = reuse.tile([P, count], U32, name="da_w", tag="da_w%d_%d" % (f, first), align_bytes=64)
            da_s = keep.tile([P, count], U8, name="da_s%d_%d" % (f, first), align_bytes=64)
            values = da[f][:, first:last, :].rearrange("p j t -> p (j t)")
            nc.vector.quantize_mx(out=da_w[:].bitcast(FP8X4), scales=da_s[:], in_=values)
            accs = []
            for kb in range(K // P):
                k_cols = slice(kb * P, (kb + 1) * P)
                acc = bank(banks[kb], [P, count])
                nc.tensor.matmul_mx(
                    out=acc[:],
                    lhsT=wgt_w[:, f, k_cols].bitcast(FP8X4),
                    lhsT_scale=wgt_s[:, f, k_cols],
                    rhs=da_w[:].bitcast(FP8X4),
                    rhs_scale=da_s[:],
                    start=True,
                    stop=True,
                )
                accs.append(acc)
            return accs

        order_words(0, range(0, 1), "lead_w")
        order_words(0, range(1, 4), "first_w")
        order_words(1, range(0, 4), "plane_w1")
        z_first = reuse.tile([P, PACK, C1], F32, name="z_first", tag="z_first", align_bytes=64)
        z = {(0, t): z_first[:, t, :] for t in range(PACK)}
        g_s = [gather_scales(f) for f in range(G)]
        for e, planes in ((0, range(0, 1)), (0, range(1, 4)), (1, range(0, 2)), (1, range(2, 4))):
            order_scales(e, planes)
        for e in range(E // G, E):
            order_scales(e, range(0, PACK))
        w_first = keep.tile([P, C1], U32, name="w_first", align_bytes=64)
        gather_words(0, w_first[:, 0:SHORT])
        gather_words(SHORT, w_first[:, SHORT:C2])
        gather_words(C2, w_first[:, C2:C1])
        for first, last, planes, n_bank in (
            (0, SHORT, range(0, 1), 0),
            (0, SHORT, range(1, 4), 1),
            (SHORT, C2, range(0, 4), 2),
            (C2, C1, range(0, 2), 3),
            (C2, C1, range(2, 4), 4),
        ):
            acc = first_product(first, w_first[:, first:last], planes, n_bank)
            weights = gate_lead[:, first:last] if first < C2 else gate_rest[:]
            times_gate(z_first[:, planes.start : planes.stop, first:last], acc, weights)

        for e in range(E // G, E):
            order_words_as_bytes(e)
        w_late = reuse.tile([P, C1], U32, name="w_late", tag="plane_w1", align_bytes=64)
        gather_words(C1, w_late[:])
        slope = {0: take_slope(a_first, "wet_late"), 1: take_slope(a_late, "slope_late")}
        late_sums = {}
        for u in range(2):
            for e in (2, 3):
                words = w_late[:, e * C2 - C1 : (e + 1) * C2 - C1]
                late_sums[e, u] = first_product(e * C2, words, range(2 * u, 2 * u + 2), (6 + 2 * u + e % 2) % 8)
        win = {(0, 3): placed.tile([P, T], F32, name="win03", offset=12 * KIB, align_bytes=64)}
        scatter_z(scatter_on_vector, 0, 3, 0, C1)

        def late_pair(u, tile):
            for e in (2, 3):
                columns = slice(e * C2 - C1, (e + 1) * C2 - C1)
                times_gate(tile[:, :, columns], late_sums[e, u], gate_late[:, columns])
            for n in range(2):
                z[1, 2 * u + n] = tile[:, n, :]

        late_pair(0, placed.tile([P, 2, C1], F32, name="z_late0", offset=8 * KIB, align_bytes=64))

        for f, t in ((0, 0), (0, 1), (1, 0), (1, 2)):
            win[f, t] = keep.tile([P, T], F32, name="win%d%d" % (f, t), align_bytes=64)
        win[0, 2] = reuse.tile([P, T], F32, name="win02", tag="win02", align_bytes=64)
        da = [placed.tile([P, C1, PACK], BF16, name="da0", offset=2 * KIB, align_bytes=64)]
        for first, last in ((0, SHORT), (SHORT, C1)):
            for t in range(PACK - 1):
                scatter_z(scatter_on_scalar, 0, t, first, last)
        for t in (0, 1, 3, 2):
            mask_plane(0, t)

        late_pair(1, reuse.tile([P, 2, C1], F32, name="z_late1", tag="z_first", align_bytes=64))
        scatter_z(scatter_on_vector, 1, 2, 0, FILL)
        for t, first, last in ((0, 0, C2), (0, C2, C1), (2, FILL, C1)):
            scatter_z(scatter_on_scalar, 1, t, first, last)
        low, high = second_product(0, 0, C1, (2, 3))
        win[1, 3] = reuse.tile([P, T], F32, name="win13", tag="win02", align_bytes=64)
        da.append(placed.tile([P, C1, PACK], BF16, name="da1", offset=4 * KIB, align_bytes=64))
        scatter_z(scatter_on_vector, 1, 3, 0, C1)
        win[1, 1] = reuse.tile([P, T], F32, name="win11", tag="da_w0_0", align_bytes=64)
        for first in (0, C2):
            scatter_z(scatter_on_scalar, 1, 1, first, first + C2)
        for t in (0, 2, 3, 1):
            mask_plane(1, t)

        def leave_psum(copy, acc, name):
            tile = keep.tile([P, acc.shape[1]], F32, name=name, align_bytes=64)
            copy(tile[:], acc)
            return tile

        out_low = keep.tile([P, T], F32, name="out_low", align_bytes=64)
        out_high = keep.tile([P, T], F32, name="out_high", align_bytes=64)
        dx_low = leave_psum(nc.vector.tensor_copy, low[:], "dx0_low")
        dx_high = leave_psum(nc.vector.tensor_copy, high[:], "dx0_high")
        for first in (0, C2):
            scatter_on_scalar(out_high, offs_sb, first, dx_high[:, first : first + C2])
        scatter_on_vector(out_low, offs_sb, 0, dx_low[:])

        late = [second_product(1, 0, C2, (4, 5)), second_product(1, C2, C1, (6, 7))]
        for place, (low, high) in enumerate(late):
            first = C1 + place * C2
            copy_low = nc.vector.tensor_copy if place == 0 else nc.scalar.copy
            scatter_on_vector(out_low, offs_sb, first, leave_psum(copy_low, low[:], "dx1_low%d" % place)[:])
            scatter_on_scalar(out_high, offs_sb, first, leave_psum(nc.scalar.copy, high[:], "dx1_high%d" % place)[:])
        nc.sync.dma_start(out[0:P, :], out_low[:])
        nc.sync.dma_start(out[P : 2 * P, :], out_high[:])
